import numpy as np
import ml_dtypes


def mxq(x, axis, fmt="e4m3"):
    dtype, down = {"e4m3": (ml_dtypes.float8_e4m3fn, 7), "e5m2": (ml_dtypes.float8_e5m2, 14)}[fmt]
    v = np.moveaxis(np.asarray(x, np.float32).astype(ml_dtypes.bfloat16).astype(np.float64), axis, -1)
    blocks = v.reshape(v.shape[:-1] + (-1, 32))
    amax = np.abs(blocks).max(-1, keepdims=True)
    byte = np.maximum(np.where(amax > 0, np.frexp(amax)[1] - 1 + 127, 0) - down, 1)
    scale = np.exp2(byte - 127.0)
    codes = (blocks / scale).astype(np.float32).astype(dtype).astype(np.float64)
    return np.moveaxis((codes * scale).reshape(v.shape), -1, axis)


WIDE = False


def mx_kscale(k):
    if not WIDE:
        return np.ones(k)
    levels = np.array([10, -10, 5, -5, 0])
    if k % 512:
        return np.exp2(np.random.permutation(np.resize(levels, k // 32))).repeat(32)
    a = np.empty((k // 512, 16))
    for p in range(k // 512):
        a[p, :8] = np.random.permutation(np.resize(levels, 8))
        for g in range(8):
            far = levels[np.abs(levels - a[p, g]) >= 10]
            a[p, g + 8] = far[np.random.randint(len(far))]
    return np.exp2(a.ravel()).repeat(32)


BF16 = ml_dtypes.bfloat16


def bf(x):
    return np.asarray(x, np.float32).astype(BF16)


def f64(x):
    return np.asarray(x).astype(np.float64)


E2M1 = np.array([0.0, 0.5, 1.0, 1.5, 2.0, 3.0, 4.0, 6.0, -0.0, -0.5, -1.0, -1.5, -2.0, -3.0, -4.0, -6.0])


def pack_weight(w, fmt):
    k, n = w.shape
    w = f64(bf(w)).reshape(k // 32, 32, n)
    amax = np.abs(w).max(1)
    if fmt == "e4m3":
        byte = np.frexp(amax)[1] - 1 + 127 - 7
    else:
        mant, ex = np.frexp(amax / 6.0)
        byte = np.where(mant > 0.5, ex, ex - 1) + 127
    byte = np.clip(np.where(amax > 0, byte, 1), 1, 254)
    scaled = (w * np.exp2(127.0 - byte)[:, None, :]).reshape(k, n).astype(np.float32)
    by_word = np.ascontiguousarray(scaled.reshape(k // 512, 128, 4, n).transpose(0, 1, 3, 2))
    if fmt == "e4m3":
        words = by_word.astype(ml_dtypes.float8_e4m3fn).view(np.uint8)
    else:
        c = by_word.astype(ml_dtypes.float4_e2m1fn).view(np.uint8) & 0xF
        words = c[..., 0::2] | (c[..., 1::2] << 4)
    return np.ascontiguousarray(words), np.ascontiguousarray(byte.astype(np.uint8).reshape(k // 512, 16, n))


def unpack_weight(words, scales, fmt):
    g, p, n, _ = words.shape
    if fmt == "e4m3":
        vals = np.ascontiguousarray(words).view(ml_dtypes.float8_e4m3fn).astype(np.float64)
    else:
        nib = np.empty((g, p, n, 4), np.uint8)
        nib[..., 0::2] = words & 0xF
        nib[..., 1::2] = words >> 4
        vals = E2M1[nib]
    vals = vals * np.repeat(np.exp2(scales.astype(np.float64) - 127.0), 8, axis=1)[..., None]
    return vals.transpose(0, 1, 3, 2).reshape(g * 512, n)
def pack4(w):
    words, scales = pack_weight(w, "e2m1")
    return words.reshape(words.shape[0], 128, -1), scales


def unpack4(words, scales):
    return unpack_weight(words.reshape(words.shape[0], 128, -1, 2), scales, "e2m1")


E4M3FN = np.array([(-1.0 if i & 128 else 1.0) * ((1.0 + (i & 7) / 8.0) * 2.0 ** (((i >> 3) & 15) - 7) if i & 120 else (i & 7) * 2.0 ** -9) for i in range(256)])


def e4m3fn_bytes(y):
    return np.clip(np.asarray(y, np.float64), -448.0, 448.0).astype(np.float32).astype(ml_dtypes.float8_e4m3fn).view(np.uint8)


def e4m3fn_values(b):
    return E4M3FN[b]


T, K, V, N, B = 1024, 1024, 2048, 1024, 128


def setup_inputs():
    s, t = mx_kscale(K), mx_kscale(V)
    x = np.random.standard_normal((T, K)) * s
    x_scale = (np.abs(x).reshape(T, K // B, B).max(axis=2) / 448.0).astype(np.float32)
    x_bytes = e4m3fn_bytes(x / np.repeat(f64(x_scale), B, axis=1))
    head = np.random.standard_normal((V, K)) / np.sqrt(K) / s * t[:, None]
    vmap = np.random.standard_normal((V, N)) / np.sqrt(V) / t[:, None]
    map_words, map_scales = pack4(vmap)
    return {"x_bytes": x_bytes,
            "x_scale": x_scale,
            "head": bf(head),
            "b": bf(0.4 * np.random.standard_normal(V) * t),
            "tau": bf(np.random.uniform(1.0, 3.0, T)),
            "map_words": map_words,
            "map_scales": map_scales,
            "c": bf(0.3 * np.random.standard_normal(N))}


def reference(x_bytes, x_scale, head, b, tau, map_words, map_scales, c):
    x = e4m3fn_values(x_bytes) * np.repeat(f64(x_scale), B, axis=1)
    logits = mxq(x, 1, "e4m3") @ mxq(f64(head), 1, "e4m3").T
    z = (logits + f64(b)) / f64(tau)[:, None]
    y = mxq(z, 1, "e4m3") @ unpack4(map_words, map_scales)
    return y + f64(c)

@@ -1,0 +1,277 @@
+from contextlib import ExitStack
+
+import concourse.mybir as mybir
+from concourse.masks import make_identity
+
+T, K, V, N, B = 1024, 1024, 2048, 1024, 128
+FLOPS = 2 * T * K * V + 2 * T * V * N
+
+F32 = mybir.dt.float32
+BF16 = mybir.dt.bfloat16
+I32 = mybir.dt.int32
+U32 = mybir.dt.uint32
+U8 = mybir.dt.uint8
+FP8 = mybir.dt.float8_e4m3fn
+FP8X4 = mybir.dt.float8_e4m3fn_x4
+FP4X4 = mybir.dt.float4_e2m1fn_x4
+COPY = mybir.ActivationFunctionType.Copy
+IDENT = mybir.ActivationFunctionType.Identity
+ADD = mybir.AluOpType.add
+MULT = mybir.AluOpType.mult
+
+P = 128
+G = 2
+TT = 8
+C = 4
+S = 4
+GROUPS = (4, 4)
+WID = ["s","v","s","sv","s","sv","v","s"]
+XCP = "svsvssss"
+HCP = "vsvsvssvsvsvssss"
+ZI = "ssssssss"
+ORDER = [("r", 0), ("h", 0), ("h", 1), ("h", 2), ("x", 0), ("h", 3), ("x", 1), ("z", (0, 0)), ("z", (1, 0)), ("z", (2, 0)), ("z", (3, 0)), ("y", 0), ("z", (1, 1)), ("z", (2, 1)), ("y", 1), ("z", (0, 1)), ("z", (3, 1)), ("y", 2), ("y", 3), ("y", 4), ("y", 5), ("y", 6), ("y", 7)]
+TPB = 3
+A1B = 3
+LOADS = [("x", 0), ("t", 0), ("x", 1), ("h", 0), ("h", 1), ("b", 0), ("h", 2), ("h", 3), ("h", 4), ("h", 5), ("x", 2), ("x", 3), ("h", 6), ("h", 7)]
+
+
+def tile_teacher_logits_remap_d4_kernel(tc, x_bytes, x_scale, head, b, tau, map_words, map_scales, c, out):
+    nc = tc.nc
+    x_v = x_bytes.rearrange("(p i) k -> p i k", i=TT)
+    head_v = head.rearrange("(c p s) k -> c p s k", p=P, s=S)
+    out_v = out.rearrange("(p i) n -> p i n", i=TT)
+
+    with ExitStack() as ctx:
+        keep = ctx.enter_context(tc.tile_pool(name="keep", bufs=1))
+        work = ctx.enter_context(tc.tile_pool(name="work", bufs=3))
+        psum = ctx.enter_context(tc.psum_pool(name="psum", bufs=1))
+
+        xs = keep.tile([P, TT, K // B], F32, name="xs")
+        nc.sync.dma_start(out=xs[:], in_=x_scale.rearrange("(p i) j -> p i j", i=TT))
+        xb = []
+        for q in range(4):
+            xb_q = keep.tile([P, 2, K], U8, name=f"xb{q}")
+            xb.append(xb_q)
+        hraw = []
+        for e in range(2 * C):
+            h_t = keep.tile([P, 2, K], BF16, name=f"hraw{e}")
+            hraw.append(h_t)
+        b_bf = keep.tile([P, C, S], BF16, name="b_bf")
+        tau_sb = keep.tile([P, TT], BF16, name="tau_sb")
+        msc = keep.tile([P, C, N], U8, name="msc", align_bytes=64)
+        mw = keep.tile([P, C, 2 * N], U8, name="mw", align_bytes=64)
+        c_bc = keep.tile([P, N], BF16, name="c_bc")
+
+        def load_x(q):
+            nc.sync.dma_start(out=xb[q][:], in_=x_v[:, 2 * q : 2 * q + 2, :])
+
+        for what, arg in LOADS:
+            if what == "x":
+                load_x(arg)
+            if what == "t":
+                nc.sync.dma_start(out=tau_sb[:], in_=tau.rearrange("(p i) -> p i", i=TT))
+            if what == "b":
+                nc.sync.dma_start(out=b_bf[:], in_=b.rearrange("(c p s) -> p c s", p=P, s=S))
+            if what == "h":
+                nc.sync.dma_start(out=hraw[arg][:], in_=head_v[arg // 2, :, 2 * (arg % 2) : 2 * (arg % 2) + 2, :])
+        nc.vector.memset(msc[:].rearrange("p c n -> p (c n)").bitcast(I32), 0)
+        for q in range(4):
+            nc.sync.dma_start(
+                out=msc[32 * q : 32 * q + 4, :, :].bitcast(I32),
+                in_=map_scales[:, 4 * q : 4 * q + 4, :].rearrange("c r n -> r c n").bitcast(I32),
+            )
+        nc.sync.dma_start(out=mw[:].bitcast(I32), in_=map_words.rearrange("c p n -> p c n").bitcast(I32))
+        nc.sync.dma_start(out=c_bc[:], in_=c.partition_broadcast(P))
+
+        ident = keep.tile([P, P], F32, name="ident")
+        make_identity(nc, ident[:])
+
+        rt_col = keep.tile([P, TT], F32, name="rt_col")
+        b_sb = keep.tile([P, C, S], F32, name="b_sb")
+        rtau = keep.tile([P, TT, P], F32, name="rtau")
+
+        def make_rtau():
+            nc.vector.reciprocal(rt_col[:], tau_sb[:])
+            for i0 in range(0, TT, 4):
+                rp = psum.tile([P, 4, P], F32, name="tp", tag="tp", bufs=3)
+                for ii in range(4):
+                    nc.tensor.transpose(rp[:, ii, :], rt_col[:, i0 + ii : i0 + ii + 1].to_broadcast([P, P]), ident[:])
+                nc.scalar.copy(rtau[:, i0 : i0 + 4, :], rp[:])
+
+        first = [sum(GROUPS[:h]) for h in range(len(GROUPS))]
+        group_of = [h for h in range(len(GROUPS)) for ii in range(GROUPS[h])]
+        xT = []
+        xc = []
+        xsc = []
+        for h in range(len(GROUPS)):
+            n = GROUPS[h] * P
+            xt_h = keep.tile([P, G, n, 4], BF16, name=f"xT{h}", align_bytes=64)
+            xc_h = keep.tile([P, G, n], U32, name=f"xc{h}", align_bytes=64)
+            xsc_h = keep.tile([P, G, n], U8, name=f"xsc{h}", align_bytes=64)
+            xT.append(xt_h)
+            xc.append(xc_h)
+            xsc.append(xsc_h)
+
+        xw = [None] * TT
+
+        def widen(i, eng):
+            xw_i = work.tile([P, K], BF16, name="xw", bufs=4)
+            xw[i] = xw_i
+            for j in range(K // B):
+                src = xb[i // 2][:, i % 2, j * B : (j + 1) * B].bitcast(FP8)
+                if (j % 2 == 0) if eng == "sv" else (eng == "s"):
+                    nc.scalar.activation(xw_i[:, j * B : (j + 1) * B], src, COPY, scale=xs[:, i, j : j + 1])
+                else:
+                    nc.vector.tensor_scalar(xw_i[:, j * B : (j + 1) * B], src, xs[:, i, j : j + 1], None, op0=MULT)
+
+        def turn(words, copy_eng, dst):
+            tp = psum.tile([P, G, 2, P], F32, name="tp", tag="tp", bufs=3)
+            for g in range(G):
+                for u in range(2):
+                    nc.tensor.transpose(tp[:, g, u, :], words[:, 256 * g + u : 256 * (g + 1) : 2], ident[:])
+            copy_eng(dst, tp[:].rearrange("p g u r -> p g r u"))
+
+        def x_turn(i, copy_eng):
+            h = group_of[i]
+            ii = i - first[h]
+            dst = xT[h][:, :, ii * P : (ii + 1) * P, :].rearrange("p g r t -> p g (r t)").bitcast(F32)
+            turn(xw[i][:].bitcast(F32), copy_eng, dst.rearrange("p g (r u) -> p g r u", u=2))
+
+        def x_quant(h):
+            for g in range(G):
+                nc.vector.quantize_mx(
+                    out=xc[h][:, g, :].bitcast(FP8X4), scales=xsc[h][:, g, :], in_=xT[h][:, g, :, :].rearrange("p n t -> p (n t)")
+                )
+
+        hT = [None] * (2 * C)
+        hc = []
+        hs = []
+        for e in range(2 * C):
+            hc_e = keep.tile([P, 2, G, P], U32, name=f"hc{e}", align_bytes=64)
+            hs_e = keep.tile([P, 2, G, P], U8, name=f"hs{e}", align_bytes=64)
+            hc.append(hc_e)
+            hs.append(hs_e)
+
+        def head_turn(cc, s, copy_eng):
+            e = 2 * cc + s // 2
+            if s % 2 == 0:
+                hT_e = work.tile([P, 2, G, P, 4], BF16, name="hT", align_bytes=64, bufs=4)
+                hT[e] = hT_e
+            dst = hT[e][:, s % 2].rearrange("p g r t -> p (g r t)").bitcast(F32)
+            turn(hraw[e][:, s % 2, :].bitcast(F32), copy_eng, dst.rearrange("p (g r u) -> p g r u", g=G, u=2))
+
+        def head_quant(cc, sp):
+            e = 2 * cc + sp
+            nc.vector.quantize_mx(
+                out=hc[e][:].rearrange("p s g m -> p (s g m)").bitcast(FP8X4),
+                scales=hs[e][:].rearrange("p s g m -> p (s g m)"),
+                in_=hT[e][:].rearrange("p s g m t -> p (s g m t)"),
+            )
+
+        zp = {}
+        zi = {}
+        zc = {}
+        zs = {}
+
+        def stage1(cc, h, s):
+            n = GROUPS[h] * P
+            if s == 0:
+                zp_t = work.tile([P, S, n], BF16, name="zp", bufs=3)
+                zp[cc, h] = zp_t
+            acc = psum.tile([P, n], F32, name="acc1", tag="acc1", bufs=3)
+            e = 2 * cc + s // 2
+            for g in range(G):
+                nc.tensor.matmul_mx(
+                    out=acc[:],
+                    lhsT=hc[e][:, s % 2, g, :].bitcast(FP8X4),
+                    lhsT_scale=hs[e][:, s % 2, g, :],
+                    rhs=xc[h][:, g, :].bitcast(FP8X4),
+                    rhs_scale=xsc[h][:, g, :],
+                    start=(g == 0),
+                    stop=(g == G - 1),
+                )
+            nc.vector.scalar_tensor_tensor(
+                zp[cc, h][:, s, :],
+                acc[:],
+                b_sb[:, cc, s : s + 1],
+                rtau[:, first[h] : first[h] + GROUPS[h], :].rearrange("p i n -> p (i n)"),
+                op0=ADD,
+                op1=MULT,
+            )
+
+        def z_inter(cc, h, copy_eng):
+            n = GROUPS[h] * P
+            zi_t = work.tile([P, n, S], BF16, name="zi", align_bytes=64, bufs=3)
+            zi[cc, h] = zi_t
+            copy_eng(
+                zi_t[:].rearrange("p (n i) s -> p n s i", i=4),
+                zp[cc, h][:].rearrange("p s (n i) -> p n s i", i=4),
+            )
+
+        def z_quant(cc, h):
+            n = GROUPS[h] * P
+            zc_t = keep.tile([P, n], U32, name=f"zc{cc}_{h}", align_bytes=64)
+            zs_t = keep.tile([P, n], U8, name=f"zs{cc}_{h}", align_bytes=64)
+            zc[cc, h] = zc_t
+            zs[cc, h] = zs_t
+            nc.vector.quantize_mx(out=zc_t[:].bitcast(FP8X4), scales=zs_t[:], in_=zi[cc, h][:].rearrange("p n s -> p (n s)"))
+
+        yt = {}
+
+        def stage2(i, nh):
+            h = group_of[i]
+            ii = i - first[h]
+            cols = slice(ii * P, (ii + 1) * P)
+            if nh == 0:
+                y = work.tile([P, N], F32, name="y", bufs=3)
+                yt[i] = y
+            acc = psum.tile([P, 512], F32, name="acc2", tag="acc2", bufs=2)
+            n0 = 512 * nh
+            for cc in range(C):
+                nc.tensor.matmul_mx(
+                    out=acc[:],
+                    lhsT=zc[cc, h][:, cols].bitcast(FP8X4),
+                    lhsT_scale=zs[cc, h][:, cols],
+                    rhs=mw[:, cc, 2 * n0 : 2 * n0 + 1024].bitcast(FP4X4),
+                    rhs_scale=msc[:, cc, n0 : n0 + 512],
+                    start=(cc == 0),
+                    stop=(cc == C - 1),
+                )
+            nc.vector.tensor_tensor(yt[i][:, n0 : n0 + 512], acc[:], c_bc[:, n0 : n0 + 512], op=ADD)
+            nc.sync.dma_start(out=out_v[:, i, n0 : n0 + 512], in_=yt[i][:, n0 : n0 + 512])
+
+        sc, ve = nc.scalar.copy, nc.vector.tensor_copy
+        eng = {"s": nc.scalar.copy, "v": nc.vector.tensor_copy}
+
+        def head_prep(cc):
+            for s in range(S):
+                head_turn(cc, s, eng[HCP[4 * cc + s]])
+                if s % 2 == 1:
+                    head_quant(cc, s // 2)
+
+        def x_prep(h):
+            for i in range(first[h], first[h] + GROUPS[h]):
+                widen(i, WID[i])
+            for i in range(first[h], first[h] + GROUPS[h]):
+                x_turn(i, eng[XCP[i]])
+            x_quant(h)
+
+        def z_unit(cc, h):
+            for s in range(S):
+                stage1(cc, h, s)
+            z_inter(cc, h, eng[ZI[4 * h + cc]])
+            z_quant(cc, h)
+
+        for what, arg in ORDER:
+            if what == "x":
+                x_prep(arg)
+            if what == "r":
+                make_rtau()
+                nc.vector.tensor_copy(b_sb[:], b_bf[:])
+            if what == "h":
+                head_prep(arg)
+            if what == "z":
+                z_unit(*arg)
+            if what == "y":
+                stage2(arg, 0)
+                stage2(arg, 1)

@@ -15,7 +15,6 @@ FP8 = mybir.dt.float8_e4m3fn
 FP8X4 = mybir.dt.float8_e4m3fn_x4
 FP4X4 = mybir.dt.float4_e2m1fn_x4
 COPY = mybir.ActivationFunctionType.Copy
-IDENT = mybir.ActivationFunctionType.Identity
 ADD = mybir.AluOpType.add
 MULT = mybir.AluOpType.mult
 
@@ -24,15 +23,11 @@ G = 2
 TT = 8
 C = 4
 S = 4
-GROUPS = (4, 4)
-WID = ["s","v","s","sv","s","sv","v","s"]
-XCP = "svsvssss"
-HCP = "vsvsvssvsvsvssss"
-ZI = "ssssssss"
-ORDER = [("r", 0), ("h", 0), ("h", 1), ("h", 2), ("x", 0), ("h", 3), ("x", 1), ("z", (0, 0)), ("z", (1, 0)), ("z", (2, 0)), ("z", (3, 0)), ("y", 0), ("z", (1, 1)), ("z", (2, 1)), ("y", 1), ("z", (0, 1)), ("z", (3, 1)), ("y", 2), ("y", 3), ("y", 4), ("y", 5), ("y", 6), ("y", 7)]
-TPB = 3
-A1B = 3
-LOADS = [("x", 0), ("t", 0), ("x", 1), ("h", 0), ("h", 1), ("b", 0), ("h", 2), ("h", 3), ("h", 4), ("h", 5), ("x", 2), ("x", 3), ("h", 6), ("h", 7)]
+HALF = 512
+XT_AT = (1, 3)
+XQ_AT = (2, 4)
+W_AT = (0, 1)
+SCALAR_BLOCKS = 2
 
 
 def tile_teacher_logits_remap_d4_kernel(tc, x_bytes, x_scale, head, b, tau, map_words, map_scales, c, out):
@@ -45,36 +40,41 @@ def tile_teacher_logits_remap_d4_kernel(tc, x_bytes, x_scale, head, b, tau, map_
         keep = ctx.enter_context(tc.tile_pool(name="keep", bufs=1))
         work = ctx.enter_context(tc.tile_pool(name="work", bufs=3))
         psum = ctx.enter_context(tc.psum_pool(name="psum", bufs=1))
+        ctx.enter_context(tc.manual_schedule())
+
+        def bank(shape):
+            return psum.tile(shape, F32, name="bank", tag="bank", bufs=8)
 
         xs = keep.tile([P, TT, K // B], F32, name="xs")
-        nc.sync.dma_start(out=xs[:], in_=x_scale.rearrange("(p i) j -> p i j", i=TT))
-        xb = []
-        for q in range(4):
-            xb_q = keep.tile([P, 2, K], U8, name=f"xb{q}")
-            xb.append(xb_q)
-        hraw = []
-        for e in range(2 * C):
-            h_t = keep.tile([P, 2, K], BF16, name=f"hraw{e}")
-            hraw.append(h_t)
+        xb = [keep.tile([P, 2, K], U8, name=f"xb{q}") for q in range(4)]
+        hraw = [keep.tile([P, 2, K], BF16, name=f"hraw{e}") for e in range(2 * C)]
         b_bf = keep.tile([P, C, S], BF16, name="b_bf")
         tau_sb = keep.tile([P, TT], BF16, name="tau_sb")
         msc = keep.tile([P, C, N], U8, name="msc", align_bytes=64)
         mw = keep.tile([P, C, 2 * N], U8, name="mw", align_bytes=64)
         c_bc = keep.tile([P, N], BF16, name="c_bc")
+        ident = keep.tile([P, P], F32, name="ident")
 
         def load_x(q):
             nc.sync.dma_start(out=xb[q][:], in_=x_v[:, 2 * q : 2 * q + 2, :])
 
-        for what, arg in LOADS:
-            if what == "x":
-                load_x(arg)
-            if what == "t":
-                nc.sync.dma_start(out=tau_sb[:], in_=tau.rearrange("(p i) -> p i", i=TT))
-            if what == "b":
-                nc.sync.dma_start(out=b_bf[:], in_=b.rearrange("(c p s) -> p c s", p=P, s=S))
-            if what == "h":
-                nc.sync.dma_start(out=hraw[arg][:], in_=head_v[arg // 2, :, 2 * (arg % 2) : 2 * (arg % 2) + 2, :])
+        def load_head(e):
+            nc.sync.dma_start(out=hraw[e][:], in_=head_v[e // 2, :, 2 * (e % 2) : 2 * (e % 2) + 2, :])
+
+        make_identity(nc, ident[:])
         nc.vector.memset(msc[:].rearrange("p c n -> p (c n)").bitcast(I32), 0)
+        nc.sync.dma_start(out=tau_sb[:], in_=tau.rearrange("(p i) -> p i", i=TT))
+        nc.sync.dma_start(out=xs[:], in_=x_scale.rearrange("(p i) j -> p i j", i=TT))
+        load_x(0)
+        load_x(1)
+        load_head(0)
+        load_head(1)
+        nc.sync.dma_start(out=b_bf[:], in_=b.rearrange("(c p s) -> p c s", p=P, s=S))
+        load_x(2)
+        load_head(2)
+        load_x(3)
+        for e in range(3, 2 * C):
+            load_head(e)
         for q in range(4):
             nc.sync.dma_start(
                 out=msc[32 * q : 32 * q + 4, :, :].bitcast(I32),
@@ -83,85 +83,65 @@ def tile_teacher_logits_remap_d4_kernel(tc, x_bytes, x_scale, head, b, tau, map_
         nc.sync.dma_start(out=mw[:].bitcast(I32), in_=map_words.rearrange("c p n -> p c n").bitcast(I32))
         nc.sync.dma_start(out=c_bc[:], in_=c.partition_broadcast(P))
 
-        ident = keep.tile([P, P], F32, name="ident")
-        make_identity(nc, ident[:])
-
         rt_col = keep.tile([P, TT], F32, name="rt_col")
         b_sb = keep.tile([P, C, S], F32, name="b_sb")
-        rtau = keep.tile([P, TT, P], F32, name="rtau")
+        rtau = [keep.tile([P, 4, P], F32, name=f"rtau{h}") for h in range(2)]
 
-        def make_rtau():
-            nc.vector.reciprocal(rt_col[:], tau_sb[:])
-            for i0 in range(0, TT, 4):
-                rp = psum.tile([P, 4, P], F32, name="tp", tag="tp", bufs=3)
-                for ii in range(4):
-                    nc.tensor.transpose(rp[:, ii, :], rt_col[:, i0 + ii : i0 + ii + 1].to_broadcast([P, P]), ident[:])
-                nc.scalar.copy(rtau[:, i0 : i0 + 4, :], rp[:])
+        def make_rtau(h):
+            rp = bank([P, 4, P])
+            for ii in range(4):
+                nc.tensor.transpose(rp[:, ii, :], rt_col[:, 4 * h + ii : 4 * h + ii + 1].to_broadcast([P, P]), ident[:])
+            nc.scalar.copy(rtau[h][:], rp[:])
 
-        first = [sum(GROUPS[:h]) for h in range(len(GROUPS))]
-        group_of = [h for h in range(len(GROUPS)) for ii in range(GROUPS[h])]
-        xT = []
-        xc = []
-        xsc = []
-        for h in range(len(GROUPS)):
-            n = GROUPS[h] * P
-            xt_h = keep.tile([P, G, n, 4], BF16, name=f"xT{h}", align_bytes=64)
-            xc_h = keep.tile([P, G, n], U32, name=f"xc{h}", align_bytes=64)
-            xsc_h = keep.tile([P, G, n], U8, name=f"xsc{h}", align_bytes=64)
-            xT.append(xt_h)
-            xc.append(xc_h)
-            xsc.append(xsc_h)
+        xw = [keep.tile([P, K], BF16, name=f"xw{i}") for i in range(TT)]
+        xT = [keep.tile([P, G, 2 * P, 4], BF16, name=f"xT{q}", align_bytes=64) for q in range(4)]
+        xc = [keep.tile([P, G, HALF], U32, name=f"xc{h}", align_bytes=64) for h in range(2)]
+        xsc = [keep.tile([P, G, HALF], U8, name=f"xsc{h}", align_bytes=64) for h in range(2)]
 
-        xw = [None] * TT
-
-        def widen(i, eng):
-            xw_i = work.tile([P, K], BF16, name="xw", bufs=4)
-            xw[i] = xw_i
+        def widen(i):
             for j in range(K // B):
                 src = xb[i // 2][:, i % 2, j * B : (j + 1) * B].bitcast(FP8)
-                if (j % 2 == 0) if eng == "sv" else (eng == "s"):
-                    nc.scalar.activation(xw_i[:, j * B : (j + 1) * B], src, COPY, scale=xs[:, i, j : j + 1])
+                if i >= 2:
+                    dst = xw[i][:].rearrange("p (g u q r e) -> p g q r u e", g=G, u=2, q=4, e=2)[:, j // 4, j % 4]
+                    nc.vector.tensor_scalar(dst, src.rearrange("p (r u e) -> p r u e", u=2, e=2), xs[:, i, j : j + 1], None, op0=MULT)
+                elif j < SCALAR_BLOCKS:
+                    nc.scalar.activation(xw[i][:, j * B : (j + 1) * B], src, COPY, scale=xs[:, i, j : j + 1])
                 else:
-                    nc.vector.tensor_scalar(xw_i[:, j * B : (j + 1) * B], src, xs[:, i, j : j + 1], None, op0=MULT)
+                    nc.vector.tensor_scalar(xw[i][:, j * B : (j + 1) * B], src, xs[:, i, j : j + 1], None, op0=MULT)
 
-        def turn(words, copy_eng, dst):
-            tp = psum.tile([P, G, 2, P], F32, name="tp", tag="tp", bufs=3)
+        def turn(words, in_order):
+            tp = bank([P, G, 2, P])
             for g in range(G):
                 for u in range(2):
-                    nc.tensor.transpose(tp[:, g, u, :], words[:, 256 * g + u : 256 * (g + 1) : 2], ident[:])
-            copy_eng(dst, tp[:].rearrange("p g u r -> p g r u"))
+                    cols = slice(256 * g + P * u, 256 * g + P * (u + 1)) if in_order else slice(256 * g + u, 256 * (g + 1), 2)
+                    nc.tensor.transpose(tp[:, g, u, :], words[:, cols], ident[:])
+            return tp[:].rearrange("p g u r -> p g r u")
 
-        def x_turn(i, copy_eng):
-            h = group_of[i]
-            ii = i - first[h]
-            dst = xT[h][:, :, ii * P : (ii + 1) * P, :].rearrange("p g r t -> p g (r t)").bitcast(F32)
-            turn(xw[i][:].bitcast(F32), copy_eng, dst.rearrange("p g (r u) -> p g r u", u=2))
+        def x_turn(q):
+            for ii in range(2):
+                turned = turn(xw[2 * q + ii][:].bitcast(F32), q >= 1)
+                dst = xT[q][:, :, ii * P : (ii + 1) * P, :].rearrange("p g r t -> p g (r t)").bitcast(F32)
+                nc.scalar.copy(dst.rearrange("p g (r u) -> p g r u", u=2), turned)
 
-        def x_quant(h):
+        def x_quant(q):
+            cols = slice((q % 2) * 2 * P, (q % 2 + 1) * 2 * P)
             for g in range(G):
                 nc.vector.quantize_mx(
-                    out=xc[h][:, g, :].bitcast(FP8X4), scales=xsc[h][:, g, :], in_=xT[h][:, g, :, :].rearrange("p n t -> p (n t)")
+                    out=xc[q // 2][:, g, cols].bitcast(FP8X4), scales=xsc[q // 2][:, g, cols], in_=xT[q][:, g].rearrange("p n t -> p (n t)")
                 )
 
-        hT = [None] * (2 * C)
-        hc = []
-        hs = []
-        for e in range(2 * C):
-            hc_e = keep.tile([P, 2, G, P], U32, name=f"hc{e}", align_bytes=64)
-            hs_e = keep.tile([P, 2, G, P], U8, name=f"hs{e}", align_bytes=64)
-            hc.append(hc_e)
-            hs.append(hs_e)
+        hT = {}
+        hc = [keep.tile([P, 2, G, P], U32, name=f"hc{e}", align_bytes=64) for e in range(2 * C)]
+        hs = [keep.tile([P, 2, G, P], U8, name=f"hs{e}", align_bytes=64) for e in range(2 * C)]
 
-        def head_turn(cc, s, copy_eng):
-            e = 2 * cc + s // 2
-            if s % 2 == 0:
-                hT_e = work.tile([P, 2, G, P, 4], BF16, name="hT", align_bytes=64, bufs=4)
-                hT[e] = hT_e
-            dst = hT[e][:, s % 2].rearrange("p g r t -> p (g r t)").bitcast(F32)
-            turn(hraw[e][:, s % 2, :].bitcast(F32), copy_eng, dst.rearrange("p (g r u) -> p g r u", g=G, u=2))
+        def head_turn(e):
+            hT[e] = work.tile([P, 2, G, P, 4], BF16, name="hT", align_bytes=64, bufs=3)
+            for s in range(2):
+                turned = turn(hraw[e][:, s, :].bitcast(F32), False)
+                dst = hT[e][:, s].rearrange("p g r t -> p (g r t)").bitcast(F32)
+                nc.scalar.copy(dst.rearrange("p (g r u) -> p g r u", g=G, u=2), turned)
 
-        def head_quant(cc, sp):
-            e = 2 * cc + sp
+        def head_quant(e):
             nc.vector.quantize_mx(
                 out=hc[e][:].rearrange("p s g m -> p (s g m)").bitcast(FP8X4),
                 scales=hs[e][:].rearrange("p s g m -> p (s g m)"),
@@ -174,11 +154,9 @@ def tile_teacher_logits_remap_d4_kernel(tc, x_bytes, x_scale, head, b, tau, map_
         zs = {}
 
         def stage1(cc, h, s):
-            n = GROUPS[h] * P
             if s == 0:
-                zp_t = work.tile([P, S, n], BF16, name="zp", bufs=3)
-                zp[cc, h] = zp_t
-            acc = psum.tile([P, n], F32, name="acc1", tag="acc1", bufs=3)
+                zp[cc, h] = work.tile([P, S, HALF], BF16, name="zp", bufs=3)
+            acc = bank([P, HALF])
             e = 2 * cc + s // 2
             for g in range(G):
                 nc.tensor.matmul_mx(
@@ -191,87 +169,89 @@ def tile_teacher_logits_remap_d4_kernel(tc, x_bytes, x_scale, head, b, tau, map_
                     stop=(g == G - 1),
                 )
             nc.vector.scalar_tensor_tensor(
-                zp[cc, h][:, s, :],
-                acc[:],
-                b_sb[:, cc, s : s + 1],
-                rtau[:, first[h] : first[h] + GROUPS[h], :].rearrange("p i n -> p (i n)"),
-                op0=ADD,
-                op1=MULT,
+                zp[cc, h][:, s, :], acc[:], b_sb[:, cc, s : s + 1], rtau[h][:].rearrange("p i n -> p (i n)"), op0=ADD, op1=MULT
             )
 
-        def z_inter(cc, h, copy_eng):
-            n = GROUPS[h] * P
-            zi_t = work.tile([P, n, S], BF16, name="zi", align_bytes=64, bufs=3)
-            zi[cc, h] = zi_t
-            copy_eng(
-                zi_t[:].rearrange("p (n i) s -> p n s i", i=4),
-                zp[cc, h][:].rearrange("p s (n i) -> p n s i", i=4),
+        def z_inter(cc, q):
+            zi[cc, q] = work.tile([P, 2 * P, S], BF16, name="zi", align_bytes=64, bufs=4)
+            nc.scalar.copy(
+                zi[cc, q][:].rearrange("p (n i) s -> p n s i", i=4),
+                zp[cc, q // 2][:, :, (q % 2) * 2 * P : (q % 2 + 1) * 2 * P].rearrange("p s (n i) -> p n s i", i=4),
             )
 
-        def z_quant(cc, h):
-            n = GROUPS[h] * P
-            zc_t = keep.tile([P, n], U32, name=f"zc{cc}_{h}", align_bytes=64)
-            zs_t = keep.tile([P, n], U8, name=f"zs{cc}_{h}", align_bytes=64)
-            zc[cc, h] = zc_t
-            zs[cc, h] = zs_t
-            nc.vector.quantize_mx(out=zc_t[:].bitcast(FP8X4), scales=zs_t[:], in_=zi[cc, h][:].rearrange("p n s -> p (n s)"))
-
-        yt = {}
+        def z_quant(cc, q):
+            zc[cc, q] = keep.tile([P, 2 * P], U32, name=f"zc{cc}_{q}", align_bytes=64)
+            zs[cc, q] = keep.tile([P, 2 * P], U8, name=f"zs{cc}_{q}", align_bytes=64)
+            nc.vector.quantize_mx(out=zc[cc, q][:].bitcast(FP8X4), scales=zs[cc, q][:], in_=zi[cc, q][:].rearrange("p n s -> p (n s)"))
 
         def stage2(i, nh):
-            h = group_of[i]
-            ii = i - first[h]
-            cols = slice(ii * P, (ii + 1) * P)
-            if nh == 0:
-                y = work.tile([P, N], F32, name="y", bufs=3)
-                yt[i] = y
-            acc = psum.tile([P, 512], F32, name="acc2", tag="acc2", bufs=2)
+            cols = slice((i % 2) * P, (i % 2 + 1) * P)
             n0 = 512 * nh
+            y = work.tile([P, 512], F32, name="y", bufs=6)
+            acc = bank([P, 512])
             for cc in range(C):
                 nc.tensor.matmul_mx(
                     out=acc[:],
-                    lhsT=zc[cc, h][:, cols].bitcast(FP8X4),
-                    lhsT_scale=zs[cc, h][:, cols],
+                    lhsT=zc[cc, i // 2][:, cols].bitcast(FP8X4),
+                    lhsT_scale=zs[cc, i // 2][:, cols],
                     rhs=mw[:, cc, 2 * n0 : 2 * n0 + 1024].bitcast(FP4X4),
                     rhs_scale=msc[:, cc, n0 : n0 + 512],
                     start=(cc == 0),
                     stop=(cc == C - 1),
                 )
-            nc.vector.tensor_tensor(yt[i][:, n0 : n0 + 512], acc[:], c_bc[:, n0 : n0 + 512], op=ADD)
-            nc.sync.dma_start(out=out_v[:, i, n0 : n0 + 512], in_=yt[i][:, n0 : n0 + 512])
+            nc.vector.tensor_tensor(y[:], acc[:], c_bc[:, n0 : n0 + 512], op=ADD)
+            nc.sync.dma_start(out=out_v[:, i, n0 : n0 + 512], in_=y[:])
 
-        sc, ve = nc.scalar.copy, nc.vector.tensor_copy
-        eng = {"s": nc.scalar.copy, "v": nc.vector.tensor_copy}
+        nc.vector.reciprocal(rt_col[:], tau_sb[:])
+        for i in range(2):
+            widen(i)
+        make_rtau(0)
+        make_rtau(1)
+        for i in range(2, 4):
+            widen(i)
+        x_turn(0)
+        head_turn(0)
+        x_quant(0)
+        x_turn(1)
+        nc.vector.tensor_copy(b_sb[:], b_bf[:])
+        head_quant(0)
+        widen(4)
+        head_turn(1)
+        x_quant(1)
+        widen(5)
+        head_quant(1)
 
-        def head_prep(cc):
-            for s in range(S):
-                head_turn(cc, s, eng[HCP[4 * cc + s]])
-                if s % 2 == 1:
-                    head_quant(cc, s // 2)
+        steps = [("z", cc, 0, a) for cc in range(C) for a in range(2)]
+        steps = steps + [("z", cc, 1, a) for cc in range(2) for a in range(2)]
+        for cc in range(2, C):
+            steps = steps + [("y", cc - 2, nh) for nh in range(2)] + [("z", cc, 1, a) for a in range(2)]
+        steps = steps + [("y", i, nh) for i in range(2, TT) for nh in range(2)]
 
-        def x_prep(h):
-            for i in range(first[h], first[h] + GROUPS[h]):
-                widen(i, WID[i])
-            for i in range(first[h], first[h] + GROUPS[h]):
-                x_turn(i, eng[XCP[i]])
-            x_quant(h)
-
-        def z_unit(cc, h):
-            for s in range(S):
-                stage1(cc, h, s)
-            z_inter(cc, h, eng[ZI[4 * h + cc]])
-            z_quant(cc, h)
-
-        for what, arg in ORDER:
-            if what == "x":
-                x_prep(arg)
-            if what == "r":
-                make_rtau()
-                nc.vector.tensor_copy(b_sb[:], b_bf[:])
-            if what == "h":
-                head_prep(arg)
-            if what == "z":
-                z_unit(*arg)
-            if what == "y":
-                stage2(arg, 0)
-                stage2(arg, 1)
+        to_inter = []
+        to_quant = []
+        for k, step in enumerate(steps):
+            if k < 6:
+                head_turn(k + 2)
+            if k in XT_AT:
+                x_turn(2 + XT_AT.index(k))
+            ready = list(to_quant)
+            to_quant.clear()
+            if to_inter:
+                to_quant.append(to_inter.pop(0))
+                z_inter(*to_quant[-1])
+            if step[0] == "z":
+                cc, h, a = step[1:]
+                stage1(cc, h, 2 * a)
+                if k < 6:
+                    head_quant(k + 2)
+                stage1(cc, h, 2 * a + 1)
+                if k in W_AT:
+                    widen(6 + W_AT.index(k))
+                if k in XQ_AT:
+                    x_quant(2 + XQ_AT.index(k))
+                if a == 1:
+                    to_inter.extend([(cc, 2 * h), (cc, 2 * h + 1)])
+            else:
+                stage2(*step[1:])
+            for item in ready:
+                z_quant(*item)

@@ -28,6 +28,17 @@ XT_AT = (1, 3)
 XQ_AT = (2, 4)
 W_AT = (0, 1)
 SCALAR_BLOCKS = 2
+FINE_END = 1
+PARKED = 0
+PARK_G = 0
+ZQ_LAG = 1
+Y_BEFORE = (5, 7)
+UNPARK = 4
+WARM0 = 0
+WARM1 = 0
+W_PRO = 2
+S_TILES = ()
+RUN16 = 0
 
 
 def tile_teacher_logits_remap_d4_kernel(tc, x_bytes, x_scale, head, b, tau, map_words, map_scales, c, out):
@@ -61,8 +72,10 @@ def tile_teacher_logits_remap_d4_kernel(tc, x_bytes, x_scale, head, b, tau, map_
         def load_head(e):
             nc.sync.dma_start(out=hraw[e][:], in_=head_v[e // 2, :, 2 * (e % 2) : 2 * (e % 2) + 2, :])
 
+        zeros = keep.tile([P, 512], BF16, name="zeros")
+        if WARM0 + WARM1:
+            nc.vector.memset(zeros[:], 0.0)
         make_identity(nc, ident[:])
-        nc.vector.memset(msc[:].rearrange("p c n -> p (c n)").bitcast(I32), 0)
         nc.sync.dma_start(out=tau_sb[:], in_=tau.rearrange("(p i) -> p i", i=TT))
         nc.sync.dma_start(out=xs[:], in_=x_scale.rearrange("(p i) j -> p i j", i=TT))
         load_x(0)
@@ -75,6 +88,9 @@ def tile_teacher_logits_remap_d4_kernel(tc, x_bytes, x_scale, head, b, tau, map_
         load_x(3)
         for e in range(3, 2 * C):
             load_head(e)
+        rt_col = keep.tile([P, TT], F32, name="rt_col")
+        nc.vector.reciprocal(rt_col[:], tau_sb[:])
+        nc.vector.memset(msc[:].rearrange("p c n -> p (c n)").bitcast(I32), 0)
         for q in range(4):
             nc.sync.dma_start(
                 out=msc[32 * q : 32 * q + 4, :, :].bitcast(I32),
@@ -83,7 +99,6 @@ def tile_teacher_logits_remap_d4_kernel(tc, x_bytes, x_scale, head, b, tau, map_
         nc.sync.dma_start(out=mw[:].bitcast(I32), in_=map_words.rearrange("c p n -> p c n").bitcast(I32))
         nc.sync.dma_start(out=c_bc[:], in_=c.partition_broadcast(P))
 
-        rt_col = keep.tile([P, TT], F32, name="rt_col")
         b_sb = keep.tile([P, C, S], F32, name="b_sb")
         rtau = [keep.tile([P, 4, P], F32, name=f"rtau{h}") for h in range(2)]
 
@@ -101,7 +116,9 @@ def tile_teacher_logits_remap_d4_kernel(tc, x_bytes, x_scale, head, b, tau, map_
         def widen(i):
             for j in range(K // B):
                 src = xb[i // 2][:, i % 2, j * B : (j + 1) * B].bitcast(FP8)
-                if i >= 2:
+                if i in S_TILES:
+                    nc.scalar.activation(xw[i][:, j * B : (j + 1) * B], src, COPY, scale=xs[:, i, j : j + 1])
+                elif i >= 2:
                     dst = xw[i][:].rearrange("p (g u q r e) -> p g q r u e", g=G, u=2, q=4, e=2)[:, j // 4, j % 4]
                     nc.vector.tensor_scalar(dst, src.rearrange("p (r u e) -> p r u e", u=2, e=2), xs[:, i, j : j + 1], None, op0=MULT)
                 elif j < SCALAR_BLOCKS:
@@ -119,7 +136,7 @@ def tile_teacher_logits_remap_d4_kernel(tc, x_bytes, x_scale, head, b, tau, map_
 
         def x_turn(q):
             for ii in range(2):
-                turned = turn(xw[2 * q + ii][:].bitcast(F32), q >= 1)
+                turned = turn(xw[2 * q + ii][:].bitcast(F32), q >= 1 and 2 * q + ii not in S_TILES)
                 dst = xT[q][:, :, ii * P : (ii + 1) * P, :].rearrange("p g r t -> p g (r t)").bitcast(F32)
                 nc.scalar.copy(dst.rearrange("p g (r u) -> p g r u", u=2), turned)
 
@@ -184,25 +201,51 @@ def tile_teacher_logits_remap_d4_kernel(tc, x_bytes, x_scale, head, b, tau, map_
             zs[cc, q] = keep.tile([P, 2 * P], U8, name=f"zs{cc}_{q}", align_bytes=64)
             nc.vector.quantize_mx(out=zc[cc, q][:].bitcast(FP8X4), scales=zs[cc, q][:], in_=zi[cc, q][:].rearrange("p n s -> p (n s)"))
 
-        def stage2(i, nh):
+        parked = []
+
+        def finish(src, i, n0, width, eng=nc.vector):
+            y = work.tile([P, width], F32, name="y", bufs=6)
+            eng.tensor_tensor(y[:], src, c_bc[:, n0 : n0 + width], op=ADD)
+            nc.sync.dma_start(out=out_v[:, i, n0 : n0 + width], in_=y[:])
+
+        def stage2_group(i, n0, width):
             cols = slice((i % 2) * P, (i % 2 + 1) * P)
-            n0 = 512 * nh
-            y = work.tile([P, 512], F32, name="y", bufs=6)
-            acc = bank([P, 512])
+            acc = bank([P, width])
             for cc in range(C):
                 nc.tensor.matmul_mx(
                     out=acc[:],
                     lhsT=zc[cc, i // 2][:, cols].bitcast(FP8X4),
                     lhsT_scale=zs[cc, i // 2][:, cols],
-                    rhs=mw[:, cc, 2 * n0 : 2 * n0 + 1024].bitcast(FP4X4),
-                    rhs_scale=msc[:, cc, n0 : n0 + 512],
+                    rhs=mw[:, cc, 2 * n0 : 2 * (n0 + width)].bitcast(FP4X4),
+                    rhs_scale=msc[:, cc, n0 : n0 + width],
                     start=(cc == 0),
                     stop=(cc == C - 1),
                 )
-            nc.vector.tensor_tensor(y[:], acc[:], c_bc[:, n0 : n0 + 512], op=ADD)
-            nc.sync.dma_start(out=out_v[:, i, n0 : n0 + 512], in_=y[:])
+            return acc
 
-        nc.vector.reciprocal(rt_col[:], tau_sb[:])
+        def stage2(i, nh):
+            if (i, nh) == (TT - 1, 1) and FINE_END:
+                for n0 in range(512, N, P):
+                    finish(stage2_group(i, n0, P)[:], i, n0, P)
+            elif i < PARKED:
+                raw = keep.tile([P, 512], F32, name=f"raw{i}_{nh}")
+                nc.scalar.copy(raw[:], stage2_group(i, 512 * nh, 512)[:])
+                if PARK_G:
+                    finish(raw[:], i, 512 * nh, 512, nc.gpsimd)
+                else:
+                    parked.append((raw[:], i, 512 * nh, 512))
+            else:
+                finish(stage2_group(i, 512 * nh, 512)[:], i, 512 * nh, 512)
+                if i >= UNPARK and parked:
+                    finish(*parked.pop(0))
+
+        def warm(n, width):
+            if n:
+                scratch = bank([P, 512])
+            for r in range(n):
+                nc.tensor.matmul(scratch[:, :width], lhsT=zeros[:, :P], rhs=zeros[:, :width], start=True, stop=True)
+
+        warm(WARM0, 512)
         for i in range(2):
             widen(i)
         make_rtau(0)
@@ -210,28 +253,37 @@ def tile_teacher_logits_remap_d4_kernel(tc, x_bytes, x_scale, head, b, tau, map_
         for i in range(2, 4):
             widen(i)
         x_turn(0)
+        warm(WARM1, 256)
         head_turn(0)
+        warm(WARM1, 256)
         x_quant(0)
         x_turn(1)
         nc.vector.tensor_copy(b_sb[:], b_bf[:])
         head_quant(0)
         widen(4)
+        warm(WARM1, 256)
         head_turn(1)
+        warm(WARM1, 256)
         x_quant(1)
         widen(5)
         head_quant(1)
 
         steps = [("z", cc, 0, a) for cc in range(C) for a in range(2)]
-        steps = steps + [("z", cc, 1, a) for cc in range(2) for a in range(2)]
-        for cc in range(2, C):
-            steps = steps + [("y", cc - 2, nh) for nh in range(2)] + [("z", cc, 1, a) for a in range(2)]
-        steps = steps + [("y", i, nh) for i in range(2, TT) for nh in range(2)]
+        second = [("y", i, nh) for i in range(TT) for nh in range(2)]
+        for n in range(2 * C):
+            if n in Y_BEFORE:
+                steps.append(second.pop(0))
+            steps.append(("z", n // 2, 1, n % 2))
+        steps = steps + second
 
         to_inter = []
         to_quant = []
         for k, step in enumerate(steps):
-            if k < 6:
+            if k < 6 and not RUN16:
                 head_turn(k + 2)
+            if k < 6 and RUN16 and k % 2 == 0:
+                head_turn(k + 2)
+                head_turn(k + 3)
             if k in XT_AT:
                 x_turn(2 + XT_AT.index(k))
             ready = list(to_quant)

@@ -27,7 +27,8 @@ HALF = 512
 XT_AT = (1, 3)
 XQ_AT = (2, 4)
 W_AT = (0, 1)
-SCALAR_BLOCKS = 2
+SCALAR_BLOCKS = 0
+FIRST_SORTED = 0
 FINE_END = 1
 PARKED = 0
 PARK_G = 0
@@ -118,7 +119,7 @@ def tile_teacher_logits_remap_d4_kernel(tc, x_bytes, x_scale, head, b, tau, map_
                 src = xb[i // 2][:, i % 2, j * B : (j + 1) * B].bitcast(FP8)
                 if i in S_TILES:
                     nc.scalar.activation(xw[i][:, j * B : (j + 1) * B], src, COPY, scale=xs[:, i, j : j + 1])
-                elif i >= 2:
+                elif i >= FIRST_SORTED:
                     dst = xw[i][:].rearrange("p (g u q r e) -> p g q r u e", g=G, u=2, q=4, e=2)[:, j // 4, j % 4]
                     nc.vector.tensor_scalar(dst, src.rearrange("p (r u e) -> p r u e", u=2, e=2), xs[:, i, j : j + 1], None, op0=MULT)
                 elif j < SCALAR_BLOCKS:
@@ -136,7 +137,7 @@ def tile_teacher_logits_remap_d4_kernel(tc, x_bytes, x_scale, head, b, tau, map_
 
         def x_turn(q):
             for ii in range(2):
-                turned = turn(xw[2 * q + ii][:].bitcast(F32), q >= 1 and 2 * q + ii not in S_TILES)
+                turned = turn(xw[2 * q + ii][:].bitcast(F32), 2 * q + ii >= FIRST_SORTED and 2 * q + ii not in S_TILES)
                 dst = xT[q][:, :, ii * P : (ii + 1) * P, :].rearrange("p g r t -> p g (r t)").bitcast(F32)
                 nc.scalar.copy(dst.rearrange("p g (r u) -> p g r u", u=2), turned)
 

@@ -31,12 +31,16 @@ SCALAR_BLOCKS = 0
 FIRST_SORTED = 0
 FINE_END = 1
 PARKED = 0
+ZI_G = ()
+ZI_V = ()
 PARK_G = 0
 ZQ_LAG = 1
 Y_BEFORE = (5, 7)
 UNPARK = 4
-WARM0 = 0
+WARM0 = 3
 WARM1 = 0
+WA = (1, 0, 1, 0, 1)
+WW = 512
 W_PRO = 2
 S_TILES = ()
 RUN16 = 0
@@ -192,10 +196,14 @@ def tile_teacher_logits_remap_d4_kernel(tc, x_bytes, x_scale, head, b, tau, map_
 
         def z_inter(cc, q):
             zi[cc, q] = work.tile([P, 2 * P, S], BF16, name="zi", align_bytes=64, bufs=4)
-            nc.scalar.copy(
-                zi[cc, q][:].rearrange("p (n i) s -> p n s i", i=4),
-                zp[cc, q // 2][:, :, (q % 2) * 2 * P : (q % 2 + 1) * 2 * P].rearrange("p s (n i) -> p n s i", i=4),
-            )
+            dst = zi[cc, q][:].rearrange("p (n i) s -> p n s i", i=4)
+            src = zp[cc, q // 2][:, :, (q % 2) * 2 * P : (q % 2 + 1) * 2 * P].rearrange("p s (n i) -> p n s i", i=4)
+            if 4 * cc + q in ZI_G:
+                nc.gpsimd.tensor_scalar(dst, src, 1.0, 0.0, op0=MULT, op1=ADD)
+            elif 4 * cc + q in ZI_V:
+                nc.vector.tensor_copy(dst, src)
+            else:
+                nc.scalar.copy(dst, src)
 
         def z_quant(cc, q):
             zc[cc, q] = keep.tile([P, 2 * P], U32, name=f"zc{cc}_{q}", align_bytes=64)
@@ -251,20 +259,21 @@ def tile_teacher_logits_remap_d4_kernel(tc, x_bytes, x_scale, head, b, tau, map_
             widen(i)
         make_rtau(0)
         make_rtau(1)
+        warm(WA[0], 512)
         for i in range(2, 4):
             widen(i)
         x_turn(0)
-        warm(WARM1, 256)
+        warm(WA[1], WW)
         head_turn(0)
-        warm(WARM1, 256)
+        warm(WA[2], WW)
         x_quant(0)
         x_turn(1)
         nc.vector.tensor_copy(b_sb[:], b_bf[:])
         head_quant(0)
         widen(4)
-        warm(WARM1, 256)
+        warm(WA[3], WW)
         head_turn(1)
-        warm(WARM1, 256)
+        warm(WA[4], WW)
         x_quant(1)
         widen(5)
         head_quant(1)

@@ -25,12 +25,32 @@ C = 4
 S = 4
 HALF = 512
 XT_AT = (1, 3)
-XQ_AT = (2, 4)
+XQ_AT = (2, 3)
 W_AT = (0, 1)
 SCALAR_BLOCKS = 0
 FIRST_SORTED = 0
 FINE_END = 1
 PARKED = 0
+LEAD = 0
+MSC_G = 0
+B_BF = 1
+SPLIT0 = 0
+MAP_AT = -1
+XS_FIRST = 0
+ZIB = 3
+YB = 19
+ZQ_SPLIT = (3, 7)
+REV_FROM = 6
+HQ_FIRST = ()
+ZQ_FROM = 0
+ZQ_NOW = ()
+END_S = 0
+Y_HOLD = ()
+SMALL_S = 2
+H2_FIRST = 0
+XQ_MID = 0
+XQ_FIRST = -1
+VIA_S = ()
 ZI_G = ()
 ZI_V = ()
 PARK_G = 0
@@ -62,7 +82,8 @@ def tile_teacher_logits_remap_d4_kernel(tc, x_bytes, x_scale, head, b, tau, map_
             return psum.tile(shape, F32, name="bank", tag="bank", bufs=8)
 
         xs = keep.tile([P, TT, K // B], F32, name="xs")
-        xb = [keep.tile([P, 2, K], U8, name=f"xb{q}") for q in range(4)]
+        xb = [keep.tile([P, K], U8, name=f"xb{i}") for i in range(2)] if SPLIT0 else []
+        xb2 = [keep.tile([P, 2, K], U8, name=f"xbp{q}") for q in range(4)]
         hraw = [keep.tile([P, 2, K], BF16, name=f"hraw{e}") for e in range(2 * C)]
         b_bf = keep.tile([P, C, S], BF16, name="b_bf")
         tau_sb = keep.tile([P, TT], BF16, name="tau_sb")
@@ -72,7 +93,11 @@ def tile_teacher_logits_remap_d4_kernel(tc, x_bytes, x_scale, head, b, tau, map_
         ident = keep.tile([P, P], F32, name="ident")
 
         def load_x(q):
-            nc.sync.dma_start(out=xb[q][:], in_=x_v[:, 2 * q : 2 * q + 2, :])
+            if q == 0 and SPLIT0:
+                for i in range(2):
+                    nc.sync.dma_start(out=xb[i][:], in_=x_v[:, i, :])
+            else:
+                nc.sync.dma_start(out=xb2[q][:], in_=x_v[:, 2 * q : 2 * q + 2, :])
 
         def load_head(e):
             nc.sync.dma_start(out=hraw[e][:], in_=head_v[e // 2, :, 2 * (e % 2) : 2 * (e % 2) + 2, :])
@@ -81,28 +106,40 @@ def tile_teacher_logits_remap_d4_kernel(tc, x_bytes, x_scale, head, b, tau, map_
         if WARM0 + WARM1:
             nc.vector.memset(zeros[:], 0.0)
         make_identity(nc, ident[:])
-        nc.sync.dma_start(out=tau_sb[:], in_=tau.rearrange("(p i) -> p i", i=TT))
-        nc.sync.dma_start(out=xs[:], in_=x_scale.rearrange("(p i) j -> p i j", i=TT))
+        small = nc.scalar if SMALL_S == 1 else nc.sync
+        small.dma_start(out=tau_sb[:], in_=tau.rearrange("(p i) -> p i", i=TT))
+        small.dma_start(out=xs[:], in_=x_scale.rearrange("(p i) j -> p i j", i=TT))
+        if SMALL_S:
+            nc.scalar.dma_start(out=b_bf[:], in_=b.rearrange("(c p s) -> p c s", p=P, s=S))
         load_x(0)
         load_x(1)
         load_head(0)
         load_head(1)
-        nc.sync.dma_start(out=b_bf[:], in_=b.rearrange("(c p s) -> p c s", p=P, s=S))
+        if not SMALL_S:
+            nc.sync.dma_start(out=b_bf[:], in_=b.rearrange("(c p s) -> p c s", p=P, s=S))
+        if H2_FIRST:
+            load_head(2)
         load_x(2)
-        load_head(2)
+        if not H2_FIRST:
+            load_head(2)
         load_x(3)
         for e in range(3, 2 * C):
             load_head(e)
         rt_col = keep.tile([P, TT], F32, name="rt_col")
         nc.vector.reciprocal(rt_col[:], tau_sb[:])
-        nc.vector.memset(msc[:].rearrange("p c n -> p (c n)").bitcast(I32), 0)
-        for q in range(4):
-            nc.sync.dma_start(
-                out=msc[32 * q : 32 * q + 4, :, :].bitcast(I32),
-                in_=map_scales[:, 4 * q : 4 * q + 4, :].rearrange("c r n -> r c n").bitcast(I32),
-            )
-        nc.sync.dma_start(out=mw[:].bitcast(I32), in_=map_words.rearrange("c p n -> p c n").bitcast(I32))
-        nc.sync.dma_start(out=c_bc[:], in_=c.partition_broadcast(P))
+
+        def load_map():
+            (nc.gpsimd if MSC_G else nc.vector).memset(msc[:].rearrange("p c n -> p (c n)").bitcast(I32), 0)
+            for q in range(4):
+                nc.sync.dma_start(
+                    out=msc[32 * q : 32 * q + 4, :, :].bitcast(I32),
+                    in_=map_scales[:, 4 * q : 4 * q + 4, :].rearrange("c r n -> r c n").bitcast(I32),
+                )
+            nc.sync.dma_start(out=mw[:].bitcast(I32), in_=map_words.rearrange("c p n -> p c n").bitcast(I32))
+            nc.sync.dma_start(out=c_bc[:], in_=c.partition_broadcast(P))
+
+        if MAP_AT == -1:
+            load_map()
 
         b_sb = keep.tile([P, C, S], F32, name="b_sb")
         rtau = [keep.tile([P, 4, P], F32, name=f"rtau{h}") for h in range(2)]
@@ -120,7 +157,7 @@ def tile_teacher_logits_remap_d4_kernel(tc, x_bytes, x_scale, head, b, tau, map_
 
         def widen(i):
             for j in range(K // B):
-                src = xb[i // 2][:, i % 2, j * B : (j + 1) * B].bitcast(FP8)
+                src = (xb[i][:] if i < 2 and SPLIT0 else xb2[i // 2][:, i % 2])[:, j * B : (j + 1) * B].bitcast(FP8)
                 if i in S_TILES:
                     nc.scalar.activation(xw[i][:, j * B : (j + 1) * B], src, COPY, scale=xs[:, i, j : j + 1])
                 elif i >= FIRST_SORTED:
@@ -176,8 +213,6 @@ def tile_teacher_logits_remap_d4_kernel(tc, x_bytes, x_scale, head, b, tau, map_
         zs = {}
 
         def stage1(cc, h, s):
-            if s == 0:
-                zp[cc, h] = work.tile([P, S, HALF], BF16, name="zp", bufs=3)
             acc = bank([P, HALF])
             e = 2 * cc + s // 2
             for g in range(G):
@@ -190,63 +225,56 @@ def tile_teacher_logits_remap_d4_kernel(tc, x_bytes, x_scale, head, b, tau, map_
                     start=(g == 0),
                     stop=(g == G - 1),
                 )
+            return acc
+
+        def z_out(cc, h, s, acc):
+            if (cc, h) not in zp:
+                zp[cc, h] = work.tile([P, S, HALF], BF16, name="zp", bufs=3)
             nc.vector.scalar_tensor_tensor(
-                zp[cc, h][:, s, :], acc[:], b_sb[:, cc, s : s + 1], rtau[h][:].rearrange("p i n -> p (i n)"), op0=ADD, op1=MULT
+                zp[cc, h][:, s, :], acc[:], (b_bf if B_BF else b_sb)[:, cc, s : s + 1], rtau[h][:].rearrange("p i n -> p (i n)"), op0=ADD, op1=MULT
             )
 
         def z_inter(cc, q):
-            zi[cc, q] = work.tile([P, 2 * P, S], BF16, name="zi", align_bytes=64, bufs=4)
-            dst = zi[cc, q][:].rearrange("p (n i) s -> p n s i", i=4)
-            src = zp[cc, q // 2][:, :, (q % 2) * 2 * P : (q % 2 + 1) * 2 * P].rearrange("p s (n i) -> p n s i", i=4)
-            if 4 * cc + q in ZI_G:
-                nc.gpsimd.tensor_scalar(dst, src, 1.0, 0.0, op0=MULT, op1=ADD)
-            elif 4 * cc + q in ZI_V:
-                nc.vector.tensor_copy(dst, src)
-            else:
-                nc.scalar.copy(dst, src)
+            h, a = divmod(q, 2)
+            if a == 0:
+                zi[cc, h] = work.tile([P, HALF, S], BF16, name="zi", align_bytes=64, bufs=ZIB)
+            cols = slice(a * 2 * P, (a + 1) * 2 * P)
+            nc.scalar.copy(zi[cc, h][:, cols, :].rearrange("p (n i) s -> p n s i", i=4), zp[cc, h][:, :, cols].rearrange("p s (n i) -> p n s i", i=4))
 
         def z_quant(cc, q):
-            zc[cc, q] = keep.tile([P, 2 * P], U32, name=f"zc{cc}_{q}", align_bytes=64)
-            zs[cc, q] = keep.tile([P, 2 * P], U8, name=f"zs{cc}_{q}", align_bytes=64)
-            nc.vector.quantize_mx(out=zc[cc, q][:].bitcast(FP8X4), scales=zs[cc, q][:], in_=zi[cc, q][:].rearrange("p n s -> p (n s)"))
+            h, a = divmod(q, 2)
+            if a == 0:
+                zc[cc, h] = keep.tile([P, HALF], U32, name=f"zc{cc}_{h}", align_bytes=64)
+                zs[cc, h] = keep.tile([P, HALF], U8, name=f"zs{cc}_{h}", align_bytes=64)
+            if 4 * h + cc in ZQ_SPLIT:
+                cols = slice(a * 2 * P, (a + 1) * 2 * P)
+            elif a == 1:
+                cols = slice(0, HALF)
+            else:
+                return
+            nc.vector.quantize_mx(out=zc[cc, h][:, cols].bitcast(FP8X4), scales=zs[cc, h][:, cols], in_=zi[cc, h][:, cols, :].rearrange("p n s -> p (n s)"))
 
         parked = []
 
         def finish(src, i, n0, width, eng=nc.vector):
-            y = work.tile([P, width], F32, name="y", bufs=6)
+            y = work.tile([P, width], F32, name="y", bufs=YB)
             eng.tensor_tensor(y[:], src, c_bc[:, n0 : n0 + width], op=ADD)
-            nc.sync.dma_start(out=out_v[:, i, n0 : n0 + width], in_=y[:])
+            (nc.scalar if width == P and END_S else nc.sync).dma_start(out=out_v[:, i, n0 : n0 + width], in_=y[:])
 
         def stage2_group(i, n0, width):
-            cols = slice((i % 2) * P, (i % 2 + 1) * P)
+            cols = slice((i % 4) * P, (i % 4 + 1) * P)
             acc = bank([P, width])
             for cc in range(C):
                 nc.tensor.matmul_mx(
                     out=acc[:],
-                    lhsT=zc[cc, i // 2][:, cols].bitcast(FP8X4),
-                    lhsT_scale=zs[cc, i // 2][:, cols],
+                    lhsT=zc[cc, i // 4][:, cols].bitcast(FP8X4),
+                    lhsT_scale=zs[cc, i // 4][:, cols],
                     rhs=mw[:, cc, 2 * n0 : 2 * (n0 + width)].bitcast(FP4X4),
                     rhs_scale=msc[:, cc, n0 : n0 + width],
                     start=(cc == 0),
                     stop=(cc == C - 1),
                 )
             return acc
-
-        def stage2(i, nh):
-            if (i, nh) == (TT - 1, 1) and FINE_END:
-                for n0 in range(512, N, P):
-                    finish(stage2_group(i, n0, P)[:], i, n0, P)
-            elif i < PARKED:
-                raw = keep.tile([P, 512], F32, name=f"raw{i}_{nh}")
-                nc.scalar.copy(raw[:], stage2_group(i, 512 * nh, 512)[:])
-                if PARK_G:
-                    finish(raw[:], i, 512 * nh, 512, nc.gpsimd)
-                else:
-                    parked.append((raw[:], i, 512 * nh, 512))
-            else:
-                finish(stage2_group(i, 512 * nh, 512)[:], i, 512 * nh, 512)
-                if i >= UNPARK and parked:
-                    finish(*parked.pop(0))
 
         def warm(n, width):
             if n:
@@ -266,16 +294,22 @@ def tile_teacher_logits_remap_d4_kernel(tc, x_bytes, x_scale, head, b, tau, map_
         warm(WA[1], WW)
         head_turn(0)
         warm(WA[2], WW)
+        if MAP_AT == -2:
+            load_map()
         x_quant(0)
         x_turn(1)
-        nc.vector.tensor_copy(b_sb[:], b_bf[:])
+        if not B_BF:
+            nc.vector.tensor_copy(b_sb[:], b_bf[:])
+        if MAP_AT == -3:
+            load_map()
         head_quant(0)
-        widen(4)
+        if not H2_FIRST:
+            widen(4)
         warm(WA[3], WW)
         head_turn(1)
         warm(WA[4], WW)
         x_quant(1)
-        widen(5)
+        widen(4 if H2_FIRST else 5)
         head_quant(1)
 
         steps = [("z", cc, 0, a) for cc in range(C) for a in range(2)]
@@ -286,16 +320,39 @@ def tile_teacher_logits_remap_d4_kernel(tc, x_bytes, x_scale, head, b, tau, map_
             steps.append(("z", n // 2, 1, n % 2))
         steps = steps + second
 
-        to_inter = []
-        to_quant = []
-        for k, step in enumerate(steps):
+        accs = {}
+
+        def multiply(k):
+            step = steps[k]
             if k < 6 and not RUN16:
                 head_turn(k + 2)
             if k < 6 and RUN16 and k % 2 == 0:
                 head_turn(k + 2)
                 head_turn(k + 3)
-            if k in XT_AT:
-                x_turn(2 + XT_AT.index(k))
+            for q in range(2):
+                if k == XT_AT[q]:
+                    x_turn(2 + q)
+            if step[0] == "z":
+                cc, h, a = step[1:]
+                accs[k] = [stage1(cc, h, 2 * a), stage1(cc, h, 2 * a + 1)]
+            else:
+                i, nh = step[1:]
+                width = P if k == len(steps) - 1 else 512
+                accs[k] = [(stage2_group(i, n0, width)[:], i, n0, width) for n0 in range(512 * nh, 512 * (nh + 1), width)]
+                if 2 * i + nh in VIA_S:
+                    raw = keep.tile([P, 512], F32, name=f"raw{i}_{nh}")
+                    nc.scalar.copy(raw[:], accs[k][0][0])
+                    accs[k] = [(raw[:], i, 512 * nh, 512)]
+
+        held = []
+        late = []
+        to_inter = []
+        to_quant = []
+        done = 0
+        for k, step in enumerate(steps):
+            while done <= min(k + (LEAD if k >= 8 else 0), len(steps) - 1):
+                multiply(done)
+                done = done + 1
             ready = list(to_quant)
             to_quant.clear()
             if to_inter:
@@ -303,17 +360,39 @@ def tile_teacher_logits_remap_d4_kernel(tc, x_bytes, x_scale, head, b, tau, map_
                 z_inter(*to_quant[-1])
             if step[0] == "z":
                 cc, h, a = step[1:]
-                stage1(cc, h, 2 * a)
-                if k < 6:
+                if k == XQ_FIRST:
+                    x_quant(3)
+                rev = 1 if k >= REV_FROM else 0
+                if k < 6 and k in HQ_FIRST:
                     head_quant(k + 2)
-                stage1(cc, h, 2 * a + 1)
+                z_out(cc, h, 2 * a + rev, accs[k][rev])
+                if k < 6 and k not in HQ_FIRST:
+                    head_quant(k + 2)
+                if k in XQ_AT and XQ_MID:
+                    x_quant(2 + XQ_AT.index(k))
+                z_out(cc, h, 2 * a + 1 - rev, accs[k][1 - rev])
                 if k in W_AT:
-                    widen(6 + W_AT.index(k))
-                if k in XQ_AT:
+                    widen(TT - len(W_AT) + W_AT.index(k))
+                if k in XQ_AT and not XQ_MID:
                     x_quant(2 + XQ_AT.index(k))
                 if a == 1:
                     to_inter.extend([(cc, 2 * h), (cc, 2 * h + 1)])
+            elif 2 * step[1] + step[2] < PARKED:
+                parked.extend(accs[k])
+            elif 2 * step[1] + step[2] in Y_HOLD:
+                held.extend(accs[k])
             else:
-                stage2(*step[1:])
-            for item in ready:
-                z_quant(*item)
+                for item in accs[k] + held:
+                    finish(*item)
+                held.clear()
+                if step[1] >= UNPARK and parked:
+                    finish(*parked.pop(0))
+            if k == MAP_AT:
+                load_map()
+            if k in ZQ_NOW:
+                ready.extend(to_quant)
+                to_quant.clear()
+            late.extend(ready)
+            for n in range(2):
+                if late and k >= ZQ_FROM:
+                    z_quant(*late.pop(0))

@@ -85,7 +85,8 @@ def tile_teacher_logits_remap_d4_kernel(tc, x_bytes, x_scale, head, b, tau, map_
         xb = [keep.tile([P, K], U8, name=f"xb{i}") for i in range(2)] if SPLIT0 else []
         xb2 = [keep.tile([P, 2, K], U8, name=f"xbp{q}") for q in range(4)]
         hraw = [keep.tile([P, 2, K], BF16, name=f"hraw{e}") for e in range(2 * C)]
-        b_bf = keep.tile([P, C, S], BF16, name="b_bf")
+        b_first = keep.tile([P, S], BF16, name="b_first")
+        b_rest = keep.tile([P, C - 1, S], BF16, name="b_rest")
         tau_sb = keep.tile([P, TT], BF16, name="tau_sb")
         msc = keep.tile([P, C, N], U8, name="msc", align_bytes=64)
         mw = keep.tile([P, C, 2 * N], U8, name="mw", align_bytes=64)
@@ -109,14 +110,12 @@ def tile_teacher_logits_remap_d4_kernel(tc, x_bytes, x_scale, head, b, tau, map_
         small = nc.scalar if SMALL_S == 1 else nc.sync
         small.dma_start(out=tau_sb[:], in_=tau.rearrange("(p i) -> p i", i=TT))
         small.dma_start(out=xs[:], in_=x_scale.rearrange("(p i) j -> p i j", i=TT))
-        if SMALL_S:
-            nc.scalar.dma_start(out=b_bf[:], in_=b.rearrange("(c p s) -> p c s", p=P, s=S))
+        b_v = b.rearrange("(c p s) -> p c s", p=P, s=S)
         load_x(0)
         load_x(1)
         load_head(0)
         load_head(1)
-        if not SMALL_S:
-            nc.sync.dma_start(out=b_bf[:], in_=b.rearrange("(c p s) -> p c s", p=P, s=S))
+        nc.sync.dma_start(out=b_first[:], in_=b_v[:, 0, :])
         if H2_FIRST:
             load_head(2)
         load_x(2)
@@ -125,6 +124,8 @@ def tile_teacher_logits_remap_d4_kernel(tc, x_bytes, x_scale, head, b, tau, map_
         load_x(3)
         for e in range(3, 2 * C):
             load_head(e)
+            if e == 4:
+                nc.sync.dma_start(out=b_rest[:], in_=b_v[:, 1:, :])
         rt_col = keep.tile([P, TT], F32, name="rt_col")
         nc.vector.reciprocal(rt_col[:], tau_sb[:])
 
@@ -141,7 +142,6 @@ def tile_teacher_logits_remap_d4_kernel(tc, x_bytes, x_scale, head, b, tau, map_
         if MAP_AT == -1:
             load_map()
 
-        b_sb = keep.tile([P, C, S], F32, name="b_sb")
         rtau = [keep.tile([P, 4, P], F32, name=f"rtau{h}") for h in range(2)]
 
         def make_rtau(h):
@@ -231,7 +231,7 @@ def tile_teacher_logits_remap_d4_kernel(tc, x_bytes, x_scale, head, b, tau, map_
             if (cc, h) not in zp:
                 zp[cc, h] = work.tile([P, S, HALF], BF16, name="zp", bufs=3)
             nc.vector.scalar_tensor_tensor(
-                zp[cc, h][:, s, :], acc[:], (b_bf if B_BF else b_sb)[:, cc, s : s + 1], rtau[h][:].rearrange("p i n -> p (i n)"), op0=ADD, op1=MULT
+                zp[cc, h][:, s, :], acc[:], (b_first[:] if cc == 0 else b_rest[:, cc - 1])[:, s : s + 1], rtau[h][:].rearrange("p i n -> p (i n)"), op0=ADD, op1=MULT
             )
 
         def z_inter(cc, q):
@@ -298,8 +298,6 @@ def tile_teacher_logits_remap_d4_kernel(tc, x_bytes, x_scale, head, b, tau, map_
             load_map()
         x_quant(0)
         x_turn(1)
-        if not B_BF:
-            nc.vector.tensor_copy(b_sb[:], b_bf[:])
         if MAP_AT == -3:
             load_map()
         head_quant(0)

@@ -24,7 +24,7 @@ TT = 8
 C = 4
 S = 4
 HALF = 512
-XT_AT = (1, 3)
+XT_AT = (0, 1, 2, 3)
 XQ_AT = (2, 3)
 W_AT = (0, 1)
 SCALAR_BLOCKS = 0
@@ -32,15 +32,18 @@ FIRST_SORTED = 0
 FINE_END = 1
 PARKED = 0
 LEAD = 0
-MSC_G = 0
+ZI_SKIP = (4,)
+ZPB = 4
+ZI_TWO = (6,)
+MSC_G = 1
 B_BF = 1
-SPLIT0 = 0
+SPLIT0 = 1
 MAP_AT = -1
 XS_FIRST = 0
 ZIB = 3
-YB = 19
-ZQ_SPLIT = (3, 7)
-REV_FROM = 6
+YB = 8
+ZQ_SPLIT = (0, 1, 2, 3, 4, 5, 6, 7)
+REV_FROM = 99
 HQ_FIRST = ()
 ZQ_FROM = 0
 ZQ_NOW = ()
@@ -59,7 +62,7 @@ Y_BEFORE = (5, 7)
 UNPARK = 4
 WARM0 = 3
 WARM1 = 0
-WA = (1, 0, 1, 0, 1)
+WA = (1, 1, 1, 0, 1)
 WW = 512
 W_PRO = 2
 S_TILES = ()
@@ -105,7 +108,7 @@ def tile_teacher_logits_remap_d4_kernel(tc, x_bytes, x_scale, head, b, tau, map_
 
         zeros = keep.tile([P, 512], BF16, name="zeros")
         if WARM0 + WARM1:
-            nc.vector.memset(zeros[:], 0.0)
+            (nc.gpsimd if MSC_G else nc.vector).memset(zeros[:].bitcast(I32), 0)
         make_identity(nc, ident[:])
         small = nc.scalar if SMALL_S == 1 else nc.sync
         small.dma_start(out=tau_sb[:], in_=tau.rearrange("(p i) -> p i", i=TT))
@@ -176,8 +179,8 @@ def tile_teacher_logits_remap_d4_kernel(tc, x_bytes, x_scale, head, b, tau, map_
                     nc.tensor.transpose(tp[:, g, u, :], words[:, cols], ident[:])
             return tp[:].rearrange("p g u r -> p g r u")
 
-        def x_turn(q):
-            for ii in range(2):
+        def x_turn(q, tiles=(0, 1)):
+            for ii in tiles:
                 turned = turn(xw[2 * q + ii][:].bitcast(F32), 2 * q + ii >= FIRST_SORTED and 2 * q + ii not in S_TILES)
                 dst = xT[q][:, :, ii * P : (ii + 1) * P, :].rearrange("p g r t -> p g (r t)").bitcast(F32)
                 nc.scalar.copy(dst.rearrange("p g (r u) -> p g r u", u=2), turned)
@@ -229,7 +232,7 @@ def tile_teacher_logits_remap_d4_kernel(tc, x_bytes, x_scale, head, b, tau, map_
 
         def z_out(cc, h, s, acc):
             if (cc, h) not in zp:
-                zp[cc, h] = work.tile([P, S, HALF], BF16, name="zp", bufs=3)
+                zp[cc, h] = work.tile([P, S, HALF], BF16, name="zp", bufs=ZPB)
             nc.vector.scalar_tensor_tensor(
                 zp[cc, h][:, s, :], acc[:], (b_first[:] if cc == 0 else b_rest[:, cc - 1])[:, s : s + 1], rtau[h][:].rearrange("p i n -> p (i n)"), op0=ADD, op1=MULT
             )
@@ -327,9 +330,9 @@ def tile_teacher_logits_remap_d4_kernel(tc, x_bytes, x_scale, head, b, tau, map_
             if k < 6 and RUN16 and k % 2 == 0:
                 head_turn(k + 2)
                 head_turn(k + 3)
-            for q in range(2):
-                if k == XT_AT[q]:
-                    x_turn(2 + q)
+            for j in range(4):
+                if k == XT_AT[j]:
+                    x_turn(2 + j // 2, (j % 2,))
             if step[0] == "z":
                 cc, h, a = step[1:]
                 accs[k] = [stage1(cc, h, 2 * a), stage1(cc, h, 2 * a + 1)]
@@ -353,7 +356,10 @@ def tile_teacher_logits_remap_d4_kernel(tc, x_bytes, x_scale, head, b, tau, map_
                 done = done + 1
             ready = list(to_quant)
             to_quant.clear()
-            if to_inter:
+            if to_inter and k not in ZI_SKIP:
+                to_quant.append(to_inter.pop(0))
+                z_inter(*to_quant[-1])
+            if to_inter and k in ZI_TWO:
                 to_quant.append(to_inter.pop(0))
                 z_inter(*to_quant[-1])
             if step[0] == "z":
@@ -369,8 +375,9 @@ def tile_teacher_logits_remap_d4_kernel(tc, x_bytes, x_scale, head, b, tau, map_
                 if k in XQ_AT and XQ_MID:
                     x_quant(2 + XQ_AT.index(k))
                 z_out(cc, h, 2 * a + 1 - rev, accs[k][1 - rev])
-                if k in W_AT:
-                    widen(TT - len(W_AT) + W_AT.index(k))
+                for j in range(len(W_AT)):
+                    if W_AT[j] == k:
+                        widen(TT - len(W_AT) + j)
                 if k in XQ_AT and not XQ_MID:
                     x_quant(2 + XQ_AT.index(k))
                 if a == 1:

@@ -14,390 +14,302 @@ U8 = mybir.dt.uint8
 FP8 = mybir.dt.float8_e4m3fn
 FP8X4 = mybir.dt.float8_e4m3fn_x4
 FP4X4 = mybir.dt.float4_e2m1fn_x4
-COPY = mybir.ActivationFunctionType.Copy
 ADD = mybir.AluOpType.add
 MULT = mybir.AluOpType.mult
 
 P = 128
-G = 2
-TT = 8
-C = 4
-S = 4
-HALF = 512
-XT_AT = (0, 1, 2, 3)
-XQ_AT = (2, 3)
-W_AT = (0, 1)
-SCALAR_BLOCKS = 0
-FIRST_SORTED = 0
-FINE_END = 1
-PARKED = 0
-LEAD = 0
-ZI_SKIP = (4,)
-ZPB = 4
-ZI_TWO = (6,)
-MSC_G = 1
-B_BF = 1
-SPLIT0 = 1
-MAP_AT = -1
-XS_FIRST = 0
-ZIB = 3
-YB = 8
-ZQ_SPLIT = (0, 1, 2, 3, 4, 5, 6, 7)
-REV_FROM = 99
-HQ_FIRST = ()
-ZQ_FROM = 0
-ZQ_NOW = ()
-END_S = 0
-Y_HOLD = ()
-SMALL_S = 2
-H2_FIRST = 0
-XQ_MID = 0
-XQ_FIRST = -1
-VIA_S = ()
-ZI_G = ()
-ZI_V = ()
-PARK_G = 0
-ZQ_LAG = 1
-Y_BEFORE = (5, 7)
-UNPARK = 4
-WARM0 = 3
-WARM1 = 0
-WA = (1, 1, 1, 0, 1)
-WW = 512
-W_PRO = 2
-S_TILES = ()
-RUN16 = 0
+BANK = 512
+PASSES = K // 512
+TILES = T // P
+CHUNKS = V // 512
+SLOTS = 4
+PARTS = 2 * CHUNKS
+HALF = T // 2
+PAIR = 2 * P
+
+AHEAD = 2
+WOVEN = (5, 7)
+INTERLEAVE_SKIP = 3
+PUT_OFF = 2
+QUANT_MAX = 3
 
 
 def tile_teacher_logits_remap_d4_kernel(tc, x_bytes, x_scale, head, b, tau, map_words, map_scales, c, out):
     nc = tc.nc
-    x_v = x_bytes.rearrange("(p i) k -> p i k", i=TT)
-    head_v = head.rearrange("(c p s) k -> c p s k", p=P, s=S)
-    out_v = out.rearrange("(p i) n -> p i n", i=TT)
+    x_v = x_bytes.rearrange("(p i) k -> p i k", i=TILES)
+    head_v = head.rearrange("(c p s) k -> c p s k", p=P, s=SLOTS)
+    b_v = b.rearrange("(c p s) -> p c s", p=P, s=SLOTS)
+    out_v = out.rearrange("(p i) n -> p i n", i=TILES)
 
     with ExitStack() as ctx:
         keep = ctx.enter_context(tc.tile_pool(name="keep", bufs=1))
-        work = ctx.enter_context(tc.tile_pool(name="work", bufs=3))
+        work = ctx.enter_context(tc.tile_pool(name="work", bufs=1))
         psum = ctx.enter_context(tc.psum_pool(name="psum", bufs=1))
         ctx.enter_context(tc.manual_schedule())
 
         def bank(shape):
             return psum.tile(shape, F32, name="bank", tag="bank", bufs=8)
 
-        xs = keep.tile([P, TT, K // B], F32, name="xs")
-        xb = [keep.tile([P, K], U8, name=f"xb{i}") for i in range(2)] if SPLIT0 else []
-        xb2 = [keep.tile([P, 2, K], U8, name=f"xbp{q}") for q in range(4)]
-        hraw = [keep.tile([P, 2, K], BF16, name=f"hraw{e}") for e in range(2 * C)]
-        b_first = keep.tile([P, S], BF16, name="b_first")
-        b_rest = keep.tile([P, C - 1, S], BF16, name="b_rest")
-        tau_sb = keep.tile([P, TT], BF16, name="tau_sb")
-        msc = keep.tile([P, C, N], U8, name="msc", align_bytes=64)
-        mw = keep.tile([P, C, 2 * N], U8, name="mw", align_bytes=64)
-        c_bc = keep.tile([P, N], BF16, name="c_bc")
+        x_scale_sb = keep.tile([P, TILES, K // B], F32, name="x_scale_sb")
+        x_single = [keep.tile([P, K], U8, name=f"x_single{i}") for i in range(2)]
+        x_pair = {q: keep.tile([P, 2, K], U8, name=f"x_pair{q}") for q in range(1, TILES // 2)}
+        head_single = [keep.tile([P, K], BF16, name=f"head_single{s}") for s in range(2)]
+        head_part = {e: keep.tile([P, 2, K], BF16, name=f"head_part{e}") for e in range(1, PARTS)}
+        b_first = keep.tile([P, SLOTS], BF16, name="b_first")
+        b_rest = keep.tile([P, CHUNKS - 1, SLOTS], BF16, name="b_rest")
+        tau_sb = keep.tile([P, TILES], BF16, name="tau_sb")
+        map_scale_sb = keep.tile([P, CHUNKS, N], U8, name="map_scale_sb", align_bytes=64)
+        map_sb = keep.tile([P, CHUNKS, 2 * N], U8, name="map_sb", align_bytes=64)
+        c_rows = keep.tile([P, N], BF16, name="c_rows")
         ident = keep.tile([P, P], F32, name="ident")
+        zeros = keep.tile([P, BANK], BF16, name="zeros")
 
         def load_x(q):
-            if q == 0 and SPLIT0:
-                for i in range(2):
-                    nc.sync.dma_start(out=xb[i][:], in_=x_v[:, i, :])
-            else:
-                nc.sync.dma_start(out=xb2[q][:], in_=x_v[:, 2 * q : 2 * q + 2, :])
+            nc.sync.dma_start(out=x_pair[q][:], in_=x_v[:, 2 * q : 2 * q + 2, :])
 
         def load_head(e):
-            nc.sync.dma_start(out=hraw[e][:], in_=head_v[e // 2, :, 2 * (e % 2) : 2 * (e % 2) + 2, :])
+            nc.sync.dma_start(out=head_part[e][:], in_=head_v[e // 2, :, 2 * (e % 2) : 2 * (e % 2) + 2, :])
 
-        zeros = keep.tile([P, 512], BF16, name="zeros")
-        if WARM0 + WARM1:
-            (nc.gpsimd if MSC_G else nc.vector).memset(zeros[:].bitcast(I32), 0)
+        nc.gpsimd.memset(zeros[:].bitcast(I32), 0)
         make_identity(nc, ident[:])
-        small = nc.scalar if SMALL_S == 1 else nc.sync
-        small.dma_start(out=tau_sb[:], in_=tau.rearrange("(p i) -> p i", i=TT))
-        small.dma_start(out=xs[:], in_=x_scale.rearrange("(p i) j -> p i j", i=TT))
-        b_v = b.rearrange("(c p s) -> p c s", p=P, s=S)
-        load_x(0)
+        nc.gpsimd.memset(map_scale_sb[:].rearrange("p c n -> p (c n)").bitcast(I32), 0)
+
+        nc.sync.dma_start(out=tau_sb[:], in_=tau.rearrange("(p i) -> p i", i=TILES))
+        nc.sync.dma_start(out=x_scale_sb[:], in_=x_scale.rearrange("(p i) j -> p i j", i=TILES))
+        for i in range(2):
+            nc.sync.dma_start(out=x_single[i][:], in_=x_v[:, i, :])
+        nc.sync.dma_start(out=head_single[0][:], in_=head_v[0, :, 0, :])
         load_x(1)
-        load_head(0)
+        nc.sync.dma_start(out=head_single[1][:], in_=head_v[0, :, 1, :])
         load_head(1)
         nc.sync.dma_start(out=b_first[:], in_=b_v[:, 0, :])
-        if H2_FIRST:
-            load_head(2)
+        load_head(2)
         load_x(2)
-        if not H2_FIRST:
-            load_head(2)
+        load_head(3)
         load_x(3)
-        for e in range(3, 2 * C):
+        load_head(4)
+        nc.sync.dma_start(out=b_rest[:], in_=b_v[:, 1:, :])
+        for e in range(5, PARTS):
             load_head(e)
-            if e == 4:
-                nc.sync.dma_start(out=b_rest[:], in_=b_v[:, 1:, :])
-        rt_col = keep.tile([P, TT], F32, name="rt_col")
-        nc.vector.reciprocal(rt_col[:], tau_sb[:])
+        for q in range(4):
+            nc.sync.dma_start(
+                out=map_scale_sb[32 * q : 32 * q + 4, :, :].bitcast(I32),
+                in_=map_scales[:, 4 * q : 4 * q + 4, :].rearrange("c r n -> r c n").bitcast(I32),
+            )
+        nc.sync.dma_start(out=map_sb[:].bitcast(I32), in_=map_words.rearrange("c p n -> p c n").bitcast(I32))
+        nc.sync.dma_start(out=c_rows[:], in_=c.partition_broadcast(P))
 
-        def load_map():
-            (nc.gpsimd if MSC_G else nc.vector).memset(msc[:].rearrange("p c n -> p (c n)").bitcast(I32), 0)
-            for q in range(4):
-                nc.sync.dma_start(
-                    out=msc[32 * q : 32 * q + 4, :, :].bitcast(I32),
-                    in_=map_scales[:, 4 * q : 4 * q + 4, :].rearrange("c r n -> r c n").bitcast(I32),
-                )
-            nc.sync.dma_start(out=mw[:].bitcast(I32), in_=map_words.rearrange("c p n -> p c n").bitcast(I32))
-            nc.sync.dma_start(out=c_bc[:], in_=c.partition_broadcast(P))
+        def warm_up(count):
+            scratch = bank([P, BANK])
+            for n in range(count):
+                nc.tensor.matmul(scratch[:], lhsT=zeros[:, :P], rhs=zeros[:], start=True, stop=True)
 
-        if MAP_AT == -1:
-            load_map()
+        inv_tau_col = keep.tile([P, TILES], F32, name="inv_tau_col")
+        inv_tau = [keep.tile([P, 4, P], F32, name=f"inv_tau{h}") for h in range(2)]
 
-        rtau = [keep.tile([P, 4, P], F32, name=f"rtau{h}") for h in range(2)]
-
-        def make_rtau(h):
-            rp = bank([P, 4, P])
+        def spread_inv_tau(h):
+            rows = bank([P, 4, P])
             for ii in range(4):
-                nc.tensor.transpose(rp[:, ii, :], rt_col[:, 4 * h + ii : 4 * h + ii + 1].to_broadcast([P, P]), ident[:])
-            nc.scalar.copy(rtau[h][:], rp[:])
+                column = inv_tau_col[:, 4 * h + ii : 4 * h + ii + 1]
+                nc.tensor.transpose(rows[:, ii, :], column.to_broadcast([P, P]), ident[:])
+            nc.scalar.copy(inv_tau[h][:], rows[:])
 
-        xw = [keep.tile([P, K], BF16, name=f"xw{i}") for i in range(TT)]
-        xT = [keep.tile([P, G, 2 * P, 4], BF16, name=f"xT{q}", align_bytes=64) for q in range(4)]
-        xc = [keep.tile([P, G, HALF], U32, name=f"xc{h}", align_bytes=64) for h in range(2)]
-        xsc = [keep.tile([P, G, HALF], U8, name=f"xsc{h}", align_bytes=64) for h in range(2)]
+        x_wide = [keep.tile([P, K], BF16, name=f"x_wide{i}") for i in range(TILES)]
+        x_turned = [keep.tile([P, PASSES, PAIR, 4], BF16, name=f"x_turned{q}", align_bytes=64) for q in range(TILES // 2)]
+        x_codes = [keep.tile([P, PASSES, HALF], U32, name=f"x_codes{h}", align_bytes=64) for h in range(2)]
+        x_scales = [keep.tile([P, PASSES, HALF], U8, name=f"x_scales{h}", align_bytes=64) for h in range(2)]
 
         def widen(i):
+            row = x_single[i][:] if i < 2 else x_pair[i // 2][:, i % 2]
+            by_word = x_wide[i][:].rearrange("p (g u q r e) -> p g q r u e", g=PASSES, u=2, q=4, e=2)
             for j in range(K // B):
-                src = (xb[i][:] if i < 2 and SPLIT0 else xb2[i // 2][:, i % 2])[:, j * B : (j + 1) * B].bitcast(FP8)
-                if i in S_TILES:
-                    nc.scalar.activation(xw[i][:, j * B : (j + 1) * B], src, COPY, scale=xs[:, i, j : j + 1])
-                elif i >= FIRST_SORTED:
-                    dst = xw[i][:].rearrange("p (g u q r e) -> p g q r u e", g=G, u=2, q=4, e=2)[:, j // 4, j % 4]
-                    nc.vector.tensor_scalar(dst, src.rearrange("p (r u e) -> p r u e", u=2, e=2), xs[:, i, j : j + 1], None, op0=MULT)
-                elif j < SCALAR_BLOCKS:
-                    nc.scalar.activation(xw[i][:, j * B : (j + 1) * B], src, COPY, scale=xs[:, i, j : j + 1])
-                else:
-                    nc.vector.tensor_scalar(xw[i][:, j * B : (j + 1) * B], src, xs[:, i, j : j + 1], None, op0=MULT)
+                codes = row[:, j * B : (j + 1) * B].bitcast(FP8).rearrange("p (r u e) -> p r u e", u=2, e=2)
+                nc.vector.tensor_scalar(by_word[:, j // 4, j % 4], codes, x_scale_sb[:, i, j : j + 1], None, op0=MULT)
 
-        def turn(words, in_order):
-            tp = bank([P, G, 2, P])
-            for g in range(G):
+        def turn(word_columns, dst):
+            turned = bank([P, PASSES, 2, P])
+            for g in range(PASSES):
                 for u in range(2):
-                    cols = slice(256 * g + P * u, 256 * g + P * (u + 1)) if in_order else slice(256 * g + u, 256 * (g + 1), 2)
-                    nc.tensor.transpose(tp[:, g, u, :], words[:, cols], ident[:])
-            return tp[:].rearrange("p g u r -> p g r u")
+                    nc.tensor.transpose(turned[:, g, u, :], word_columns(g, u), ident[:])
+            nc.scalar.copy(dst, turned[:].rearrange("p g u r -> p g r u"))
 
-        def x_turn(q, tiles=(0, 1)):
-            for ii in tiles:
-                turned = turn(xw[2 * q + ii][:].bitcast(F32), 2 * q + ii >= FIRST_SORTED and 2 * q + ii not in S_TILES)
-                dst = xT[q][:, :, ii * P : (ii + 1) * P, :].rearrange("p g r t -> p g (r t)").bitcast(F32)
-                nc.scalar.copy(dst.rearrange("p g (r u) -> p g r u", u=2), turned)
+        def x_turn(i):
+            words = x_wide[i][:].bitcast(F32)
+            dst = x_turned[i // 2][:, :, (i % 2) * P : (i % 2 + 1) * P, :].rearrange("p g r t -> p g (r t)").bitcast(F32)
+            turn(lambda g, u: words[:, 256 * g + P * u : 256 * g + P * (u + 1)], dst.rearrange("p g (r u) -> p g r u", u=2))
 
-        def x_quant(q):
-            cols = slice((q % 2) * 2 * P, (q % 2 + 1) * 2 * P)
-            for g in range(G):
+        def x_quantise(q):
+            cols = slice((q % 2) * PAIR, (q % 2 + 1) * PAIR)
+            for g in range(PASSES):
                 nc.vector.quantize_mx(
-                    out=xc[q // 2][:, g, cols].bitcast(FP8X4), scales=xsc[q // 2][:, g, cols], in_=xT[q][:, g].rearrange("p n t -> p (n t)")
+                    out=x_codes[q // 2][:, g, cols].bitcast(FP8X4),
+                    scales=x_scales[q // 2][:, g, cols],
+                    in_=x_turned[q][:, g].rearrange("p n t -> p (n t)"),
                 )
 
-        hT = {}
-        hc = [keep.tile([P, 2, G, P], U32, name=f"hc{e}", align_bytes=64) for e in range(2 * C)]
-        hs = [keep.tile([P, 2, G, P], U8, name=f"hs{e}", align_bytes=64) for e in range(2 * C)]
+        head_turned = {}
+        head_codes = [keep.tile([P, 2, PASSES, P], U32, name=f"head_codes{e}", align_bytes=64) for e in range(PARTS)]
+        head_scales = [keep.tile([P, 2, PASSES, P], U8, name=f"head_scales{e}", align_bytes=64) for e in range(PARTS)]
 
-        def head_turn(e):
-            hT[e] = work.tile([P, 2, G, P, 4], BF16, name="hT", align_bytes=64, bufs=3)
-            for s in range(2):
-                turned = turn(hraw[e][:, s, :].bitcast(F32), False)
-                dst = hT[e][:, s].rearrange("p g r t -> p (g r t)").bitcast(F32)
-                nc.scalar.copy(dst.rearrange("p (g r u) -> p g r u", g=G, u=2), turned)
+        def head_turn(e, s):
+            if s == 0:
+                head_turned[e] = work.tile([P, 2, PASSES, P, 4], BF16, name="head_turned", align_bytes=64, bufs=3)
+            words = (head_single[s][:] if e == 0 else head_part[e][:, s, :]).bitcast(F32)
+            dst = head_turned[e][:, s].rearrange("p g r t -> p (g r t)").bitcast(F32)
+            turn(lambda g, u: words[:, 256 * g + u : 256 * (g + 1) : 2], dst.rearrange("p (g r u) -> p g r u", g=PASSES, u=2))
 
-        def head_quant(e):
+        def head_quantise(e):
             nc.vector.quantize_mx(
-                out=hc[e][:].rearrange("p s g m -> p (s g m)").bitcast(FP8X4),
-                scales=hs[e][:].rearrange("p s g m -> p (s g m)"),
-                in_=hT[e][:].rearrange("p s g m t -> p (s g m t)"),
+                out=head_codes[e][:].rearrange("p s g m -> p (s g m)").bitcast(FP8X4),
+                scales=head_scales[e][:].rearrange("p s g m -> p (s g m)"),
+                in_=head_turned[e][:].rearrange("p s g m t -> p (s g m t)"),
             )
 
-        zp = {}
-        zi = {}
-        zc = {}
-        zs = {}
+        z_slots = {}
+        z_words = {}
+        z_codes = {}
+        z_scales = {}
 
-        def stage1(cc, h, s):
+        def first_product(e, s, h):
             acc = bank([P, HALF])
-            e = 2 * cc + s // 2
-            for g in range(G):
+            for g in range(PASSES):
                 nc.tensor.matmul_mx(
                     out=acc[:],
-                    lhsT=hc[e][:, s % 2, g, :].bitcast(FP8X4),
-                    lhsT_scale=hs[e][:, s % 2, g, :],
-                    rhs=xc[h][:, g, :].bitcast(FP8X4),
-                    rhs_scale=xsc[h][:, g, :],
+                    lhsT=head_codes[e][:, s, g, :].bitcast(FP8X4),
+                    lhsT_scale=head_scales[e][:, s, g, :],
+                    rhs=x_codes[h][:, g, :].bitcast(FP8X4),
+                    rhs_scale=x_scales[h][:, g, :],
                     start=(g == 0),
-                    stop=(g == G - 1),
+                    stop=(g == PASSES - 1),
                 )
             return acc
 
-        def z_out(cc, h, s, acc):
-            if (cc, h) not in zp:
-                zp[cc, h] = work.tile([P, S, HALF], BF16, name="zp", bufs=ZPB)
+        def z_out(e, s, h, acc):
+            cc, slot = e // 2, 2 * (e % 2) + s
+            if slot == 0:
+                z_slots[cc, h] = work.tile([P, SLOTS, HALF], BF16, name="z_slots", bufs=4)
+            bias = b_first[:] if cc == 0 else b_rest[:, cc - 1]
             nc.vector.scalar_tensor_tensor(
-                zp[cc, h][:, s, :], acc[:], (b_first[:] if cc == 0 else b_rest[:, cc - 1])[:, s : s + 1], rtau[h][:].rearrange("p i n -> p (i n)"), op0=ADD, op1=MULT
+                z_slots[cc, h][:, slot, :], acc[:], bias[:, slot : slot + 1], inv_tau[h][:].rearrange("p i n -> p (i n)"), op0=ADD, op1=MULT
             )
 
-        def z_inter(cc, q):
-            h, a = divmod(q, 2)
-            if a == 0:
-                zi[cc, h] = work.tile([P, HALF, S], BF16, name="zi", align_bytes=64, bufs=ZIB)
-            cols = slice(a * 2 * P, (a + 1) * 2 * P)
-            nc.scalar.copy(zi[cc, h][:, cols, :].rearrange("p (n i) s -> p n s i", i=4), zp[cc, h][:, :, cols].rearrange("p s (n i) -> p n s i", i=4))
+        def z_interleave(cc, q):
+            h = q // 2
+            if q % 2 == 0:
+                z_words[cc, h] = work.tile([P, HALF, SLOTS], BF16, name="z_words", align_bytes=64, bufs=5)
+            cols = slice((q % 2) * PAIR, (q % 2 + 1) * PAIR)
+            nc.scalar.copy(
+                z_words[cc, h][:, cols, :].rearrange("p (n i) s -> p n s i", i=4),
+                z_slots[cc, h][:, :, cols].rearrange("p s (n i) -> p n s i", i=4),
+            )
 
-        def z_quant(cc, q):
-            h, a = divmod(q, 2)
-            if a == 0:
-                zc[cc, h] = keep.tile([P, HALF], U32, name=f"zc{cc}_{h}", align_bytes=64)
-                zs[cc, h] = keep.tile([P, HALF], U8, name=f"zs{cc}_{h}", align_bytes=64)
-            if 4 * h + cc in ZQ_SPLIT:
-                cols = slice(a * 2 * P, (a + 1) * 2 * P)
-            elif a == 1:
-                cols = slice(0, HALF)
-            else:
-                return
-            nc.vector.quantize_mx(out=zc[cc, h][:, cols].bitcast(FP8X4), scales=zs[cc, h][:, cols], in_=zi[cc, h][:, cols, :].rearrange("p n s -> p (n s)"))
+        def z_quantise(cc, q):
+            h = q // 2
+            if q % 2 == 0:
+                z_codes[cc, h] = keep.tile([P, HALF], U32, name=f"z_codes{cc}_{h}", align_bytes=64)
+                z_scales[cc, h] = keep.tile([P, HALF], U8, name=f"z_scales{cc}_{h}", align_bytes=64)
+            cols = slice((q % 2) * PAIR, (q % 2 + 1) * PAIR)
+            nc.vector.quantize_mx(
+                out=z_codes[cc, h][:, cols].bitcast(FP8X4),
+                scales=z_scales[cc, h][:, cols],
+                in_=z_words[cc, h][:, cols, :].rearrange("p n s -> p (n s)"),
+            )
 
-        parked = []
-
-        def finish(src, i, n0, width, eng=nc.vector):
-            y = work.tile([P, width], F32, name="y", bufs=YB)
-            eng.tensor_tensor(y[:], src, c_bc[:, n0 : n0 + width], op=ADD)
-            (nc.scalar if width == P and END_S else nc.sync).dma_start(out=out_v[:, i, n0 : n0 + width], in_=y[:])
-
-        def stage2_group(i, n0, width):
+        def second_product(i, n0, width):
             cols = slice((i % 4) * P, (i % 4 + 1) * P)
             acc = bank([P, width])
-            for cc in range(C):
+            for cc in range(CHUNKS):
                 nc.tensor.matmul_mx(
                     out=acc[:],
-                    lhsT=zc[cc, i // 4][:, cols].bitcast(FP8X4),
-                    lhsT_scale=zs[cc, i // 4][:, cols],
-                    rhs=mw[:, cc, 2 * n0 : 2 * (n0 + width)].bitcast(FP4X4),
-                    rhs_scale=msc[:, cc, n0 : n0 + width],
+                    lhsT=z_codes[cc, i // 4][:, cols].bitcast(FP8X4),
+                    lhsT_scale=z_scales[cc, i // 4][:, cols],
+                    rhs=map_sb[:, cc, 2 * n0 : 2 * (n0 + width)].bitcast(FP4X4),
+                    rhs_scale=map_scale_sb[:, cc, n0 : n0 + width],
                     start=(cc == 0),
-                    stop=(cc == C - 1),
+                    stop=(cc == CHUNKS - 1),
                 )
-            return acc
+            y = work.tile([P, width], F32, name="y", bufs=8)
+            nc.vector.tensor_tensor(y[:], acc[:], c_rows[:, n0 : n0 + width], op=ADD)
+            nc.sync.dma_start(out=out_v[:, i, n0 : n0 + width], in_=y[:])
 
-        def warm(n, width):
-            if n:
-                scratch = bank([P, 512])
-            for r in range(n):
-                nc.tensor.matmul(scratch[:, :width], lhsT=zeros[:, :P], rhs=zeros[:, :width], start=True, stop=True)
-
-        warm(WARM0, 512)
-        for i in range(2):
-            widen(i)
-        make_rtau(0)
-        make_rtau(1)
-        warm(WA[0], 512)
-        for i in range(2, 4):
-            widen(i)
+        warm_up(3)
+        nc.vector.reciprocal(inv_tau_col[:], tau_sb[:])
+        widen(0)
+        widen(1)
+        spread_inv_tau(0)
+        spread_inv_tau(1)
+        warm_up(1)
         x_turn(0)
-        warm(WA[1], WW)
-        head_turn(0)
-        warm(WA[2], WW)
-        if MAP_AT == -2:
-            load_map()
-        x_quant(0)
+        head_turn(0, 0)
         x_turn(1)
-        if MAP_AT == -3:
-            load_map()
-        head_quant(0)
-        if not H2_FIRST:
-            widen(4)
-        warm(WA[3], WW)
-        head_turn(1)
-        warm(WA[4], WW)
-        x_quant(1)
-        widen(4 if H2_FIRST else 5)
-        head_quant(1)
+        warm_up(1)
+        widen(2)
+        widen(3)
+        head_turn(0, 1)
+        x_turn(2)
+        warm_up(1)
+        x_quantise(0)
+        x_turn(3)
+        head_quantise(0)
+        head_turn(1, 0)
+        head_turn(1, 1)
+        warm_up(1)
+        x_quantise(1)
+        widen(4)
+        head_quantise(1)
 
-        steps = [("z", cc, 0, a) for cc in range(C) for a in range(2)]
-        second = [("y", i, nh) for i in range(TT) for nh in range(2)]
-        for n in range(2 * C):
-            if n in Y_BEFORE:
+        second = [("y", i, n0) for i in range(TILES) for n0 in range(0, N, BANK)]
+        steps = [("z", e, 0) for e in range(PARTS)]
+        for e in range(PARTS):
+            if e in WOVEN:
                 steps.append(second.pop(0))
-            steps.append(("z", n // 2, 1, n % 2))
+            steps.append(("z", e, 1))
+        last_z = len(steps) - 1
         steps = steps + second
 
-        accs = {}
-
-        def multiply(k):
-            step = steps[k]
-            if k < 6 and not RUN16:
-                head_turn(k + 2)
-            if k < 6 and RUN16 and k % 2 == 0:
-                head_turn(k + 2)
-                head_turn(k + 3)
-            for j in range(4):
-                if k == XT_AT[j]:
-                    x_turn(2 + j // 2, (j % 2,))
-            if step[0] == "z":
-                cc, h, a = step[1:]
-                accs[k] = [stage1(cc, h, 2 * a), stage1(cc, h, 2 * a + 1)]
-            else:
-                i, nh = step[1:]
-                width = P if k == len(steps) - 1 else 512
-                accs[k] = [(stage2_group(i, n0, width)[:], i, n0, width) for n0 in range(512 * nh, 512 * (nh + 1), width)]
-                if 2 * i + nh in VIA_S:
-                    raw = keep.tile([P, 512], F32, name=f"raw{i}_{nh}")
-                    nc.scalar.copy(raw[:], accs[k][0][0])
-                    accs[k] = [(raw[:], i, 512 * nh, 512)]
-
-        held = []
-        late = []
-        to_inter = []
-        to_quant = []
-        done = 0
+        to_interleave = []
+        interleaved = []
+        to_quantise = []
+        put_off = []
         for k, step in enumerate(steps):
-            while done <= min(k + (LEAD if k >= 8 else 0), len(steps) - 1):
-                multiply(done)
-                done = done + 1
-            ready = list(to_quant)
-            to_quant.clear()
-            if to_inter and k not in ZI_SKIP:
-                to_quant.append(to_inter.pop(0))
-                z_inter(*to_quant[-1])
-            if to_inter and k in ZI_TWO:
-                to_quant.append(to_inter.pop(0))
-                z_inter(*to_quant[-1])
+            if k + AHEAD < PARTS:
+                head_turn(k + AHEAD, 0)
+                head_turn(k + AHEAD, 1)
+            if 1 <= k <= 4:
+                x_turn(3 + k)
             if step[0] == "z":
-                cc, h, a = step[1:]
-                if k == XQ_FIRST:
-                    x_quant(3)
-                rev = 1 if k >= REV_FROM else 0
-                if k < 6 and k in HQ_FIRST:
-                    head_quant(k + 2)
-                z_out(cc, h, 2 * a + rev, accs[k][rev])
-                if k < 6 and k not in HQ_FIRST:
-                    head_quant(k + 2)
-                if k in XQ_AT and XQ_MID:
-                    x_quant(2 + XQ_AT.index(k))
-                z_out(cc, h, 2 * a + 1 - rev, accs[k][1 - rev])
-                for j in range(len(W_AT)):
-                    if W_AT[j] == k:
-                        widen(TT - len(W_AT) + j)
-                if k in XQ_AT and not XQ_MID:
-                    x_quant(2 + XQ_AT.index(k))
-                if a == 1:
-                    to_inter.extend([(cc, 2 * h), (cc, 2 * h + 1)])
-            elif 2 * step[1] + step[2] < PARKED:
-                parked.extend(accs[k])
-            elif 2 * step[1] + step[2] in Y_HOLD:
-                held.extend(accs[k])
+                e, h = step[1:]
+                accs = [first_product(e, s, h) for s in range(2)]
+
+            ready = list(interleaved)
+            interleaved.clear()
+            count = 0 if k == INTERLEAVE_SKIP else 2 if k == PARTS - AHEAD else 1
+            for pair in to_interleave[:count]:
+                z_interleave(*pair)
+                interleaved.append(pair)
+                to_interleave.remove(pair)
+
+            if step[0] == "z":
+                z_out(e, 0, h, accs[0])
+                if k + AHEAD < PARTS:
+                    head_quantise(k + AHEAD)
+                z_out(e, 1, h, accs[1])
+                if k < 3:
+                    widen(5 + k)
+                if k in (2, 4):
+                    x_quantise(1 + k // 2)
+                if e % 2 == 1:
+                    to_interleave.extend([(e // 2, 2 * h), (e // 2, 2 * h + 1)])
             else:
-                for item in accs[k] + held:
-                    finish(*item)
-                held.clear()
-                if step[1] >= UNPARK and parked:
-                    finish(*parked.pop(0))
-            if k == MAP_AT:
-                load_map()
-            if k in ZQ_NOW:
-                ready.extend(to_quant)
-                to_quant.clear()
-            late.extend(ready)
-            for n in range(2):
-                if late and k >= ZQ_FROM:
-                    z_quant(*late.pop(0))
+                i, n0 = step[1:]
+                width = P if k == len(steps) - 1 else BANK
+                for n in range(n0, n0 + BANK, width):
+                    second_product(i, n, width)
+
+            for cc, q in ready:
+                (put_off if q >= 2 and cc < PUT_OFF and k < last_z else to_quantise).append((cc, q))
+            if k == last_z:
+                to_quantise.extend(put_off)
+            for pair in to_quantise[:QUANT_MAX]:
+                z_quantise(*pair)
+                to_quantise.remove(pair)

@@ -28,10 +28,8 @@ HALF = T // 2
 PAIR = 2 * P
 
 AHEAD = 2
-WOVEN = (5, 7)
-INTERLEAVE_SKIP = 3
-PUT_OFF = 2
-QUANT_MAX = 3
+SORTED_PARTS = (5, 6)
+X_STEPS = 4
 
 
 def tile_teacher_logits_remap_d4_kernel(tc, x_bytes, x_scale, head, b, tau, map_words, map_scales, c, out):
@@ -51,8 +49,8 @@ def tile_teacher_logits_remap_d4_kernel(tc, x_bytes, x_scale, head, b, tau, map_
             return psum.tile(shape, F32, name="bank", tag="bank", bufs=8)
 
         x_scale_sb = keep.tile([P, TILES, K // B], F32, name="x_scale_sb")
-        x_single = [keep.tile([P, K], U8, name=f"x_single{i}") for i in range(2)]
-        x_pair = {q: keep.tile([P, 2, K], U8, name=f"x_pair{q}") for q in range(1, TILES // 2)}
+        x_single = {i: keep.tile([P, K], U8, name=f"x_single{i}") for i in (0, 1, 4, 5)}
+        x_pair = {q: keep.tile([P, 2, K], U8, name=f"x_pair{q}") for q in (1, 3)}
         head_single = [keep.tile([P, K], BF16, name=f"head_single{s}") for s in range(2)]
         head_part = {e: keep.tile([P, 2, K], BF16, name=f"head_part{e}") for e in range(1, PARTS)}
         b_first = keep.tile([P, SLOTS], BF16, name="b_first")
@@ -64,7 +62,10 @@ def tile_teacher_logits_remap_d4_kernel(tc, x_bytes, x_scale, head, b, tau, map_
         ident = keep.tile([P, P], F32, name="ident")
         zeros = keep.tile([P, BANK], BF16, name="zeros")
 
-        def load_x(q):
+        def load_x_tile(i):
+            nc.sync.dma_start(out=x_single[i][:], in_=x_v[:, i, :])
+
+        def load_x_pair(q):
             nc.sync.dma_start(out=x_pair[q][:], in_=x_v[:, 2 * q : 2 * q + 2, :])
 
         def load_head(e):
@@ -76,17 +77,18 @@ def tile_teacher_logits_remap_d4_kernel(tc, x_bytes, x_scale, head, b, tau, map_
 
         nc.sync.dma_start(out=tau_sb[:], in_=tau.rearrange("(p i) -> p i", i=TILES))
         nc.sync.dma_start(out=x_scale_sb[:], in_=x_scale.rearrange("(p i) j -> p i j", i=TILES))
-        for i in range(2):
-            nc.sync.dma_start(out=x_single[i][:], in_=x_v[:, i, :])
+        load_x_tile(0)
+        load_x_tile(1)
         nc.sync.dma_start(out=head_single[0][:], in_=head_v[0, :, 0, :])
-        load_x(1)
+        load_x_pair(1)
         nc.sync.dma_start(out=head_single[1][:], in_=head_v[0, :, 1, :])
+        load_x_tile(4)
         load_head(1)
         nc.sync.dma_start(out=b_first[:], in_=b_v[:, 0, :])
         load_head(2)
-        load_x(2)
+        load_x_tile(5)
         load_head(3)
-        load_x(3)
+        load_x_pair(3)
         load_head(4)
         nc.sync.dma_start(out=b_rest[:], in_=b_v[:, 1:, :])
         for e in range(5, PARTS):
@@ -114,29 +116,33 @@ def tile_teacher_logits_remap_d4_kernel(tc, x_bytes, x_scale, head, b, tau, map_
                 nc.tensor.transpose(rows[:, ii, :], column.to_broadcast([P, P]), ident[:])
             nc.scalar.copy(inv_tau[h][:], rows[:])
 
-        x_wide = [keep.tile([P, K], BF16, name=f"x_wide{i}") for i in range(TILES)]
-        x_turned = [keep.tile([P, PASSES, PAIR, 4], BF16, name=f"x_turned{q}", align_bytes=64) for q in range(TILES // 2)]
+        x_wide = {}
+        x_turned = {}
         x_codes = [keep.tile([P, PASSES, HALF], U32, name=f"x_codes{h}", align_bytes=64) for h in range(2)]
         x_scales = [keep.tile([P, PASSES, HALF], U8, name=f"x_scales{h}", align_bytes=64) for h in range(2)]
 
         def widen(i):
-            row = x_single[i][:] if i < 2 else x_pair[i // 2][:, i % 2]
+            x_wide[i] = work.tile([P, K], BF16, name="x_wide", bufs=5)
+            row = x_single[i][:] if i in x_single else x_pair[i // 2][:, i % 2]
             by_word = x_wide[i][:].rearrange("p (g u q r e) -> p g q r u e", g=PASSES, u=2, q=4, e=2)
             for j in range(K // B):
                 codes = row[:, j * B : (j + 1) * B].bitcast(FP8).rearrange("p (r u e) -> p r u e", u=2, e=2)
                 nc.vector.tensor_scalar(by_word[:, j // 4, j % 4], codes, x_scale_sb[:, i, j : j + 1], None, op0=MULT)
 
-        def turn(word_columns, dst):
+        def turn(words, is_sorted, dst):
             turned = bank([P, PASSES, 2, P])
             for g in range(PASSES):
                 for u in range(2):
-                    nc.tensor.transpose(turned[:, g, u, :], word_columns(g, u), ident[:])
+                    cols = slice(256 * g + P * u, 256 * g + P * (u + 1)) if is_sorted else slice(256 * g + u, 256 * (g + 1), 2)
+                    nc.tensor.transpose(turned[:, g, u, :], words[:, cols], ident[:])
             nc.scalar.copy(dst, turned[:].rearrange("p g u r -> p g r u"))
 
         def x_turn(i):
+            if i % 2 == 0:
+                x_turned[i // 2] = work.tile([P, PASSES, PAIR, 4], BF16, name="x_turned", align_bytes=64, bufs=2)
             words = x_wide[i][:].bitcast(F32)
             dst = x_turned[i // 2][:, :, (i % 2) * P : (i % 2 + 1) * P, :].rearrange("p g r t -> p g (r t)").bitcast(F32)
-            turn(lambda g, u: words[:, 256 * g + P * u : 256 * g + P * (u + 1)], dst.rearrange("p g (r u) -> p g r u", u=2))
+            turn(words, True, dst.rearrange("p g (r u) -> p g r u", u=2))
 
         def x_quantise(q):
             cols = slice((q % 2) * PAIR, (q % 2 + 1) * PAIR)
@@ -147,16 +153,23 @@ def tile_teacher_logits_remap_d4_kernel(tc, x_bytes, x_scale, head, b, tau, map_
                     in_=x_turned[q][:, g].rearrange("p n t -> p (n t)"),
                 )
 
+        head_sorted = {e: keep.tile([P, 2, K], BF16, name=f"head_sorted{e}") for e in SORTED_PARTS}
         head_turned = {}
         head_codes = [keep.tile([P, 2, PASSES, P], U32, name=f"head_codes{e}", align_bytes=64) for e in range(PARTS)]
         head_scales = [keep.tile([P, 2, PASSES, P], U8, name=f"head_scales{e}", align_bytes=64) for e in range(PARTS)]
 
+        def head_sort(e):
+            nc.scalar.copy(
+                head_sorted[e][:].bitcast(F32).rearrange("p s (g u r) -> p (s g) u r", g=PASSES, u=2),
+                head_part[e][:].bitcast(F32).rearrange("p s (g r u) -> p (s g) u r", g=PASSES, u=2),
+            )
+
         def head_turn(e, s):
             if s == 0:
                 head_turned[e] = work.tile([P, 2, PASSES, P, 4], BF16, name="head_turned", align_bytes=64, bufs=3)
-            words = (head_single[s][:] if e == 0 else head_part[e][:, s, :]).bitcast(F32)
+            row = head_single[s][:] if e == 0 else head_sorted.get(e, head_part[e])[:, s, :]
             dst = head_turned[e][:, s].rearrange("p g r t -> p (g r t)").bitcast(F32)
-            turn(lambda g, u: words[:, 256 * g + u : 256 * (g + 1) : 2], dst.rearrange("p (g r u) -> p g r u", g=PASSES, u=2))
+            turn(row.bitcast(F32), e in head_sorted, dst.rearrange("p (g r u) -> p g r u", g=PASSES, u=2))
 
         def head_quantise(e):
             nc.vector.quantize_mx(
@@ -165,10 +178,11 @@ def tile_teacher_logits_remap_d4_kernel(tc, x_bytes, x_scale, head, b, tau, map_
                 in_=head_turned[e][:].rearrange("p s g m t -> p (s g m t)"),
             )
 
-        z_slots = {}
-        z_words = {}
-        z_codes = {}
-        z_scales = {}
+        units = [(cc, h) for h in range(2) for cc in range(CHUNKS)]
+        z_slots = {u: keep.tile([P, SLOTS, HALF], BF16, name=f"z_slots{u[0]}_{u[1]}") for u in units}
+        z_words = {u: keep.tile([P, HALF, SLOTS], BF16, name=f"z_words{u[0]}_{u[1]}", align_bytes=64) for u in units}
+        z_codes = {u: keep.tile([P, HALF], U32, name=f"z_codes{u[0]}_{u[1]}", align_bytes=64) for u in units}
+        z_scales = {u: keep.tile([P, HALF], U8, name=f"z_scales{u[0]}_{u[1]}", align_bytes=64) for u in units}
 
         def first_product(e, s, h):
             acc = bank([P, HALF])
@@ -186,8 +200,6 @@ def tile_teacher_logits_remap_d4_kernel(tc, x_bytes, x_scale, head, b, tau, map_
 
         def z_out(e, s, h, acc):
             cc, slot = e // 2, 2 * (e % 2) + s
-            if slot == 0:
-                z_slots[cc, h] = work.tile([P, SLOTS, HALF], BF16, name="z_slots", bufs=4)
             bias = b_first[:] if cc == 0 else b_rest[:, cc - 1]
             nc.vector.scalar_tensor_tensor(
                 z_slots[cc, h][:, slot, :], acc[:], bias[:, slot : slot + 1], inv_tau[h][:].rearrange("p i n -> p (i n)"), op0=ADD, op1=MULT
@@ -195,8 +207,6 @@ def tile_teacher_logits_remap_d4_kernel(tc, x_bytes, x_scale, head, b, tau, map_
 
         def z_interleave(cc, q):
             h = q // 2
-            if q % 2 == 0:
-                z_words[cc, h] = work.tile([P, HALF, SLOTS], BF16, name="z_words", align_bytes=64, bufs=5)
             cols = slice((q % 2) * PAIR, (q % 2 + 1) * PAIR)
             nc.scalar.copy(
                 z_words[cc, h][:, cols, :].rearrange("p (n i) s -> p n s i", i=4),
@@ -205,9 +215,6 @@ def tile_teacher_logits_remap_d4_kernel(tc, x_bytes, x_scale, head, b, tau, map_
 
         def z_quantise(cc, q):
             h = q // 2
-            if q % 2 == 0:
-                z_codes[cc, h] = keep.tile([P, HALF], U32, name=f"z_codes{cc}_{h}", align_bytes=64)
-                z_scales[cc, h] = keep.tile([P, HALF], U8, name=f"z_scales{cc}_{h}", align_bytes=64)
             cols = slice((q % 2) * PAIR, (q % 2 + 1) * PAIR)
             nc.vector.quantize_mx(
                 out=z_codes[cc, h][:, cols].bitcast(FP8X4),
@@ -228,7 +235,7 @@ def tile_teacher_logits_remap_d4_kernel(tc, x_bytes, x_scale, head, b, tau, map_
                     start=(cc == 0),
                     stop=(cc == CHUNKS - 1),
                 )
-            y = work.tile([P, width], F32, name="y", bufs=8)
+            y = work.tile([P, width], F32, name="y", bufs=6)
             nc.vector.tensor_tensor(y[:], acc[:], c_rows[:, n0 : n0 + width], op=ADD)
             nc.sync.dma_start(out=out_v[:, i, n0 : n0 + width], in_=y[:])
 
@@ -248,6 +255,7 @@ def tile_teacher_logits_remap_d4_kernel(tc, x_bytes, x_scale, head, b, tau, map_
         head_turn(0, 1)
         x_turn(2)
         warm_up(1)
+        widen(4)
         x_quantise(0)
         x_turn(3)
         head_quantise(0)
@@ -255,61 +263,64 @@ def tile_teacher_logits_remap_d4_kernel(tc, x_bytes, x_scale, head, b, tau, map_
         head_turn(1, 1)
         warm_up(1)
         x_quantise(1)
-        widen(4)
+        widen(5)
         head_quantise(1)
-
-        second = [("y", i, n0) for i in range(TILES) for n0 in range(0, N, BANK)]
-        steps = [("z", e, 0) for e in range(PARTS)]
-        for e in range(PARTS):
-            if e in WOVEN:
-                steps.append(second.pop(0))
-            steps.append(("z", e, 1))
-        last_z = len(steps) - 1
-        steps = steps + second
 
         to_interleave = []
         interleaved = []
-        to_quantise = []
         put_off = []
-        for k, step in enumerate(steps):
-            if k + AHEAD < PARTS:
+
+        def interleave_next():
+            item = min(to_interleave, key=lambda cq: cq[1])
+            to_interleave.remove(item)
+            z_interleave(*item)
+            interleaved.append(item)
+
+        for k in range(2 * PARTS):
+            h, e = divmod(k, PARTS)
+            turns_head = k + AHEAD < PARTS
+            if turns_head:
                 head_turn(k + AHEAD, 0)
                 head_turn(k + AHEAD, 1)
-            if 1 <= k <= 4:
-                x_turn(3 + k)
-            if step[0] == "z":
-                e, h = step[1:]
-                accs = [first_product(e, s, h) for s in range(2)]
+            if k < X_STEPS:
+                x_turn(4 + k)
+            accs = [first_product(e, s, h) for s in range(2)]
+            if k + 2 * AHEAD in SORTED_PARTS:
+                head_sort(k + 2 * AHEAD)
 
             ready = list(interleaved)
             interleaved.clear()
-            count = 0 if k == INTERLEAVE_SKIP else 2 if k == PARTS - AHEAD else 1
-            for pair in to_interleave[:count]:
-                z_interleave(*pair)
-                interleaved.append(pair)
-                to_interleave.remove(pair)
+            if k >= X_STEPS and to_interleave:
+                interleave_next()
 
-            if step[0] == "z":
-                z_out(e, 0, h, accs[0])
-                if k + AHEAD < PARTS:
-                    head_quantise(k + AHEAD)
-                z_out(e, 1, h, accs[1])
-                if k < 3:
-                    widen(5 + k)
-                if k in (2, 4):
-                    x_quantise(1 + k // 2)
-                if e % 2 == 1:
-                    to_interleave.extend([(e // 2, 2 * h), (e // 2, 2 * h + 1)])
-            else:
-                i, n0 = step[1:]
-                width = P if k == len(steps) - 1 else BANK
+            first, second = (0, 1) if turns_head else (1, 0)
+            z_out(e, first, h, accs[first])
+            if turns_head:
+                head_quantise(k + AHEAD)
+            z_out(e, second, h, accs[second])
+            if k < 2:
+                widen(6 + k)
+            if k in (2, 4):
+                x_quantise(1 + k // 2)
+            if e % 2 == 1:
+                to_interleave.extend([(e // 2, 2 * h), (e // 2, 2 * h + 1)])
+
+            put_off.extend([item for item in ready if item[1] > 0])
+            for item in ready:
+                if item[1] == 0:
+                    z_quantise(*item)
+
+        for item in sorted(put_off, key=lambda cq: cq[1]):
+            z_quantise(*item)
+
+        for i in range(TILES):
+            for n0 in range(0, N, BANK):
+                ready = list(interleaved)
+                interleaved.clear()
+                if to_interleave:
+                    interleave_next()
+                width = P if (i, n0) == (TILES - 1, N - BANK) else BANK
                 for n in range(n0, n0 + BANK, width):
                     second_product(i, n, width)
-
-            for cc, q in ready:
-                (put_off if q >= 2 and cc < PUT_OFF and k < last_z else to_quantise).append((cc, q))
-            if k == last_z:
-                to_quantise.extend(put_off)
-            for pair in to_quantise[:QUANT_MAX]:
-                z_quantise(*pair)
-                to_quantise.remove(pair)
+                for item in ready:
+                    z_quantise(*item)

@@ -36,7 +36,6 @@ def tile_teacher_logits_remap_d4_kernel(tc, x_bytes, x_scale, head, b, tau, map_
     nc = tc.nc
     x_v = x_bytes.rearrange("(p i) k -> p i k", i=TILES)
     head_v = head.rearrange("(c p s) k -> c p s k", p=P, s=SLOTS)
-    b_v = b.rearrange("(c p s) -> p c s", p=P, s=SLOTS)
     out_v = out.rearrange("(p i) n -> p i n", i=TILES)
 
     with ExitStack() as ctx:
@@ -53,8 +52,8 @@ def tile_teacher_logits_remap_d4_kernel(tc, x_bytes, x_scale, head, b, tau, map_
         x_pair = {q: keep.tile([P, 2, K], U8, name=f"x_pair{q}") for q in (1, 3)}
         head_single = [keep.tile([P, K], BF16, name=f"head_single{s}") for s in range(2)]
         head_part = {e: keep.tile([P, 2, K], BF16, name=f"head_part{e}") for e in range(1, PARTS)}
-        b_first = keep.tile([P, SLOTS], BF16, name="b_first")
-        b_rest = keep.tile([P, CHUNKS - 1, SLOTS], BF16, name="b_rest")
+        b_rows = keep.tile([P, 512], BF16, name="b_rows")
+        b_sb = keep.tile([P, CHUNKS, SLOTS], BF16, name="b_sb")
         tau_sb = keep.tile([P, TILES], BF16, name="tau_sb")
         map_scale_sb = keep.tile([P, CHUNKS, N], U8, name="map_scale_sb", align_bytes=64)
         map_sb = keep.tile([P, CHUNKS, 2 * N], U8, name="map_sb", align_bytes=64)
@@ -72,25 +71,25 @@ def tile_teacher_logits_remap_d4_kernel(tc, x_bytes, x_scale, head, b, tau, map_
             nc.sync.dma_start(out=head_part[e][:], in_=head_v[e // 2, :, 2 * (e % 2) : 2 * (e % 2) + 2, :])
 
         nc.gpsimd.memset(zeros[:].bitcast(I32), 0)
+        nc.gpsimd.memset(b_rows[:].bitcast(I32), 0)
         make_identity(nc, ident[:])
-        nc.gpsimd.memset(map_scale_sb[:].rearrange("p c n -> p (c n)").bitcast(I32), 0)
+        nc.vector.memset(map_scale_sb[:].rearrange("p c n -> p (c n)").bitcast(I32), 0)
 
         nc.sync.dma_start(out=tau_sb[:], in_=tau.rearrange("(p i) -> p i", i=TILES))
         nc.sync.dma_start(out=x_scale_sb[:], in_=x_scale.rearrange("(p i) j -> p i j", i=TILES))
         load_x_tile(0)
         load_x_tile(1)
+        nc.sync.dma_start(out=b_rows[:CHUNKS, :], in_=b.rearrange("(c v) -> c v", c=CHUNKS))
         nc.sync.dma_start(out=head_single[0][:], in_=head_v[0, :, 0, :])
         load_x_pair(1)
         nc.sync.dma_start(out=head_single[1][:], in_=head_v[0, :, 1, :])
         load_x_tile(4)
         load_head(1)
-        nc.sync.dma_start(out=b_first[:], in_=b_v[:, 0, :])
         load_head(2)
         load_x_tile(5)
         load_head(3)
         load_x_pair(3)
         load_head(4)
-        nc.sync.dma_start(out=b_rest[:], in_=b_v[:, 1:, :])
         for e in range(5, PARTS):
             load_head(e)
         for q in range(4):
@@ -115,6 +114,12 @@ def tile_teacher_logits_remap_d4_kernel(tc, x_bytes, x_scale, head, b, tau, map_
                 column = inv_tau_col[:, 4 * h + ii : 4 * h + ii + 1]
                 nc.tensor.transpose(rows[:, ii, :], column.to_broadcast([P, P]), ident[:])
             nc.scalar.copy(inv_tau[h][:], rows[:])
+
+        def turn_b():
+            turned = bank([P, 2, P])
+            for u in range(2):
+                nc.tensor.transpose(turned[:, u, :], b_rows[:].bitcast(F32)[:, u::2], ident[:])
+            nc.scalar.copy(b_sb[:].bitcast(F32), turned[:, :, :CHUNKS].rearrange("p u c -> p c u"))
 
         x_wide = {}
         x_turned = {}
@@ -200,7 +205,7 @@ def tile_teacher_logits_remap_d4_kernel(tc, x_bytes, x_scale, head, b, tau, map_
 
         def z_out(e, s, h, acc):
             cc, slot = e // 2, 2 * (e % 2) + s
-            bias = b_first[:] if cc == 0 else b_rest[:, cc - 1]
+            bias = b_sb[:, cc]
             nc.vector.scalar_tensor_tensor(
                 z_slots[cc, h][:, slot, :], acc[:], bias[:, slot : slot + 1], inv_tau[h][:].rearrange("p i n -> p (i n)"), op0=ADD, op1=MULT
             )
@@ -222,7 +227,7 @@ def tile_teacher_logits_remap_d4_kernel(tc, x_bytes, x_scale, head, b, tau, map_
                 in_=z_words[cc, h][:, cols, :].rearrange("p n s -> p (n s)"),
             )
 
-        def second_product(i, n0, width):
+        def second_product(i, n0, width, piece):
             cols = slice((i % 4) * P, (i % 4 + 1) * P)
             acc = bank([P, width])
             for cc in range(CHUNKS):
@@ -235,9 +240,10 @@ def tile_teacher_logits_remap_d4_kernel(tc, x_bytes, x_scale, head, b, tau, map_
                     start=(cc == 0),
                     stop=(cc == CHUNKS - 1),
                 )
-            y = work.tile([P, width], F32, name="y", bufs=6)
-            nc.vector.tensor_tensor(y[:], acc[:], c_rows[:, n0 : n0 + width], op=ADD)
-            nc.sync.dma_start(out=out_v[:, i, n0 : n0 + width], in_=y[:])
+            for lo in range(0, width, piece):
+                y = work.tile([P, piece], F32, name="y" if piece == BANK else "y_narrow", bufs=6)
+                nc.vector.tensor_tensor(y[:], acc[:, lo : lo + piece], c_rows[:, n0 + lo : n0 + lo + piece], op=ADD)
+                nc.sync.dma_start(out=out_v[:, i, n0 + lo : n0 + lo + piece], in_=y[:])
 
         warm_up(3)
         nc.vector.reciprocal(inv_tau_col[:], tau_sb[:])
@@ -245,6 +251,7 @@ def tile_teacher_logits_remap_d4_kernel(tc, x_bytes, x_scale, head, b, tau, map_
         widen(1)
         spread_inv_tau(0)
         spread_inv_tau(1)
+        turn_b()
         warm_up(1)
         x_turn(0)
         head_turn(0, 0)
@@ -321,6 +328,6 @@ def tile_teacher_logits_remap_d4_kernel(tc, x_bytes, x_scale, head, b, tau, map_
                     interleave_next()
                 width = P if (i, n0) == (TILES - 1, N - BANK) else BANK
                 for n in range(n0, n0 + BANK, width):
-                    second_product(i, n, width)
+                    second_product(i, n, width, min(width, BANK // 2) if i == TILES - 1 else width)
                 for item in ready:
                     z_quantise(*item)

@@ -29,6 +29,7 @@ PAIR = 2 * P
 
 AHEAD = 2
 SORTED_PARTS = (5, 6)
+ZQ_STEPS = [12, 14]
 X_STEPS = 4
 
 
@@ -51,7 +52,7 @@ def tile_teacher_logits_remap_d4_kernel(tc, x_bytes, x_scale, head, b, tau, map_
         x_single = {i: keep.tile([P, K], U8, name=f"x_single{i}") for i in (0, 1, 4, 5)}
         x_pair = {q: keep.tile([P, 2, K], U8, name=f"x_pair{q}") for q in (1, 3)}
         head_single = [keep.tile([P, K], BF16, name=f"head_single{s}") for s in range(2)]
-        head_part = {e: keep.tile([P, 2, K], BF16, name=f"head_part{e}") for e in range(1, PARTS)}
+        head_part = {e: work.tile([P, 2, K], BF16, name=f"head_part{e}", tag="rows", bufs=PARTS - 1) for e in range(1, PARTS)}
         b_rows = keep.tile([P, 512], BF16, name="b_rows")
         b_sb = keep.tile([P, CHUNKS, SLOTS], BF16, name="b_sb")
         tau_sb = keep.tile([P, TILES], BF16, name="tau_sb")
@@ -227,7 +228,10 @@ def tile_teacher_logits_remap_d4_kernel(tc, x_bytes, x_scale, head, b, tau, map_
                 in_=z_words[cc, h][:, cols, :].rearrange("p n s -> p (n s)"),
             )
 
-        def second_product(i, n0, width, piece):
+        y_accs = {}
+        y_rows = {}
+
+        def second_product(i, n0, width):
             cols = slice((i % 4) * P, (i % 4 + 1) * P)
             acc = bank([P, width])
             for cc in range(CHUNKS):
@@ -240,10 +244,17 @@ def tile_teacher_logits_remap_d4_kernel(tc, x_bytes, x_scale, head, b, tau, map_
                     start=(cc == 0),
                     stop=(cc == CHUNKS - 1),
                 )
-            for lo in range(0, width, piece):
-                y = work.tile([P, piece], F32, name="y" if piece == BANK else "y_narrow", bufs=6)
-                nc.vector.tensor_tensor(y[:], acc[:, lo : lo + piece], c_rows[:, n0 + lo : n0 + lo + piece], op=ADD)
-                nc.sync.dma_start(out=out_v[:, i, n0 + lo : n0 + lo + piece], in_=y[:])
+            y_accs[i, n0] = acc
+
+        def y_out(i, n0, lo, hi):
+            if i not in y_rows:
+                if i < TILES - 1:
+                    y_rows[i] = work.tile([P, N], F32, name="y", tag="rows", bufs=PARTS - 1)
+                else:
+                    y_rows[i] = keep.tile([P, N], F32, name="y_last")
+            cols = slice(n0 + lo, n0 + hi)
+            nc.vector.tensor_tensor(y_rows[i][:, cols], y_accs[i, n0][:, lo:hi], c_rows[:, cols], op=ADD)
+            nc.sync.dma_start(out=out_v[:, i, cols], in_=y_rows[i][:, cols])
 
         warm_up(3)
         nc.vector.reciprocal(inv_tau_col[:], tau_sb[:])
@@ -273,20 +284,17 @@ def tile_teacher_logits_remap_d4_kernel(tc, x_bytes, x_scale, head, b, tau, map_
         widen(5)
         head_quantise(1)
 
-        to_interleave = []
-        interleaved = []
-        put_off = []
+        last_turn = PARTS - 1 - AHEAD
+        to_interleave = [(cc, q) for q in range(4) for cc in range(CHUNKS)]
 
-        def interleave_next():
-            item = min(to_interleave, key=lambda cq: cq[1])
+        def interleave_next(k):
+            item = [(cc, q) for cc, q in to_interleave if PARTS * (q // 2) + 2 * cc + 1 <= k - 2][0]
             to_interleave.remove(item)
             z_interleave(*item)
-            interleaved.append(item)
 
         for k in range(2 * PARTS):
             h, e = divmod(k, PARTS)
-            turns_head = k + AHEAD < PARTS
-            if turns_head:
+            if k <= last_turn:
                 head_turn(k + AHEAD, 0)
                 head_turn(k + AHEAD, 1)
             if k < X_STEPS:
@@ -294,40 +302,38 @@ def tile_teacher_logits_remap_d4_kernel(tc, x_bytes, x_scale, head, b, tau, map_
             accs = [first_product(e, s, h) for s in range(2)]
             if k + 2 * AHEAD in SORTED_PARTS:
                 head_sort(k + 2 * AHEAD)
+            if k >= last_turn:
+                interleave_next(k)
 
-            ready = list(interleaved)
-            interleaved.clear()
-            if k >= X_STEPS and to_interleave:
-                interleave_next()
-
-            first, second = (0, 1) if turns_head else (1, 0)
-            z_out(e, first, h, accs[first])
-            if turns_head:
+            if k == last_turn:
                 head_quantise(k + AHEAD)
+            first, second = (1, 0) if last_turn < k < ZQ_STEPS[0] else (0, 1)
+            z_out(e, first, h, accs[first])
+            if k < last_turn and k != -1:
+                head_quantise(k + AHEAD)
+            if k in ZQ_STEPS:
+                for cc in range(CHUNKS):
+                    z_quantise(cc, ZQ_STEPS.index(k))
             z_out(e, second, h, accs[second])
+            if k == -1:
+                head_quantise(k + AHEAD)
             if k < 2:
                 widen(6 + k)
             if k in (2, 4):
                 x_quantise(1 + k // 2)
-            if e % 2 == 1:
-                to_interleave.extend([(e // 2, 2 * h), (e // 2, 2 * h + 1)])
 
-            put_off.extend([item for item in ready if item[1] > 0])
-            for item in ready:
-                if item[1] == 0:
-                    z_quantise(*item)
-
-        for item in sorted(put_off, key=lambda cq: cq[1]):
-            z_quantise(*item)
-
-        for i in range(TILES):
-            for n0 in range(0, N, BANK):
-                ready = list(interleaved)
-                interleaved.clear()
-                if to_interleave:
-                    interleave_next()
-                width = P if (i, n0) == (TILES - 1, N - BANK) else BANK
-                for n in range(n0, n0 + BANK, width):
-                    second_product(i, n, width, min(width, BANK // 2) if i == TILES - 1 else width)
-                for item in ready:
-                    z_quantise(*item)
+        for k in range(2 * PARTS, 2 * PARTS + len(to_interleave)):
+            interleave_next(k)
+        quantise_behind = {1: [(0, 2), (1, 2)], 2: [(2, 2)], 3: [(3, 2)], 4: [(0, 3)], 5: [(1, 3)], 7: [(2, 3)], 8: [(3, 3)]}
+        for j in range(2 * TILES - 1):
+            i, n0 = j // 2, (j % 2) * BANK
+            second_product(i, n0, BANK)
+            if j < 2 * TILES - 2:
+                y_out(i, n0, 0, BANK)
+            for item in quantise_behind.get(j, []):
+                z_quantise(*item)
+        y_out(TILES - 1, 0, 0, BANK // 2)
+        y_out(TILES - 1, 0, BANK // 2, BANK)
+        for n0 in range(BANK, N, P):
+            second_product(TILES - 1, n0, P)
+            y_out(TILES - 1, n0, 0, P)

@@ -37,6 +37,7 @@ def tile_teacher_logits_remap_d4_kernel(tc, x_bytes, x_scale, head, b, tau, map_
     nc = tc.nc
     x_v = x_bytes.rearrange("(p i) k -> p i k", i=TILES)
     head_v = head.rearrange("(c p s) k -> c p s k", p=P, s=SLOTS)
+    b_v = b.rearrange("(c p s) -> p c s", p=P, s=SLOTS)
     out_v = out.rearrange("(p i) n -> p i n", i=TILES)
 
     with ExitStack() as ctx:
@@ -53,8 +54,8 @@ def tile_teacher_logits_remap_d4_kernel(tc, x_bytes, x_scale, head, b, tau, map_
         x_pair = {q: keep.tile([P, 2, K], U8, name=f"x_pair{q}") for q in (1, 3)}
         head_single = [keep.tile([P, K], BF16, name=f"head_single{s}") for s in range(2)]
         head_part = {e: work.tile([P, 2, K], BF16, name=f"head_part{e}", tag="rows", bufs=PARTS - 1) for e in range(1, PARTS)}
-        b_rows = keep.tile([P, 512], BF16, name="b_rows")
-        b_sb = keep.tile([P, CHUNKS, SLOTS], BF16, name="b_sb")
+        b_first = keep.tile([P, SLOTS], BF16, name="b_first")
+        b_rest = keep.tile([P, CHUNKS - 1, SLOTS], BF16, name="b_rest")
         tau_sb = keep.tile([P, TILES], BF16, name="tau_sb")
         map_scale_sb = keep.tile([P, CHUNKS, N], U8, name="map_scale_sb", align_bytes=64)
         map_sb = keep.tile([P, CHUNKS, 2 * N], U8, name="map_sb", align_bytes=64)
@@ -72,7 +73,6 @@ def tile_teacher_logits_remap_d4_kernel(tc, x_bytes, x_scale, head, b, tau, map_
             nc.sync.dma_start(out=head_part[e][:], in_=head_v[e // 2, :, 2 * (e % 2) : 2 * (e % 2) + 2, :])
 
         nc.gpsimd.memset(zeros[:].bitcast(I32), 0)
-        nc.gpsimd.memset(b_rows[:].bitcast(I32), 0)
         make_identity(nc, ident[:])
         nc.vector.memset(map_scale_sb[:].rearrange("p c n -> p (c n)").bitcast(I32), 0)
 
@@ -80,17 +80,18 @@ def tile_teacher_logits_remap_d4_kernel(tc, x_bytes, x_scale, head, b, tau, map_
         nc.sync.dma_start(out=x_scale_sb[:], in_=x_scale.rearrange("(p i) j -> p i j", i=TILES))
         load_x_tile(0)
         load_x_tile(1)
-        nc.sync.dma_start(out=b_rows[:CHUNKS, :], in_=b.rearrange("(c v) -> c v", c=CHUNKS))
         nc.sync.dma_start(out=head_single[0][:], in_=head_v[0, :, 0, :])
         load_x_pair(1)
         nc.sync.dma_start(out=head_single[1][:], in_=head_v[0, :, 1, :])
         load_x_tile(4)
         load_head(1)
+        nc.sync.dma_start(out=b_first[:], in_=b_v[:, 0, :])
         load_head(2)
         load_x_tile(5)
         load_head(3)
         load_x_pair(3)
         load_head(4)
+        nc.sync.dma_start(out=b_rest[:], in_=b_v[:, 1:, :])
         for e in range(5, PARTS):
             load_head(e)
         for q in range(4):
@@ -115,12 +116,6 @@ def tile_teacher_logits_remap_d4_kernel(tc, x_bytes, x_scale, head, b, tau, map_
                 column = inv_tau_col[:, 4 * h + ii : 4 * h + ii + 1]
                 nc.tensor.transpose(rows[:, ii, :], column.to_broadcast([P, P]), ident[:])
             nc.scalar.copy(inv_tau[h][:], rows[:])
-
-        def turn_b():
-            turned = bank([P, 2, P])
-            for u in range(2):
-                nc.tensor.transpose(turned[:, u, :], b_rows[:].bitcast(F32)[:, u::2], ident[:])
-            nc.scalar.copy(b_sb[:].bitcast(F32), turned[:, :, :CHUNKS].rearrange("p u c -> p c u"))
 
         x_wide = {}
         x_turned = {}
@@ -206,7 +201,7 @@ def tile_teacher_logits_remap_d4_kernel(tc, x_bytes, x_scale, head, b, tau, map_
 
         def z_out(e, s, h, acc):
             cc, slot = e // 2, 2 * (e % 2) + s
-            bias = b_sb[:, cc]
+            bias = b_first[:] if cc == 0 else b_rest[:, cc - 1]
             nc.vector.scalar_tensor_tensor(
                 z_slots[cc, h][:, slot, :], acc[:], bias[:, slot : slot + 1], inv_tau[h][:].rearrange("p i n -> p (i n)"), op0=ADD, op1=MULT
             )
@@ -262,7 +257,6 @@ def tile_teacher_logits_remap_d4_kernel(tc, x_bytes, x_scale, head, b, tau, map_
         widen(1)
         spread_inv_tau(0)
         spread_inv_tau(1)
-        turn_b()
         warm_up(1)
         x_turn(0)
         head_turn(0, 0)

@@ -27,10 +27,13 @@ PARTS = 2 * CHUNKS
 HALF = T // 2
 PAIR = 2 * P
 
+STEPS = 2 * PARTS
 AHEAD = 2
+LAST_TURN = PARTS - 1 - AHEAD
 SORTED_PARTS = (5, 6)
-ZQ_STEPS = [12, 14]
 X_STEPS = 4
+LAG = 2
+Z_STEP = STEPS - 4
 
 
 def tile_teacher_logits_remap_d4_kernel(tc, x_bytes, x_scale, head, b, tau, map_words, map_scales, c, out):
@@ -53,7 +56,9 @@ def tile_teacher_logits_remap_d4_kernel(tc, x_bytes, x_scale, head, b, tau, map_
         x_single = {i: keep.tile([P, K], U8, name=f"x_single{i}") for i in (0, 1, 4, 5)}
         x_pair = {q: keep.tile([P, 2, K], U8, name=f"x_pair{q}") for q in (1, 3)}
         head_single = [keep.tile([P, K], BF16, name=f"head_single{s}") for s in range(2)]
-        head_part = {e: work.tile([P, 2, K], BF16, name=f"head_part{e}", tag="rows", bufs=PARTS - 1) for e in range(1, PARTS)}
+        head_part = {
+            e: work.tile([P, 2, K], BF16, name=f"head_part{e}", tag="rows", bufs=PARTS - 1) for e in range(1, PARTS)
+        }
         b_first = keep.tile([P, SLOTS], BF16, name="b_first")
         b_rest = keep.tile([P, CHUNKS - 1, SLOTS], BF16, name="b_rest")
         tau_sb = keep.tile([P, TILES], BF16, name="tau_sb")
@@ -278,17 +283,16 @@ def tile_teacher_logits_remap_d4_kernel(tc, x_bytes, x_scale, head, b, tau, map_
         widen(5)
         head_quantise(1)
 
-        last_turn = PARTS - 1 - AHEAD
         to_interleave = [(cc, q) for q in range(4) for cc in range(CHUNKS)]
 
         def interleave_next(k):
-            item = [(cc, q) for cc, q in to_interleave if PARTS * (q // 2) + 2 * cc + 1 <= k - 2][0]
+            item = [(cc, q) for cc, q in to_interleave if PARTS * (q // 2) + 2 * cc + 1 <= k - LAG][0]
             to_interleave.remove(item)
             z_interleave(*item)
 
-        for k in range(2 * PARTS):
+        for k in range(STEPS):
             h, e = divmod(k, PARTS)
-            if k <= last_turn:
+            if k <= LAST_TURN:
                 head_turn(k + AHEAD, 0)
                 head_turn(k + AHEAD, 1)
             if k < X_STEPS:
@@ -296,36 +300,33 @@ def tile_teacher_logits_remap_d4_kernel(tc, x_bytes, x_scale, head, b, tau, map_
             accs = [first_product(e, s, h) for s in range(2)]
             if k + 2 * AHEAD in SORTED_PARTS:
                 head_sort(k + 2 * AHEAD)
-            if k >= last_turn:
+            if k >= LAST_TURN:
                 interleave_next(k)
 
-            if k == last_turn:
+            if k == LAST_TURN:
                 head_quantise(k + AHEAD)
-            first, second = (1, 0) if last_turn < k < ZQ_STEPS[0] else (0, 1)
+            first, second = (1, 0) if LAST_TURN < k < Z_STEP else (0, 1)
             z_out(e, first, h, accs[first])
-            if k < last_turn and k != -1:
+            if k < LAST_TURN:
                 head_quantise(k + AHEAD)
-            if k in ZQ_STEPS:
+            if k in (Z_STEP, Z_STEP + 2):
                 for cc in range(CHUNKS):
-                    z_quantise(cc, ZQ_STEPS.index(k))
+                    z_quantise(cc, (k - Z_STEP) // 2)
             z_out(e, second, h, accs[second])
-            if k == -1:
-                head_quantise(k + AHEAD)
             if k < 2:
                 widen(6 + k)
             if k in (2, 4):
                 x_quantise(1 + k // 2)
 
-        for k in range(2 * PARTS, 2 * PARTS + len(to_interleave)):
+        for k in range(STEPS, STEPS + len(to_interleave)):
             interleave_next(k)
-        quantise_behind = {1: [(0, 2), (1, 2)], 2: [(2, 2)], 3: [(3, 2)], 4: [(0, 3)], 5: [(1, 3)], 7: [(2, 3)], 8: [(3, 3)]}
-        for j in range(2 * TILES - 1):
+        for j in range(2 * (TILES - 1)):
             i, n0 = j // 2, (j % 2) * BANK
             second_product(i, n0, BANK)
-            if j < 2 * TILES - 2:
-                y_out(i, n0, 0, BANK)
-            for item in quantise_behind.get(j, []):
-                z_quantise(*item)
+            y_out(i, n0, 0, BANK)
+            if j < 2 * CHUNKS:
+                z_quantise(j % CHUNKS, 2 + j // CHUNKS)
+        second_product(TILES - 1, 0, BANK)
         y_out(TILES - 1, 0, 0, BANK // 2)
         y_out(TILES - 1, 0, BANK // 2, BANK)
         for n0 in range(BANK, N, P):

@@ -33,7 +33,7 @@ LAST_TURN = PARTS - 1 - AHEAD
 SORTED_PARTS = (5, 6)
 X_STEPS = 4
 LAG = 2
-Z_STEP = STEPS - 4
+Z_STEPS = (STEPS - 4, STEPS - 2)
 
 
 def tile_teacher_logits_remap_d4_kernel(tc, x_bytes, x_scale, head, b, tau, map_words, map_scales, c, out):
@@ -135,9 +135,9 @@ def tile_teacher_logits_remap_d4_kernel(tc, x_bytes, x_scale, head, b, tau, map_
                 codes = row[:, j * B : (j + 1) * B].bitcast(FP8).rearrange("p (r u e) -> p r u e", u=2, e=2)
                 nc.vector.tensor_scalar(by_word[:, j // 4, j % 4], codes, x_scale_sb[:, i, j : j + 1], None, op0=MULT)
 
-        def turn(words, is_sorted, dst):
+        def turn(words, is_sorted, dst, passes):
             turned = bank([P, PASSES, 2, P])
-            for g in range(PASSES):
+            for g in passes:
                 for u in range(2):
                     cols = slice(256 * g + P * u, 256 * g + P * (u + 1)) if is_sorted else slice(256 * g + u, 256 * (g + 1), 2)
                     nc.tensor.transpose(turned[:, g, u, :], words[:, cols], ident[:])
@@ -148,7 +148,7 @@ def tile_teacher_logits_remap_d4_kernel(tc, x_bytes, x_scale, head, b, tau, map_
                 x_turned[i // 2] = work.tile([P, PASSES, PAIR, 4], BF16, name="x_turned", align_bytes=64, bufs=2)
             words = x_wide[i][:].bitcast(F32)
             dst = x_turned[i // 2][:, :, (i % 2) * P : (i % 2 + 1) * P, :].rearrange("p g r t -> p g (r t)").bitcast(F32)
-            turn(words, True, dst.rearrange("p g (r u) -> p g r u", u=2))
+            turn(words, True, dst.rearrange("p g (r u) -> p g r u", u=2), (0, 1) if i < 4 else (1, 0))
 
         def x_quantise(q):
             cols = slice((q % 2) * PAIR, (q % 2 + 1) * PAIR)
@@ -175,7 +175,7 @@ def tile_teacher_logits_remap_d4_kernel(tc, x_bytes, x_scale, head, b, tau, map_
                 head_turned[e] = work.tile([P, 2, PASSES, P, 4], BF16, name="head_turned", align_bytes=64, bufs=3)
             row = head_single[s][:] if e == 0 else head_sorted.get(e, head_part[e])[:, s, :]
             dst = head_turned[e][:, s].rearrange("p g r t -> p (g r t)").bitcast(F32)
-            turn(row.bitcast(F32), e in head_sorted, dst.rearrange("p (g r u) -> p g r u", g=PASSES, u=2))
+            turn(row.bitcast(F32), e in head_sorted, dst.rearrange("p (g r u) -> p g r u", g=PASSES, u=2), (0, 1))
 
         def head_quantise(e):
             nc.vector.quantize_mx(
@@ -231,18 +231,18 @@ def tile_teacher_logits_remap_d4_kernel(tc, x_bytes, x_scale, head, b, tau, map_
         y_accs = {}
         y_rows = {}
 
-        def second_product(i, n0, width):
+        def second_product(i, n0, width, acc):
             cols = slice((i % 4) * P, (i % 4 + 1) * P)
-            acc = bank([P, width])
-            for cc in range(CHUNKS):
+            order = (0, 1, 2, 3) if i == 0 else (2, 0, 1, 3)
+            for cc in order:
                 nc.tensor.matmul_mx(
                     out=acc[:],
                     lhsT=z_codes[cc, i // 4][:, cols].bitcast(FP8X4),
                     lhsT_scale=z_scales[cc, i // 4][:, cols],
                     rhs=map_sb[:, cc, 2 * n0 : 2 * (n0 + width)].bitcast(FP4X4),
                     rhs_scale=map_scale_sb[:, cc, n0 : n0 + width],
-                    start=(cc == 0),
-                    stop=(cc == CHUNKS - 1),
+                    start=(cc == order[0]),
+                    stop=(cc == order[-1]),
                 )
             y_accs[i, n0] = acc
 
@@ -305,13 +305,13 @@ def tile_teacher_logits_remap_d4_kernel(tc, x_bytes, x_scale, head, b, tau, map_
 
             if k == LAST_TURN:
                 head_quantise(k + AHEAD)
-            first, second = (1, 0) if LAST_TURN < k < Z_STEP else (0, 1)
+            first, second = (1, 0) if LAST_TURN < k and k not in Z_STEPS else (0, 1)
             z_out(e, first, h, accs[first])
             if k < LAST_TURN:
                 head_quantise(k + AHEAD)
-            if k in (Z_STEP, Z_STEP + 2):
+            if k in Z_STEPS:
                 for cc in range(CHUNKS):
-                    z_quantise(cc, (k - Z_STEP) // 2)
+                    z_quantise(cc, Z_STEPS.index(k))
             z_out(e, second, h, accs[second])
             if k < 2:
                 widen(6 + k)
@@ -322,13 +322,14 @@ def tile_teacher_logits_remap_d4_kernel(tc, x_bytes, x_scale, head, b, tau, map_
             interleave_next(k)
         for j in range(2 * (TILES - 1)):
             i, n0 = j // 2, (j % 2) * BANK
-            second_product(i, n0, BANK)
+            second_product(i, n0, BANK, bank([P, BANK]))
             y_out(i, n0, 0, BANK)
             if j < 2 * CHUNKS:
                 z_quantise(j % CHUNKS, 2 + j // CHUNKS)
-        second_product(TILES - 1, 0, BANK)
+        second_product(TILES - 1, 0, BANK, bank([P, BANK]))
         y_out(TILES - 1, 0, 0, BANK // 2)
         y_out(TILES - 1, 0, BANK // 2, BANK)
+        narrow = [bank([P, P]) for n0 in range(BANK, N, P)]
         for n0 in range(BANK, N, P):
-            second_product(TILES - 1, n0, P)
+            second_product(TILES - 1, n0, P, narrow.pop())
             y_out(TILES - 1, n0, 0, P)

@@ -16,6 +16,8 @@ FP8X4 = mybir.dt.float8_e4m3fn_x4
 FP4X4 = mybir.dt.float4_e2m1fn_x4
 ADD = mybir.AluOpType.add
 MULT = mybir.AluOpType.mult
+COPY = mybir.ActivationFunctionType.Copy
+IDENTITY = mybir.ActivationFunctionType.Identity
 
 P = 128
 BANK = 512
@@ -27,13 +29,10 @@ PARTS = 2 * CHUNKS
 HALF = T // 2
 PAIR = 2 * P
 
-STEPS = 2 * PARTS
-AHEAD = 2
-LAST_TURN = PARTS - 1 - AHEAD
-SORTED_PARTS = (5, 6)
-X_STEPS = 4
-LAG = 2
-Z_STEPS = (STEPS - 4, STEPS - 2)
+SHARED_TILES = 2
+STAGED = 3
+ZQ = {1: (2, 2, 2), 4: (0, 2, 3), 7: (2, 2, 3)}
+SHARED_BANKS = ((0, 0, 1), (0, 1, 1))
 
 
 def tile_teacher_logits_remap_d4_kernel(tc, x_bytes, x_scale, head, b, tau, map_words, map_scales, c, out):
@@ -49,8 +48,11 @@ def tile_teacher_logits_remap_d4_kernel(tc, x_bytes, x_scale, head, b, tau, map_
         psum = ctx.enter_context(tc.psum_pool(name="psum", bufs=1))
         ctx.enter_context(tc.manual_schedule())
 
-        def bank(shape):
-            return psum.tile(shape, F32, name="bank", tag="bank", bufs=8)
+        free_banks = list(range(8))
+
+        def take_bank(shape):
+            n = free_banks.pop(0)
+            return n, psum.tile(shape, F32, name=f"bank{n}", tag=f"bank{n}")
 
         x_scale_sb = keep.tile([P, TILES, K // B], F32, name="x_scale_sb")
         x_single = {i: keep.tile([P, K], U8, name=f"x_single{i}") for i in (0, 1, 4, 5)}
@@ -77,7 +79,7 @@ def tile_teacher_logits_remap_d4_kernel(tc, x_bytes, x_scale, head, b, tau, map_
         def load_head(e):
             nc.sync.dma_start(out=head_part[e][:], in_=head_v[e // 2, :, 2 * (e % 2) : 2 * (e % 2) + 2, :])
 
-        nc.gpsimd.memset(zeros[:].bitcast(I32), 0)
+        nc.vector.memset(zeros[:].bitcast(I32), 0)
         make_identity(nc, ident[:])
         nc.vector.memset(map_scale_sb[:].rearrange("p c n -> p (c n)").bitcast(I32), 0)
 
@@ -107,48 +109,76 @@ def tile_teacher_logits_remap_d4_kernel(tc, x_bytes, x_scale, head, b, tau, map_
         nc.sync.dma_start(out=map_sb[:].bitcast(I32), in_=map_words.rearrange("c p n -> p c n").bitcast(I32))
         nc.sync.dma_start(out=c_rows[:], in_=c.partition_broadcast(P))
 
-        def warm_up(count):
-            scratch = bank([P, BANK])
-            for n in range(count):
-                nc.tensor.matmul(scratch[:], lhsT=zeros[:, :P], rhs=zeros[:], start=True, stop=True)
-
         inv_tau_col = keep.tile([P, TILES], F32, name="inv_tau_col")
         inv_tau = [keep.tile([P, 4, P], F32, name=f"inv_tau{h}") for h in range(2)]
+        tau_bank = {}
 
-        def spread_inv_tau(h):
-            rows = bank([P, 4, P])
-            for ii in range(4):
-                column = inv_tau_col[:, 4 * h + ii : 4 * h + ii + 1]
-                nc.tensor.transpose(rows[:, ii, :], column.to_broadcast([P, P]), ident[:])
-            nc.scalar.copy(inv_tau[h][:], rows[:])
+        def spread_inv_tau(i, as_product):
+            if i % 4 == 0 and i // 4 not in tau_bank:
+                tau_bank[i // 4] = take_bank([P, 4, P])
+            rows = tau_bank[i // 4][1]
+            column = inv_tau_col[:, i : i + 1].to_broadcast([P, P])
+            if as_product:
+                nc.tensor.matmul(rows[:, i % 4, :], lhsT=column, rhs=ident[:], start=True, stop=True)
+            else:
+                nc.tensor.transpose(rows[:, i % 4, :], column, ident[:])
+
+        def inv_tau_out(h):
+            n, rows = tau_bank[h]
+            if h == 0:
+                nc.scalar.copy(inv_tau[h][:], rows[:])
+            else:
+                nc.vector.tensor_copy(inv_tau[h][:], rows[:])
+            free_banks.append(n)
+
+        def warm_up(count):
+            tau_bank[0] = take_bank([P, 4, P])
+            for n in range(count):
+                nc.tensor.matmul(tau_bank[0][1][:].rearrange("p i n -> p (i n)"), lhsT=zeros[:, :P], rhs=zeros[:], start=True, stop=True)
 
         x_wide = {}
         x_turned = {}
+        x_banks = {}
         x_codes = [keep.tile([P, PASSES, HALF], U32, name=f"x_codes{h}", align_bytes=64) for h in range(2)]
         x_scales = [keep.tile([P, PASSES, HALF], U8, name=f"x_scales{h}", align_bytes=64) for h in range(2)]
 
-        def widen(i):
-            x_wide[i] = work.tile([P, K], BF16, name="x_wide", bufs=5)
-            row = x_single[i][:] if i in x_single else x_pair[i // 2][:, i % 2]
-            by_word = x_wide[i][:].rearrange("p (g u q r e) -> p g q r u e", g=PASSES, u=2, q=4, e=2)
-            for j in range(K // B):
-                codes = row[:, j * B : (j + 1) * B].bitcast(FP8).rearrange("p (r u e) -> p r u e", u=2, e=2)
-                nc.vector.tensor_scalar(by_word[:, j // 4, j % 4], codes, x_scale_sb[:, i, j : j + 1], None, op0=MULT)
+        shared_scale = keep.tile([P, SHARED_TILES, 4], F32, name="shared_scale")
+        nc.scalar.activation(shared_scale[:], x_scale_sb[:, :SHARED_TILES, 4:], COPY)
 
-        def turn(words, is_sorted, dst, passes):
-            turned = bank([P, PASSES, 2, P])
-            for g in passes:
+        def widen(i, g):
+            x_wide[i, g] = work.tile([P, 512], BF16, name="x_wide", bufs=10)
+            row = x_single[i][:] if i in x_single else x_pair[i // 2][:, i % 2]
+            by_word = x_wide[i, g][:].rearrange("p (u q r e) -> p q r u e", u=2, q=4, e=2)
+            for q in range(4):
+                j = 4 * g + q
+                codes = row[:, j * B : (j + 1) * B].bitcast(FP8)
+                scale = x_scale_sb[:, i, j : j + 1]
+                if g == 1 and i < SHARED_TILES:
+                    nc.scalar.activation(x_wide[i, g][:, q * B : (q + 1) * B], codes, COPY, scale=shared_scale[:, i, q : q + 1])
+                else:
+                    nc.vector.tensor_scalar(by_word[:, q], codes.rearrange("p (r u e) -> p r u e", u=2, e=2), scale, None, op0=MULT)
+
+        def turn(passes):
+            n, turned = take_bank([P, PASSES, 2, P])
+            for g, (words, is_sorted) in enumerate(passes):
                 for u in range(2):
-                    cols = slice(256 * g + P * u, 256 * g + P * (u + 1)) if is_sorted else slice(256 * g + u, 256 * (g + 1), 2)
+                    cols = slice(P * u, P * (u + 1)) if is_sorted else slice(u, 2 * P, 2)
                     nc.tensor.transpose(turned[:, g, u, :], words[:, cols], ident[:])
+            return n, turned
+
+        def turned_out(bank, dst):
+            n, turned = bank
             nc.scalar.copy(dst, turned[:].rearrange("p g u r -> p g r u"))
+            free_banks.append(n)
 
         def x_turn(i):
+            x_banks[i] = turn([(x_wide[i, g][:].bitcast(F32), not (g == 1 and i < SHARED_TILES)) for g in range(PASSES)])
+
+        def x_out(i):
             if i % 2 == 0:
                 x_turned[i // 2] = work.tile([P, PASSES, PAIR, 4], BF16, name="x_turned", align_bytes=64, bufs=2)
-            words = x_wide[i][:].bitcast(F32)
             dst = x_turned[i // 2][:, :, (i % 2) * P : (i % 2 + 1) * P, :].rearrange("p g r t -> p g (r t)").bitcast(F32)
-            turn(words, True, dst.rearrange("p g (r u) -> p g r u", u=2), (0, 1) if i < 4 else (1, 0))
+            turned_out(x_banks[i], dst.rearrange("p g (r u) -> p g r u", u=2))
 
         def x_quantise(q):
             cols = slice((q % 2) * PAIR, (q % 2 + 1) * PAIR)
@@ -159,39 +189,47 @@ def tile_teacher_logits_remap_d4_kernel(tc, x_bytes, x_scale, head, b, tau, map_
                     in_=x_turned[q][:, g].rearrange("p n t -> p (n t)"),
                 )
 
-        head_sorted = {e: keep.tile([P, 2, K], BF16, name=f"head_sorted{e}") for e in SORTED_PARTS}
+        head_sorted = {}
         head_turned = {}
+        head_banks = {}
         head_codes = [keep.tile([P, 2, PASSES, P], U32, name=f"head_codes{e}", align_bytes=64) for e in range(PARTS)]
         head_scales = [keep.tile([P, 2, PASSES, P], U8, name=f"head_scales{e}", align_bytes=64) for e in range(PARTS)]
 
         def head_sort(e):
+            head_sorted[e] = work.tile([P, 2, K], BF16, name="head_sorted", bufs=3)
             nc.scalar.copy(
                 head_sorted[e][:].bitcast(F32).rearrange("p s (g u r) -> p (s g) u r", g=PASSES, u=2),
                 head_part[e][:].bitcast(F32).rearrange("p s (g r u) -> p (s g) u r", g=PASSES, u=2),
             )
 
+        def staged():
+            return work.tile([P, 2048], BF16, name="staged", align_bytes=64, bufs=STAGED)
+
         def head_turn(e, s):
-            if s == 0:
-                head_turned[e] = work.tile([P, 2, PASSES, P, 4], BF16, name="head_turned", align_bytes=64, bufs=3)
             row = head_single[s][:] if e == 0 else head_sorted.get(e, head_part[e])[:, s, :]
-            dst = head_turned[e][:, s].rearrange("p g r t -> p (g r t)").bitcast(F32)
-            turn(row.bitcast(F32), e in head_sorted, dst.rearrange("p (g r u) -> p g r u", g=PASSES, u=2), (0, 1))
+            words = row.bitcast(F32)
+            head_banks[e, s] = turn([(words[:, 256 * g : 256 * (g + 1)], e in head_sorted) for g in range(PASSES)])
+
+        def head_out(e, s):
+            if s == 0:
+                head_turned[e] = staged()
+            dst = head_turned[e][:, 1024 * s : 1024 * (s + 1)].bitcast(F32)
+            turned_out(head_banks[e, s], dst.rearrange("p (g r u) -> p g r u", g=PASSES, u=2))
 
         def head_quantise(e):
             nc.vector.quantize_mx(
                 out=head_codes[e][:].rearrange("p s g m -> p (s g m)").bitcast(FP8X4),
                 scales=head_scales[e][:].rearrange("p s g m -> p (s g m)"),
-                in_=head_turned[e][:].rearrange("p s g m t -> p (s g m t)"),
+                in_=head_turned[e][:],
             )
 
-        units = [(cc, h) for h in range(2) for cc in range(CHUNKS)]
-        z_slots = {u: keep.tile([P, SLOTS, HALF], BF16, name=f"z_slots{u[0]}_{u[1]}") for u in units}
-        z_words = {u: keep.tile([P, HALF, SLOTS], BF16, name=f"z_words{u[0]}_{u[1]}", align_bytes=64) for u in units}
-        z_codes = {u: keep.tile([P, HALF], U32, name=f"z_codes{u[0]}_{u[1]}", align_bytes=64) for u in units}
-        z_scales = {u: keep.tile([P, HALF], U8, name=f"z_scales{u[0]}_{u[1]}", align_bytes=64) for u in units}
+        z_slots = {(cc, h): keep.tile([P, SLOTS, HALF], BF16, name=f"z_slots{cc}_{h}") for h in range(2) for cc in range(CHUNKS)}
+        z_words = {}
+        z_codes = [keep.tile([P, CHUNKS, PAIR], U32, name=f"z_codes{q}", align_bytes=64) for q in range(4)]
+        z_scales = [keep.tile([P, CHUNKS, PAIR], U8, name=f"z_scales{q}", align_bytes=64) for q in range(4)]
 
         def first_product(e, s, h):
-            acc = bank([P, HALF])
+            n, acc = take_bank([P, HALF])
             for g in range(PASSES):
                 nc.tensor.matmul_mx(
                     out=acc[:],
@@ -202,134 +240,240 @@ def tile_teacher_logits_remap_d4_kernel(tc, x_bytes, x_scale, head, b, tau, map_
                     start=(g == 0),
                     stop=(g == PASSES - 1),
                 )
-            return acc
+            return n, acc
 
-        def z_out(e, s, h, acc):
+        def z_out(e, s, h, bank):
+            n, acc = bank
             cc, slot = e // 2, 2 * (e % 2) + s
-            bias = b_first[:] if cc == 0 else b_rest[:, cc - 1]
-            nc.vector.scalar_tensor_tensor(
-                z_slots[cc, h][:, slot, :], acc[:], bias[:, slot : slot + 1], inv_tau[h][:].rearrange("p i n -> p (i n)"), op0=ADD, op1=MULT
-            )
+            bias = (b_first[:] if cc == 0 else b_rest[:, cc - 1])[:, slot : slot + 1]
+            factor = inv_tau[h][:].rearrange("p i n -> p (i n)")
+            if (e, s, h) in SHARED_BANKS:
+                sums = work.tile([P, HALF], F32, name="sums", bufs=2)
+                nc.scalar.activation(sums[:], acc[:], IDENTITY, bias=bias)
+                nc.gpsimd.tensor_tensor(z_slots[cc, h][:, slot, :], sums[:], factor, op=MULT)
+            else:
+                nc.vector.scalar_tensor_tensor(z_slots[cc, h][:, slot, :], acc[:], bias, factor, op0=ADD, op1=MULT)
+            free_banks.append(n)
 
         def z_interleave(cc, q):
-            h = q // 2
             cols = slice((q % 2) * PAIR, (q % 2 + 1) * PAIR)
-            nc.scalar.copy(
-                z_words[cc, h][:, cols, :].rearrange("p (n i) s -> p n s i", i=4),
-                z_slots[cc, h][:, :, cols].rearrange("p s (n i) -> p n s i", i=4),
-            )
+            dst = z_words[cc // 2, q][:, 1024 * (cc % 2) : 1024 * (cc % 2 + 1)].rearrange("p (n i s) -> p n s i", i=4, s=SLOTS)
+            src = z_slots[cc, q // 2][:, :, cols].rearrange("p s (n i) -> p n s i", i=4)
+            nc.scalar.copy(dst, src)
 
-        def z_quantise(cc, q):
-            h = q // 2
-            cols = slice((q % 2) * PAIR, (q % 2 + 1) * PAIR)
+        def z_quantise(first, count, q):
+            lo = 1024 * (first % 2)
             nc.vector.quantize_mx(
-                out=z_codes[cc, h][:, cols].bitcast(FP8X4),
-                scales=z_scales[cc, h][:, cols],
-                in_=z_words[cc, h][:, cols, :].rearrange("p n s -> p (n s)"),
+                out=z_codes[q][:, first : first + count, :].rearrange("p c n -> p (c n)").bitcast(FP8X4),
+                scales=z_scales[q][:, first : first + count, :].rearrange("p c n -> p (c n)"),
+                in_=z_words[first // 2, q][:, lo : lo + 1024 * count],
             )
 
-        y_accs = {}
         y_rows = {}
 
         def second_product(i, n0, width, acc):
-            cols = slice((i % 4) * P, (i % 4 + 1) * P)
-            order = (0, 1, 2, 3) if i == 0 else (2, 0, 1, 3)
-            for cc in order:
+            cols = slice((i % 2) * P, (i % 2 + 1) * P)
+            for cc in range(CHUNKS):
                 nc.tensor.matmul_mx(
-                    out=acc[:],
-                    lhsT=z_codes[cc, i // 4][:, cols].bitcast(FP8X4),
-                    lhsT_scale=z_scales[cc, i // 4][:, cols],
+                    out=acc,
+                    lhsT=z_codes[i // 2][:, cc, cols].bitcast(FP8X4),
+                    lhsT_scale=z_scales[i // 2][:, cc, cols],
                     rhs=map_sb[:, cc, 2 * n0 : 2 * (n0 + width)].bitcast(FP4X4),
                     rhs_scale=map_scale_sb[:, cc, n0 : n0 + width],
-                    start=(cc == order[0]),
-                    stop=(cc == order[-1]),
+                    start=(cc == 0),
+                    stop=(cc == CHUNKS - 1),
                 )
-            y_accs[i, n0] = acc
 
-        def y_out(i, n0, lo, hi):
+        def y_out(i, n0, width, acc):
             if i not in y_rows:
                 if i < TILES - 1:
                     y_rows[i] = work.tile([P, N], F32, name="y", tag="rows", bufs=PARTS - 1)
                 else:
                     y_rows[i] = keep.tile([P, N], F32, name="y_last")
-            cols = slice(n0 + lo, n0 + hi)
-            nc.vector.tensor_tensor(y_rows[i][:, cols], y_accs[i, n0][:, lo:hi], c_rows[:, cols], op=ADD)
+            cols = slice(n0, n0 + width)
+            nc.vector.tensor_tensor(y_rows[i][:, cols], acc, c_rows[:, cols], op=ADD)
             nc.sync.dma_start(out=out_v[:, i, cols], in_=y_rows[i][:, cols])
 
-        warm_up(3)
         nc.vector.reciprocal(inv_tau_col[:], tau_sb[:])
-        widen(0)
-        widen(1)
-        spread_inv_tau(0)
-        spread_inv_tau(1)
-        warm_up(1)
+        warm_up(3)
+        for i in range(4, 8):
+            spread_inv_tau(i, False)
+        spread_inv_tau(0, True)
+        for i in range(2):
+            widen(i, 0)
+            widen(i, 1)
+        inv_tau_out(1)
         x_turn(0)
+        x_out(0)
         head_turn(0, 0)
+        head_out(0, 0)
         x_turn(1)
-        warm_up(1)
-        widen(2)
-        widen(3)
+        x_out(1)
+        for i in range(2, 5):
+            widen(i, 0)
+            widen(i, 1)
+        spread_inv_tau(1, True)
         head_turn(0, 1)
+        head_out(0, 1)
         x_turn(2)
-        warm_up(1)
-        widen(4)
-        x_quantise(0)
+        x_out(2)
         x_turn(3)
+        x_out(3)
+        spread_inv_tau(2, True)
+        x_quantise(0)
         head_quantise(0)
         head_turn(1, 0)
+        head_out(1, 0)
         head_turn(1, 1)
-        warm_up(1)
+        head_out(1, 1)
+        spread_inv_tau(3, True)
+        inv_tau_out(0)
         x_quantise(1)
-        widen(5)
+        widen(5, 0)
+        widen(5, 1)
         head_quantise(1)
 
-        to_interleave = [(cc, q) for q in range(4) for cc in range(CHUNKS)]
+        accs = {}
 
-        def interleave_next(k):
-            item = [(cc, q) for cc, q in to_interleave if PARTS * (q // 2) + 2 * cc + 1 <= k - LAG][0]
-            to_interleave.remove(item)
-            z_interleave(*item)
+        def step(e, h):
+            for s in range(2):
+                accs[e, s, h] = first_product(e, s, h)
 
-        for k in range(STEPS):
-            h, e = divmod(k, PARTS)
-            if k <= LAST_TURN:
-                head_turn(k + AHEAD, 0)
-                head_turn(k + AHEAD, 1)
-            if k < X_STEPS:
-                x_turn(4 + k)
-            accs = [first_product(e, s, h) for s in range(2)]
-            if k + 2 * AHEAD in SORTED_PARTS:
-                head_sort(k + 2 * AHEAD)
-            if k >= LAST_TURN:
-                interleave_next(k)
+        def zo(e, s, h):
+            z_out(e, s, h, accs[e, s, h])
 
-            if k == LAST_TURN:
-                head_quantise(k + AHEAD)
-            first, second = (1, 0) if LAST_TURN < k and k not in Z_STEPS else (0, 1)
-            z_out(e, first, h, accs[first])
-            if k < LAST_TURN:
-                head_quantise(k + AHEAD)
-            if k in Z_STEPS:
-                for cc in range(CHUNKS):
-                    z_quantise(cc, Z_STEPS.index(k))
-            z_out(e, second, h, accs[second])
-            if k < 2:
-                widen(6 + k)
-            if k in (2, 4):
-                x_quantise(1 + k // 2)
+        def part(e):
+            head_turn(e, 0)
+            head_turn(e, 1)
 
-        for k in range(STEPS, STEPS + len(to_interleave)):
-            interleave_next(k)
-        for j in range(2 * (TILES - 1)):
+        def part_out(e):
+            head_out(e, 0)
+            head_out(e, 1)
+
+        def wide(i):
+            widen(i, 0)
+            widen(i, 1)
+
+        for q in range(4):
+            for cp in range(2):
+                z_words[cp, q] = keep.tile([P, 2048], BF16, name=f"z_words{cp}_{q}", align_bytes=64)
+        part(2)
+        x_turn(4)
+        step(0, 0)
+        part_out(2)
+        x_out(4)
+        zo(0, 0, 0)
+        head_quantise(2)
+        zo(0, 1, 0)
+        wide(6)
+        part(3)
+        x_turn(5)
+        step(1, 0)
+        part_out(3)
+        x_out(5)
+        head_sort(5)
+        zo(1, 0, 0)
+        head_quantise(3)
+        zo(1, 1, 0)
+        x_quantise(2)
+        part(4)
+        x_turn(6)
+        step(2, 0)
+        part_out(4)
+        head_sort(6)
+        x_out(6)
+        zo(2, 0, 0)
+        head_quantise(4)
+        zo(2, 1, 0)
+        wide(7)
+        part(5)
+        step(3, 0)
+        part_out(5)
+        head_sort(7)
+        zo(3, 0, 0)
+        head_quantise(5)
+        zo(3, 1, 0)
+        part(6)
+        x_turn(7)
+        step(4, 0)
+        part_out(6)
+        zo(4, 0, 0)
+        head_quantise(6)
+        zo(4, 1, 0)
+        part(7)
+        step(5, 0)
+        part_out(7)
+        x_out(7)
+        head_quantise(7)
+        x_quantise(3)
+        zo(5, 1, 0)
+        zo(5, 0, 0)
+        ybank = {}
+
+        def y_mm(j):
             i, n0 = j // 2, (j % 2) * BANK
-            second_product(i, n0, BANK, bank([P, BANK]))
-            y_out(i, n0, 0, BANK)
-            if j < 2 * CHUNKS:
-                z_quantise(j % CHUNKS, 2 + j // CHUNKS)
-        second_product(TILES - 1, 0, BANK, bank([P, BANK]))
-        y_out(TILES - 1, 0, 0, BANK // 2)
-        y_out(TILES - 1, 0, BANK // 2, BANK)
-        narrow = [bank([P, P]) for n0 in range(BANK, N, P)]
-        for n0 in range(BANK, N, P):
-            second_product(TILES - 1, n0, P, narrow.pop())
-            y_out(TILES - 1, n0, 0, P)
+            ybank[j] = take_bank([P, BANK])
+            second_product(i, n0, BANK, ybank[j][1][:])
+
+        def y_o(j):
+            y_out(j // 2, (j % 2) * BANK, BANK, ybank[j][1][:])
+            free_banks.append(ybank[j][0])
+
+        def both(e, h):
+            zo(e, 1, h)
+            zo(e, 0, h)
+
+        z_interleave(0, 0)
+        z_interleave(1, 0)
+        step(6, 0)
+        both(6, 0)
+        step(7, 0)
+        both(7, 0)
+        step(0, 1)
+        zo(0, 0, 1)
+        zo(0, 1, 1)
+        z_interleave(2, 0)
+        z_interleave(3, 0)
+        z_interleave(0, 1)
+        step(1, 1)
+        both(1, 1)
+        for cc in range(1, 4):
+            z_interleave(cc, 1)
+        step(2, 1)
+        both(2, 1)
+        step(3, 1)
+        both(3, 1)
+        z_quantise(0, 2, 0)
+        z_interleave(0, 2)
+        z_interleave(1, 2)
+        step(4, 1)
+        zo(4, 0, 1)
+        z_quantise(2, 2, 0)
+        zo(4, 1, 1)
+        step(5, 1)
+        both(5, 1)
+        z_quantise(0, 2, 1)
+        z_interleave(2, 2)
+        step(6, 1)
+        zo(6, 0, 1)
+        z_quantise(2, 2, 1)
+        zo(6, 1, 1)
+        step(7, 1)
+        both(7, 1)
+        z_interleave(3, 2)
+        for cc in range(4):
+            z_interleave(cc, 3)
+        z_quantise(0, 2, 2)
+        for j in range(14):
+            y_mm(j)
+            y_o(j)
+            if j in ZQ:
+                z_quantise(*ZQ[j])
+        n, acc = take_bank([P, BANK])
+        second_product(TILES - 1, 0, BANK, acc[:])
+        y_out(TILES - 1, 0, BANK // 2, acc[:, : BANK // 2])
+        y_out(TILES - 1, BANK // 2, BANK // 2, acc[:, BANK // 2 :])
+        for n0, width in ((512, 256), (768, 128), (896, 128)):
+            n, acc = take_bank([P, width])
+            second_product(TILES - 1, n0, width, acc[:])
+            y_out(TILES - 1, n0, width, acc[:])

@@ -113,28 +113,22 @@ def tile_teacher_logits_remap_d4_kernel(tc, x_bytes, x_scale, head, b, tau, map_
         inv_tau = [keep.tile([P, 4, P], F32, name=f"inv_tau{h}") for h in range(2)]
         tau_bank = {}
 
-        def spread_inv_tau(i, as_product):
-            if i % 4 == 0 and i // 4 not in tau_bank:
-                tau_bank[i // 4] = take_bank([P, 4, P])
-            rows = tau_bank[i // 4][1]
-            column = inv_tau_col[:, i : i + 1].to_broadcast([P, P])
-            if as_product:
-                nc.tensor.matmul(rows[:, i % 4, :], lhsT=column, rhs=ident[:], start=True, stop=True)
-            else:
-                nc.tensor.transpose(rows[:, i % 4, :], column, ident[:])
+        def warm_up(bank, count):
+            for n in range(count):
+                nc.tensor.matmul(bank, lhsT=zeros[:, :P], rhs=zeros[:], start=True, stop=True)
+
+        def spread_inv_tau(h, warm_ups):
+            tau_bank[h] = take_bank([P, 4, P])
+            rows = tau_bank[h][1]
+            warm_up(rows[:].rearrange("p i n -> p (i n)"), warm_ups)
+            for ii in range(4):
+                column = inv_tau_col[:, 4 * h + ii : 4 * h + ii + 1]
+                nc.tensor.transpose(rows[:, ii, :], column.to_broadcast([P, P]), ident[:])
 
         def inv_tau_out(h):
             n, rows = tau_bank[h]
-            if h == 0:
-                nc.scalar.copy(inv_tau[h][:], rows[:])
-            else:
-                nc.vector.tensor_copy(inv_tau[h][:], rows[:])
+            nc.vector.tensor_copy(inv_tau[h][:], rows[:])
             free_banks.append(n)
-
-        def warm_up(count):
-            tau_bank[0] = take_bank([P, 4, P])
-            for n in range(count):
-                nc.tensor.matmul(tau_bank[0][1][:].rearrange("p i n -> p (i n)"), lhsT=zeros[:, :P], rhs=zeros[:], start=True, stop=True)
 
         x_wide = {}
         x_turned = {}
@@ -158,8 +152,9 @@ def tile_teacher_logits_remap_d4_kernel(tc, x_bytes, x_scale, head, b, tau, map_
                 else:
                     nc.vector.tensor_scalar(by_word[:, q], codes.rearrange("p (r u e) -> p r u e", u=2, e=2), scale, None, op0=MULT)
 
-        def turn(passes):
+        def turn(passes, warm_ups):
             n, turned = take_bank([P, PASSES, 2, P])
+            warm_up(turned[:].rearrange("p g u r -> p (g u r)"), warm_ups)
             for g, (words, is_sorted) in enumerate(passes):
                 for u in range(2):
                     cols = slice(P * u, P * (u + 1)) if is_sorted else slice(u, 2 * P, 2)
@@ -171,8 +166,8 @@ def tile_teacher_logits_remap_d4_kernel(tc, x_bytes, x_scale, head, b, tau, map_
             nc.scalar.copy(dst, turned[:].rearrange("p g u r -> p g r u"))
             free_banks.append(n)
 
-        def x_turn(i):
-            x_banks[i] = turn([(x_wide[i, g][:].bitcast(F32), not (g == 1 and i < SHARED_TILES)) for g in range(PASSES)])
+        def x_turn(i, warm_ups=0):
+            x_banks[i] = turn([(x_wide[i, g][:].bitcast(F32), not (g == 1 and i < SHARED_TILES)) for g in range(PASSES)], warm_ups)
 
         def x_out(i):
             if i % 2 == 0:
@@ -205,10 +200,10 @@ def tile_teacher_logits_remap_d4_kernel(tc, x_bytes, x_scale, head, b, tau, map_
         def staged():
             return work.tile([P, 2048], BF16, name="staged", align_bytes=64, bufs=STAGED)
 
-        def head_turn(e, s):
+        def head_turn(e, s, warm_ups=0):
             row = head_single[s][:] if e == 0 else head_sorted.get(e, head_part[e])[:, s, :]
             words = row.bitcast(F32)
-            head_banks[e, s] = turn([(words[:, 256 * g : 256 * (g + 1)], e in head_sorted) for g in range(PASSES)])
+            head_banks[e, s] = turn([(words[:, 256 * g : 256 * (g + 1)], e in head_sorted) for g in range(PASSES)], warm_ups)
 
         def head_out(e, s):
             if s == 0:
@@ -295,15 +290,13 @@ def tile_teacher_logits_remap_d4_kernel(tc, x_bytes, x_scale, head, b, tau, map_
             nc.sync.dma_start(out=out_v[:, i, cols], in_=y_rows[i][:, cols])
 
         nc.vector.reciprocal(inv_tau_col[:], tau_sb[:])
-        warm_up(3)
-        for i in range(4, 8):
-            spread_inv_tau(i, False)
-        spread_inv_tau(0, True)
+        spread_inv_tau(1, 3)
+        spread_inv_tau(0, 0)
         for i in range(2):
             widen(i, 0)
             widen(i, 1)
         inv_tau_out(1)
-        x_turn(0)
+        x_turn(0, 1)
         x_out(0)
         head_turn(0, 0)
         head_out(0, 0)
@@ -312,26 +305,23 @@ def tile_teacher_logits_remap_d4_kernel(tc, x_bytes, x_scale, head, b, tau, map_
         for i in range(2, 5):
             widen(i, 0)
             widen(i, 1)
-        spread_inv_tau(1, True)
-        head_turn(0, 1)
+        head_turn(0, 1, 1)
         head_out(0, 1)
         x_turn(2)
         x_out(2)
         x_turn(3)
         x_out(3)
-        spread_inv_tau(2, True)
         x_quantise(0)
         head_quantise(0)
-        head_turn(1, 0)
+        head_turn(1, 0, 1)
         head_out(1, 0)
         head_turn(1, 1)
         head_out(1, 1)
-        spread_inv_tau(3, True)
-        inv_tau_out(0)
         x_quantise(1)
         widen(5, 0)
         widen(5, 1)
         head_quantise(1)
+        inv_tau_out(0)
 
         accs = {}
 
@@ -357,7 +347,8 @@ def tile_teacher_logits_remap_d4_kernel(tc, x_bytes, x_scale, head, b, tau, map_
         for q in range(4):
             for cp in range(2):
                 z_words[cp, q] = keep.tile([P, 2048], BF16, name=f"z_words{cp}_{q}", align_bytes=64)
-        part(2)
+        head_turn(2, 0, 1)
+        head_turn(2, 1)
         x_turn(4)
         step(0, 0)
         part_out(2)
@@ -389,7 +380,6 @@ def tile_teacher_logits_remap_d4_kernel(tc, x_bytes, x_scale, head, b, tau, map_
         part(5)
         step(3, 0)
         part_out(5)
-        head_sort(7)
         zo(3, 0, 0)
         head_quantise(5)
         zo(3, 1, 0)

@@ -31,8 +31,9 @@ PAIR = 2 * P
 
 SHARED_TILES = 2
 STAGED = 3
-ZQ = {1: (2, 2, 2), 4: (0, 2, 3), 7: (2, 2, 3)}
+ZQ = {2: (0, 2, 2), 3: (2, 2, 2), 5: (0, 2, 3), 7: (2, 2, 3)}
 SHARED_BANKS = ((0, 0, 1), (0, 1, 1))
+GPSIMD_UNITS = ((0, 3), (1, 3))
 
 
 def tile_teacher_logits_remap_d4_kernel(tc, x_bytes, x_scale, head, b, tau, map_words, map_scales, c, out):
@@ -79,7 +80,7 @@ def tile_teacher_logits_remap_d4_kernel(tc, x_bytes, x_scale, head, b, tau, map_
         def load_head(e):
             nc.sync.dma_start(out=head_part[e][:], in_=head_v[e // 2, :, 2 * (e % 2) : 2 * (e % 2) + 2, :])
 
-        nc.vector.memset(zeros[:].bitcast(I32), 0)
+        nc.gpsimd.memset(zeros[:].bitcast(I32), 0)
         make_identity(nc, ident[:])
         nc.vector.memset(map_scale_sb[:].rearrange("p c n -> p (c n)").bitcast(I32), 0)
 
@@ -113,14 +114,15 @@ def tile_teacher_logits_remap_d4_kernel(tc, x_bytes, x_scale, head, b, tau, map_
         inv_tau = [keep.tile([P, 4, P], F32, name=f"inv_tau{h}") for h in range(2)]
         tau_bank = {}
 
-        def warm_up(bank, count):
-            for n in range(count):
-                nc.tensor.matmul(bank, lhsT=zeros[:, :P], rhs=zeros[:], start=True, stop=True)
+        def warm_up(count):
+            n, scratch = take_bank([P, BANK])
+            for m in range(count):
+                nc.tensor.matmul(scratch[:], lhsT=zeros[:, :P], rhs=zeros[:], start=True, stop=True)
+            free_banks.append(n)
 
-        def spread_inv_tau(h, warm_ups):
+        def spread_inv_tau(h):
             tau_bank[h] = take_bank([P, 4, P])
             rows = tau_bank[h][1]
-            warm_up(rows[:].rearrange("p i n -> p (i n)"), warm_ups)
             for ii in range(4):
                 column = inv_tau_col[:, 4 * h + ii : 4 * h + ii + 1]
                 nc.tensor.transpose(rows[:, ii, :], column.to_broadcast([P, P]), ident[:])
@@ -152,9 +154,8 @@ def tile_teacher_logits_remap_d4_kernel(tc, x_bytes, x_scale, head, b, tau, map_
                 else:
                     nc.vector.tensor_scalar(by_word[:, q], codes.rearrange("p (r u e) -> p r u e", u=2, e=2), scale, None, op0=MULT)
 
-        def turn(passes, warm_ups):
+        def turn(passes):
             n, turned = take_bank([P, PASSES, 2, P])
-            warm_up(turned[:].rearrange("p g u r -> p (g u r)"), warm_ups)
             for g, (words, is_sorted) in enumerate(passes):
                 for u in range(2):
                     cols = slice(P * u, P * (u + 1)) if is_sorted else slice(u, 2 * P, 2)
@@ -166,8 +167,8 @@ def tile_teacher_logits_remap_d4_kernel(tc, x_bytes, x_scale, head, b, tau, map_
             nc.scalar.copy(dst, turned[:].rearrange("p g u r -> p g r u"))
             free_banks.append(n)
 
-        def x_turn(i, warm_ups=0):
-            x_banks[i] = turn([(x_wide[i, g][:].bitcast(F32), not (g == 1 and i < SHARED_TILES)) for g in range(PASSES)], warm_ups)
+        def x_turn(i):
+            x_banks[i] = turn([(x_wide[i, g][:].bitcast(F32), not (g == 1 and i < SHARED_TILES)) for g in range(PASSES)])
 
         def x_out(i):
             if i % 2 == 0:
@@ -200,10 +201,10 @@ def tile_teacher_logits_remap_d4_kernel(tc, x_bytes, x_scale, head, b, tau, map_
         def staged():
             return work.tile([P, 2048], BF16, name="staged", align_bytes=64, bufs=STAGED)
 
-        def head_turn(e, s, warm_ups=0):
+        def head_turn(e, s):
             row = head_single[s][:] if e == 0 else head_sorted.get(e, head_part[e])[:, s, :]
             words = row.bitcast(F32)
-            head_banks[e, s] = turn([(words[:, 256 * g : 256 * (g + 1)], e in head_sorted) for g in range(PASSES)], warm_ups)
+            head_banks[e, s] = turn([(words[:, 256 * g : 256 * (g + 1)], e in head_sorted) for g in range(PASSES)])
 
         def head_out(e, s):
             if s == 0:
@@ -254,7 +255,10 @@ def tile_teacher_logits_remap_d4_kernel(tc, x_bytes, x_scale, head, b, tau, map_
             cols = slice((q % 2) * PAIR, (q % 2 + 1) * PAIR)
             dst = z_words[cc // 2, q][:, 1024 * (cc % 2) : 1024 * (cc % 2 + 1)].rearrange("p (n i s) -> p n s i", i=4, s=SLOTS)
             src = z_slots[cc, q // 2][:, :, cols].rearrange("p s (n i) -> p n s i", i=4)
-            nc.scalar.copy(dst, src)
+            if (cc, q) in GPSIMD_UNITS:
+                nc.gpsimd.tensor_scalar(dst, src, 1.0, 0.0, op0=MULT, op1=ADD)
+            else:
+                nc.scalar.copy(dst, src)
 
         def z_quantise(first, count, q):
             lo = 1024 * (first % 2)
@@ -290,30 +294,35 @@ def tile_teacher_logits_remap_d4_kernel(tc, x_bytes, x_scale, head, b, tau, map_
             nc.sync.dma_start(out=out_v[:, i, cols], in_=y_rows[i][:, cols])
 
         nc.vector.reciprocal(inv_tau_col[:], tau_sb[:])
-        spread_inv_tau(1, 3)
-        spread_inv_tau(0, 0)
+        warm_up(3)
+        spread_inv_tau(1)
+        spread_inv_tau(0)
         for i in range(2):
             widen(i, 0)
             widen(i, 1)
         inv_tau_out(1)
-        x_turn(0, 1)
+        warm_up(1)
+        x_turn(0)
         x_out(0)
         head_turn(0, 0)
         head_out(0, 0)
+        warm_up(1)
         x_turn(1)
         x_out(1)
         for i in range(2, 5):
             widen(i, 0)
             widen(i, 1)
-        head_turn(0, 1, 1)
+        head_turn(0, 1)
         head_out(0, 1)
         x_turn(2)
         x_out(2)
+        warm_up(1)
         x_turn(3)
         x_out(3)
         x_quantise(0)
         head_quantise(0)
-        head_turn(1, 0, 1)
+        inv_tau_out(0)
+        head_turn(1, 0)
         head_out(1, 0)
         head_turn(1, 1)
         head_out(1, 1)
@@ -321,7 +330,6 @@ def tile_teacher_logits_remap_d4_kernel(tc, x_bytes, x_scale, head, b, tau, map_
         widen(5, 0)
         widen(5, 1)
         head_quantise(1)
-        inv_tau_out(0)
 
         accs = {}
 
@@ -344,11 +352,11 @@ def tile_teacher_logits_remap_d4_kernel(tc, x_bytes, x_scale, head, b, tau, map_
             widen(i, 0)
             widen(i, 1)
 
-        for q in range(4):
-            for cp in range(2):
-                z_words[cp, q] = keep.tile([P, 2048], BF16, name=f"z_words{cp}_{q}", align_bytes=64)
-        head_turn(2, 0, 1)
-        head_turn(2, 1)
+        for cp, q in ((0, 0), (1, 0), (0, 1), (0, 2), (1, 2), (1, 3)):
+            z_words[cp, q] = keep.tile([P, 2048], BF16, name=f"z_words{cp}_{q}", align_bytes=64)
+        z_words[1, 1] = work.tile([P, 2048], BF16, name="z_words1_1", tag="handed", align_bytes=64)
+        warm_up(1)
+        part(2)
         x_turn(4)
         step(0, 0)
         part_out(2)
@@ -366,25 +374,26 @@ def tile_teacher_logits_remap_d4_kernel(tc, x_bytes, x_scale, head, b, tau, map_
         zo(1, 0, 0)
         head_quantise(3)
         zo(1, 1, 0)
-        x_quantise(2)
+        wide(7)
         part(4)
         x_turn(6)
         step(2, 0)
         part_out(4)
-        head_sort(6)
         x_out(6)
+        head_sort(6)
         zo(2, 0, 0)
         head_quantise(4)
         zo(2, 1, 0)
-        wide(7)
+        x_quantise(2)
         part(5)
+        x_turn(7)
         step(3, 0)
         part_out(5)
+        x_out(7)
         zo(3, 0, 0)
         head_quantise(5)
         zo(3, 1, 0)
         part(6)
-        x_turn(7)
         step(4, 0)
         part_out(6)
         zo(4, 0, 0)
@@ -393,7 +402,6 @@ def tile_teacher_logits_remap_d4_kernel(tc, x_bytes, x_scale, head, b, tau, map_
         part(7)
         step(5, 0)
         part_out(7)
-        x_out(7)
         head_quantise(7)
         x_quantise(3)
         zo(5, 1, 0)
@@ -415,6 +423,7 @@ def tile_teacher_logits_remap_d4_kernel(tc, x_bytes, x_scale, head, b, tau, map_
 
         z_interleave(0, 0)
         z_interleave(1, 0)
+        z_interleave(0, 1)
         step(6, 0)
         both(6, 0)
         step(7, 0)
@@ -424,7 +433,6 @@ def tile_teacher_logits_remap_d4_kernel(tc, x_bytes, x_scale, head, b, tau, map_
         zo(0, 1, 1)
         z_interleave(2, 0)
         z_interleave(3, 0)
-        z_interleave(0, 1)
         step(1, 1)
         both(1, 1)
         for cc in range(1, 4):
@@ -450,10 +458,10 @@ def tile_teacher_logits_remap_d4_kernel(tc, x_bytes, x_scale, head, b, tau, map_
         zo(6, 1, 1)
         step(7, 1)
         both(7, 1)
+        z_words[0, 3] = work.tile([P, 2048], BF16, name="z_words0_3", tag="handed", align_bytes=64)
         z_interleave(3, 2)
         for cc in range(4):
             z_interleave(cc, 3)
-        z_quantise(0, 2, 2)
         for j in range(14):
             y_mm(j)
             y_o(j)

@@ -29,10 +29,10 @@ PARTS = 2 * CHUNKS
 HALF = T // 2
 PAIR = 2 * P
 
-SHARED_TILES = 2
+SCALAR_TILE = 1
 STAGED = 3
 ZQ = {2: (0, 2, 2), 3: (2, 2, 2), 5: (0, 2, 3), 7: (2, 2, 3)}
-SHARED_BANKS = ((0, 0, 1), (0, 1, 1))
+SHARED_BANKS = ((7, 0, 0), (7, 1, 0))
 GPSIMD_UNITS = ((0, 3), (1, 3))
 
 
@@ -80,7 +80,7 @@ def tile_teacher_logits_remap_d4_kernel(tc, x_bytes, x_scale, head, b, tau, map_
         def load_head(e):
             nc.sync.dma_start(out=head_part[e][:], in_=head_v[e // 2, :, 2 * (e % 2) : 2 * (e % 2) + 2, :])
 
-        nc.gpsimd.memset(zeros[:].bitcast(I32), 0)
+        nc.vector.memset(zeros[:].bitcast(I32), 0)
         make_identity(nc, ident[:])
         nc.vector.memset(map_scale_sb[:].rearrange("p c n -> p (c n)").bitcast(I32), 0)
 
@@ -138,8 +138,8 @@ def tile_teacher_logits_remap_d4_kernel(tc, x_bytes, x_scale, head, b, tau, map_
         x_codes = [keep.tile([P, PASSES, HALF], U32, name=f"x_codes{h}", align_bytes=64) for h in range(2)]
         x_scales = [keep.tile([P, PASSES, HALF], U8, name=f"x_scales{h}", align_bytes=64) for h in range(2)]
 
-        shared_scale = keep.tile([P, SHARED_TILES, 4], F32, name="shared_scale")
-        nc.scalar.activation(shared_scale[:], x_scale_sb[:, :SHARED_TILES, 4:], COPY)
+        shared_scale = keep.tile([P, K // B], F32, name="shared_scale")
+        nc.scalar.activation(shared_scale[:], x_scale_sb[:, SCALAR_TILE, :], COPY)
 
         def widen(i, g):
             x_wide[i, g] = work.tile([P, 512], BF16, name="x_wide", bufs=10)
@@ -149,8 +149,8 @@ def tile_teacher_logits_remap_d4_kernel(tc, x_bytes, x_scale, head, b, tau, map_
                 j = 4 * g + q
                 codes = row[:, j * B : (j + 1) * B].bitcast(FP8)
                 scale = x_scale_sb[:, i, j : j + 1]
-                if g == 1 and i < SHARED_TILES:
-                    nc.scalar.activation(x_wide[i, g][:, q * B : (q + 1) * B], codes, COPY, scale=shared_scale[:, i, q : q + 1])
+                if i == SCALAR_TILE:
+                    nc.scalar.activation(x_wide[i, g][:, q * B : (q + 1) * B], codes, COPY, scale=shared_scale[:, j : j + 1])
                 else:
                     nc.vector.tensor_scalar(by_word[:, q], codes.rearrange("p (r u e) -> p r u e", u=2, e=2), scale, None, op0=MULT)
 
@@ -168,7 +168,7 @@ def tile_teacher_logits_remap_d4_kernel(tc, x_bytes, x_scale, head, b, tau, map_
             free_banks.append(n)
 
         def x_turn(i):
-            x_banks[i] = turn([(x_wide[i, g][:].bitcast(F32), not (g == 1 and i < SHARED_TILES)) for g in range(PASSES)])
+            x_banks[i] = turn([(x_wide[i, g][:].bitcast(F32), i != SCALAR_TILE) for g in range(PASSES)])
 
         def x_out(i):
             if i % 2 == 0:
@@ -293,45 +293,8 @@ def tile_teacher_logits_remap_d4_kernel(tc, x_bytes, x_scale, head, b, tau, map_
             nc.vector.tensor_tensor(y_rows[i][:, cols], acc, c_rows[:, cols], op=ADD)
             nc.sync.dma_start(out=out_v[:, i, cols], in_=y_rows[i][:, cols])
 
-        nc.vector.reciprocal(inv_tau_col[:], tau_sb[:])
-        warm_up(3)
-        spread_inv_tau(1)
-        spread_inv_tau(0)
-        for i in range(2):
-            widen(i, 0)
-            widen(i, 1)
-        inv_tau_out(1)
-        warm_up(1)
-        x_turn(0)
-        x_out(0)
-        head_turn(0, 0)
-        head_out(0, 0)
-        warm_up(1)
-        x_turn(1)
-        x_out(1)
-        for i in range(2, 5):
-            widen(i, 0)
-            widen(i, 1)
-        head_turn(0, 1)
-        head_out(0, 1)
-        x_turn(2)
-        x_out(2)
-        warm_up(1)
-        x_turn(3)
-        x_out(3)
-        x_quantise(0)
-        head_quantise(0)
-        inv_tau_out(0)
-        head_turn(1, 0)
-        head_out(1, 0)
-        head_turn(1, 1)
-        head_out(1, 1)
-        x_quantise(1)
-        widen(5, 0)
-        widen(5, 1)
-        head_quantise(1)
-
         accs = {}
+        ybank = {}
 
         def step(e, h):
             for s in range(2):
@@ -339,6 +302,10 @@ def tile_teacher_logits_remap_d4_kernel(tc, x_bytes, x_scale, head, b, tau, map_
 
         def zo(e, s, h):
             z_out(e, s, h, accs[e, s, h])
+
+        def both(e, h):
+            zo(e, 1, h)
+            zo(e, 0, h)
 
         def part(e):
             head_turn(e, 0)
@@ -352,9 +319,52 @@ def tile_teacher_logits_remap_d4_kernel(tc, x_bytes, x_scale, head, b, tau, map_
             widen(i, 0)
             widen(i, 1)
 
+        def y_mm(j):
+            i, n0 = j // 2, (j % 2) * BANK
+            ybank[j] = take_bank([P, BANK])
+            second_product(i, n0, BANK, ybank[j][1][:])
+
+        def y_o(j):
+            y_out(j // 2, (j % 2) * BANK, BANK, ybank[j][1][:])
+            free_banks.append(ybank[j][0])
+
         for cp, q in ((0, 0), (1, 0), (0, 1), (0, 2), (1, 2), (1, 3)):
             z_words[cp, q] = keep.tile([P, 2048], BF16, name=f"z_words{cp}_{q}", align_bytes=64)
         z_words[1, 1] = work.tile([P, 2048], BF16, name="z_words1_1", tag="handed", align_bytes=64)
+
+        nc.vector.reciprocal(inv_tau_col[:], tau_sb[:])
+        warm_up(3)
+        spread_inv_tau(1)
+        spread_inv_tau(0)
+        wide(0)
+        wide(1)
+        inv_tau_out(1)
+        warm_up(1)
+        x_turn(0)
+        x_out(0)
+        head_turn(0, 0)
+        head_out(0, 0)
+        x_turn(1)
+        x_out(1)
+        wide(2)
+        wide(3)
+        wide(4)
+        warm_up(1)
+        head_turn(0, 1)
+        head_out(0, 1)
+        x_turn(2)
+        x_out(2)
+        warm_up(1)
+        x_turn(3)
+        x_out(3)
+        x_quantise(0)
+        head_quantise(0)
+        part(1)
+        part_out(1)
+        x_quantise(1)
+        inv_tau_out(0)
+        wide(5)
+        head_quantise(1)
         warm_up(1)
         part(2)
         x_turn(4)
@@ -404,35 +414,19 @@ def tile_teacher_logits_remap_d4_kernel(tc, x_bytes, x_scale, head, b, tau, map_
         part_out(7)
         head_quantise(7)
         x_quantise(3)
-        zo(5, 1, 0)
-        zo(5, 0, 0)
-        ybank = {}
-
-        def y_mm(j):
-            i, n0 = j // 2, (j % 2) * BANK
-            ybank[j] = take_bank([P, BANK])
-            second_product(i, n0, BANK, ybank[j][1][:])
-
-        def y_o(j):
-            y_out(j // 2, (j % 2) * BANK, BANK, ybank[j][1][:])
-            free_banks.append(ybank[j][0])
-
-        def both(e, h):
-            zo(e, 1, h)
-            zo(e, 0, h)
-
+        both(5, 0)
         z_interleave(0, 0)
-        z_interleave(1, 0)
-        z_interleave(0, 1)
         step(6, 0)
         both(6, 0)
         step(7, 0)
-        both(7, 0)
-        step(0, 1)
-        zo(0, 0, 1)
-        zo(0, 1, 1)
+        zo(7, 0, 0)
+        zo(7, 1, 0)
+        z_interleave(1, 0)
         z_interleave(2, 0)
+        z_interleave(0, 1)
         z_interleave(3, 0)
+        step(0, 1)
+        both(0, 1)
         step(1, 1)
         both(1, 1)
         for cc in range(1, 4):

@@ -32,7 +32,7 @@ PAIR = 2 * P
 SCALAR_TILE = 1
 STAGED = 3
 ZQ = {2: (0, 2, 2), 3: (2, 2, 2), 5: (0, 2, 3), 7: (2, 2, 3)}
-SHARED_BANKS = ((7, 0, 0), (7, 1, 0))
+SHARED_BANKS = ((0, 0, 1), (0, 1, 1))
 GPSIMD_UNITS = ((0, 3), (1, 3))
 
 
@@ -409,24 +409,24 @@ def tile_teacher_logits_remap_d4_kernel(tc, x_bytes, x_scale, head, b, tau, map_
         zo(4, 0, 0)
         head_quantise(6)
         zo(4, 1, 0)
+        x_quantise(3)
         part(7)
         step(5, 0)
         part_out(7)
         head_quantise(7)
-        x_quantise(3)
         both(5, 0)
         z_interleave(0, 0)
         step(6, 0)
         both(6, 0)
-        step(7, 0)
-        zo(7, 0, 0)
-        zo(7, 1, 0)
+        step(0, 1)
+        zo(0, 0, 1)
+        zo(0, 1, 1)
         z_interleave(1, 0)
+        step(7, 0)
+        both(7, 0)
         z_interleave(2, 0)
         z_interleave(0, 1)
         z_interleave(3, 0)
-        step(0, 1)
-        both(0, 1)
         step(1, 1)
         both(1, 1)
         for cc in range(1, 4):

from contextlib import ExitStack

import concourse.mybir as mybir
from concourse.masks import make_identity

T, K, V, N, B = 1024, 1024, 2048, 1024, 128
FLOPS = 2 * T * K * V + 2 * T * V * N

F32 = mybir.dt.float32
BF16 = mybir.dt.bfloat16
I32 = mybir.dt.int32
U32 = mybir.dt.uint32
U8 = mybir.dt.uint8
FP8 = mybir.dt.float8_e4m3fn
FP8X4 = mybir.dt.float8_e4m3fn_x4
FP4X4 = mybir.dt.float4_e2m1fn_x4
ADD = mybir.AluOpType.add
MULT = mybir.AluOpType.mult
COPY = mybir.ActivationFunctionType.Copy
IDENTITY = mybir.ActivationFunctionType.Identity

P = 128
BANK = 512
PASSES = K // 512
TILES = T // P
CHUNKS = V // 512
SLOTS = 4
PARTS = 2 * CHUNKS
HALF = T // 2
PAIR = 2 * P

SCALAR_TILE = 1
STAGED = 3
ZQ = {2: (0, 2, 2), 3: (2, 2, 2), 5: (0, 2, 3), 7: (2, 2, 3)}
SHARED_BANKS = ((0, 0, 1), (0, 1, 1))
GPSIMD_UNITS = ((0, 3), (1, 3))


def tile_teacher_logits_remap_d4_kernel(tc, x_bytes, x_scale, head, b, tau, map_words, map_scales, c, out):
    nc = tc.nc
    x_v = x_bytes.rearrange("(p i) k -> p i k", i=TILES)
    head_v = head.rearrange("(c p s) k -> c p s k", p=P, s=SLOTS)
    b_v = b.rearrange("(c p s) -> p c s", p=P, s=SLOTS)
    out_v = out.rearrange("(p i) n -> p i n", i=TILES)

    with ExitStack() as ctx:
        keep = ctx.enter_context(tc.tile_pool(name="keep", bufs=1))
        work = ctx.enter_context(tc.tile_pool(name="work", bufs=1))
        psum = ctx.enter_context(tc.psum_pool(name="psum", bufs=1))
        ctx.enter_context(tc.manual_schedule())

        free_banks = list(range(8))

        def take_bank(shape):
            n = free_banks.pop(0)
            return n, psum.tile(shape, F32, name=f"bank{n}", tag=f"bank{n}")

        x_scale_sb = keep.tile([P, TILES, K // B], F32, name="x_scale_sb")
        x_single = {i: keep.tile([P, K], U8, name=f"x_single{i}") for i in (0, 1, 4, 5)}
        x_pair = {q: keep.tile([P, 2, K], U8, name=f"x_pair{q}") for q in (1, 3)}
        head_single = [keep.tile([P, K], BF16, name=f"head_single{s}") for s in range(2)]
        head_part = {
            e: work.tile([P, 2, K], BF16, name=f"head_part{e}", tag="rows", bufs=PARTS - 1) for e in range(1, PARTS)
        }
        b_first = keep.tile([P, SLOTS], BF16, name="b_first")
        b_rest = keep.tile([P, CHUNKS - 1, SLOTS], BF16, name="b_rest")
        tau_sb = keep.tile([P, TILES], BF16, name="tau_sb")
        map_scale_sb = keep.tile([P, CHUNKS, N], U8, name="map_scale_sb", align_bytes=64)
        map_sb = keep.tile([P, CHUNKS, 2 * N], U8, name="map_sb", align_bytes=64)
        c_rows = keep.tile([P, N], BF16, name="c_rows")
        ident = keep.tile([P, P], F32, name="ident")
        zeros = keep.tile([P, BANK], BF16, name="zeros")

        def load_x_tile(i):
            nc.sync.dma_start(out=x_single[i][:], in_=x_v[:, i, :])

        def load_x_pair(q):
            nc.sync.dma_start(out=x_pair[q][:], in_=x_v[:, 2 * q : 2 * q + 2, :])

        def load_head(e):
            nc.sync.dma_start(out=head_part[e][:], in_=head_v[e // 2, :, 2 * (e % 2) : 2 * (e % 2) + 2, :])

        nc.vector.memset(zeros[:].bitcast(I32), 0)
        make_identity(nc, ident[:])
        nc.vector.memset(map_scale_sb[:].rearrange("p c n -> p (c n)").bitcast(I32), 0)

        nc.sync.dma_start(out=tau_sb[:], in_=tau.rearrange("(p i) -> p i", i=TILES))
        nc.sync.dma_start(out=x_scale_sb[:], in_=x_scale.rearrange("(p i) j -> p i j", i=TILES))
        load_x_tile(0)
        load_x_tile(1)
        nc.sync.dma_start(out=head_single[0][:], in_=head_v[0, :, 0, :])
        load_x_pair(1)
        nc.sync.dma_start(out=head_single[1][:], in_=head_v[0, :, 1, :])
        load_x_tile(4)
        load_head(1)
        nc.sync.dma_start(out=b_first[:], in_=b_v[:, 0, :])
        load_head(2)
        load_x_tile(5)
        load_head(3)
        load_x_pair(3)
        load_head(4)
        nc.sync.dma_start(out=b_rest[:], in_=b_v[:, 1:, :])
        for e in range(5, PARTS):
            load_head(e)
        for q in range(4):
            nc.sync.dma_start(
                out=map_scale_sb[32 * q : 32 * q + 4, :, :].bitcast(I32),
                in_=map_scales[:, 4 * q : 4 * q + 4, :].rearrange("c r n -> r c n").bitcast(I32),
            )
        nc.sync.dma_start(out=map_sb[:].bitcast(I32), in_=map_words.rearrange("c p n -> p c n").bitcast(I32))
        nc.sync.dma_start(out=c_rows[:], in_=c.partition_broadcast(P))

        inv_tau_col = keep.tile([P, TILES], F32, name="inv_tau_col")
        inv_tau = [keep.tile([P, 4, P], F32, name=f"inv_tau{h}") for h in range(2)]
        tau_bank = {}

        def warm_up(count):
            n, scratch = take_bank([P, BANK])
            for m in range(count):
                nc.tensor.matmul(scratch[:], lhsT=zeros[:, :P], rhs=zeros[:], start=True, stop=True)
            free_banks.append(n)

        def spread_inv_tau(h):
            tau_bank[h] = take_bank([P, 4, P])
            rows = tau_bank[h][1]
            for ii in range(4):
                column = inv_tau_col[:, 4 * h + ii : 4 * h + ii + 1]
                nc.tensor.transpose(rows[:, ii, :], column.to_broadcast([P, P]), ident[:])

        def inv_tau_out(h):
            n, rows = tau_bank[h]
            nc.vector.tensor_copy(inv_tau[h][:], rows[:])
            free_banks.append(n)

        x_wide = {}
        x_turned = {}
        x_banks = {}
        x_codes = [keep.tile([P, PASSES, HALF], U32, name=f"x_codes{h}", align_bytes=64) for h in range(2)]
        x_scales = [keep.tile([P, PASSES, HALF], U8, name=f"x_scales{h}", align_bytes=64) for h in range(2)]

        shared_scale = keep.tile([P, K // B], F32, name="shared_scale")
        nc.scalar.activation(shared_scale[:], x_scale_sb[:, SCALAR_TILE, :], COPY)

        def widen(i, g):
            x_wide[i, g] = work.tile([P, 512], BF16, name="x_wide", bufs=10)
            row = x_single[i][:] if i in x_single else x_pair[i // 2][:, i % 2]
            by_word = x_wide[i, g][:].rearrange("p (u q r e) -> p q r u e", u=2, q=4, e=2)
            for q in range(4):
                j = 4 * g + q
                codes = row[:, j * B : (j + 1) * B].bitcast(FP8)
                scale = x_scale_sb[:, i, j : j + 1]
                if i == SCALAR_TILE:
                    nc.scalar.activation(x_wide[i, g][:, q * B : (q + 1) * B], codes, COPY, scale=shared_scale[:, j : j + 1])
                else:
                    nc.vector.tensor_scalar(by_word[:, q], codes.rearrange("p (r u e) -> p r u e", u=2, e=2), scale, None, op0=MULT)

        def turn(passes):
            n, turned = take_bank([P, PASSES, 2, P])
            for g, (words, is_sorted) in enumerate(passes):
                for u in range(2):
                    cols = slice(P * u, P * (u + 1)) if is_sorted else slice(u, 2 * P, 2)
                    nc.tensor.transpose(turned[:, g, u, :], words[:, cols], ident[:])
            return n, turned

        def turned_out(bank, dst):
            n, turned = bank
            nc.scalar.copy(dst, turned[:].rearrange("p g u r -> p g r u"))
            free_banks.append(n)

        def x_turn(i):
            x_banks[i] = turn([(x_wide[i, g][:].bitcast(F32), i != SCALAR_TILE) for g in range(PASSES)])

        def x_out(i):
            if i % 2 == 0:
                x_turned[i // 2] = work.tile([P, PASSES, PAIR, 4], BF16, name="x_turned", align_bytes=64, bufs=2)
            dst = x_turned[i // 2][:, :, (i % 2) * P : (i % 2 + 1) * P, :].rearrange("p g r t -> p g (r t)").bitcast(F32)
            turned_out(x_banks[i], dst.rearrange("p g (r u) -> p g r u", u=2))

        def x_quantise(q):
            cols = slice((q % 2) * PAIR, (q % 2 + 1) * PAIR)
            for g in range(PASSES):
                nc.vector.quantize_mx(
                    out=x_codes[q // 2][:, g, cols].bitcast(FP8X4),
                    scales=x_scales[q // 2][:, g, cols],
                    in_=x_turned[q][:, g].rearrange("p n t -> p (n t)"),
                )

        head_sorted = {}
        head_turned = {}
        head_banks = {}
        head_codes = [keep.tile([P, 2, PASSES, P], U32, name=f"head_codes{e}", align_bytes=64) for e in range(PARTS)]
        head_scales = [keep.tile([P, 2, PASSES, P], U8, name=f"head_scales{e}", align_bytes=64) for e in range(PARTS)]

        def head_sort(e):
            head_sorted[e] = work.tile([P, 2, K], BF16, name="head_sorted", bufs=3)
            nc.scalar.copy(
                head_sorted[e][:].bitcast(F32).rearrange("p s (g u r) -> p (s g) u r", g=PASSES, u=2),
                head_part[e][:].bitcast(F32).rearrange("p s (g r u) -> p (s g) u r", g=PASSES, u=2),
            )

        def staged():
            return work.tile([P, 2048], BF16, name="staged", align_bytes=64, bufs=STAGED)

        def head_turn(e, s):
            row = head_single[s][:] if e == 0 else head_sorted.get(e, head_part[e])[:, s, :]
            words = row.bitcast(F32)
            head_banks[e, s] = turn([(words[:, 256 * g : 256 * (g + 1)], e in head_sorted) for g in range(PASSES)])

        def head_out(e, s):
            if s == 0:
                head_turned[e] = staged()
            dst = head_turned[e][:, 1024 * s : 1024 * (s + 1)].bitcast(F32)
            turned_out(head_banks[e, s], dst.rearrange("p (g r u) -> p g r u", g=PASSES, u=2))

        def head_quantise(e):
            nc.vector.quantize_mx(
                out=head_codes[e][:].rearrange("p s g m -> p (s g m)").bitcast(FP8X4),
                scales=head_scales[e][:].rearrange("p s g m -> p (s g m)"),
                in_=head_turned[e][:],
            )

        z_slots = {(cc, h): keep.tile([P, SLOTS, HALF], BF16, name=f"z_slots{cc}_{h}") for h in range(2) for cc in range(CHUNKS)}
        z_words = {}
        z_codes = [keep.tile([P, CHUNKS, PAIR], U32, name=f"z_codes{q}", align_bytes=64) for q in range(4)]
        z_scales = [keep.tile([P, CHUNKS, PAIR], U8, name=f"z_scales{q}", align_bytes=64) for q in range(4)]

        def first_product(e, s, h):
            n, acc = take_bank([P, HALF])
            for g in range(PASSES):
                nc.tensor.matmul_mx(
                    out=acc[:],
                    lhsT=head_codes[e][:, s, g, :].bitcast(FP8X4),
                    lhsT_scale=head_scales[e][:, s, g, :],
                    rhs=x_codes[h][:, g, :].bitcast(FP8X4),
                    rhs_scale=x_scales[h][:, g, :],
                    start=(g == 0),
                    stop=(g == PASSES - 1),
                )
            return n, acc

        def z_out(e, s, h, bank):
            n, acc = bank
            cc, slot = e // 2, 2 * (e % 2) + s
            bias = (b_first[:] if cc == 0 else b_rest[:, cc - 1])[:, slot : slot + 1]
            factor = inv_tau[h][:].rearrange("p i n -> p (i n)")
            if (e, s, h) in SHARED_BANKS:
                sums = work.tile([P, HALF], F32, name="sums", bufs=2)
                nc.scalar.activation(sums[:], acc[:], IDENTITY, bias=bias)
                nc.gpsimd.tensor_tensor(z_slots[cc, h][:, slot, :], sums[:], factor, op=MULT)
            else:
                nc.vector.scalar_tensor_tensor(z_slots[cc, h][:, slot, :], acc[:], bias, factor, op0=ADD, op1=MULT)
            free_banks.append(n)

        def z_interleave(cc, q):
            cols = slice((q % 2) * PAIR, (q % 2 + 1) * PAIR)
            dst = z_words[cc // 2, q][:, 1024 * (cc % 2) : 1024 * (cc % 2 + 1)].rearrange("p (n i s) -> p n s i", i=4, s=SLOTS)
            src = z_slots[cc, q // 2][:, :, cols].rearrange("p s (n i) -> p n s i", i=4)
            if (cc, q) in GPSIMD_UNITS:
                nc.gpsimd.tensor_scalar(dst, src, 1.0, 0.0, op0=MULT, op1=ADD)
            else:
                nc.scalar.copy(dst, src)

        def z_quantise(first, count, q):
            lo = 1024 * (first % 2)
            nc.vector.quantize_mx(
                out=z_codes[q][:, first : first + count, :].rearrange("p c n -> p (c n)").bitcast(FP8X4),
                scales=z_scales[q][:, first : first + count, :].rearrange("p c n -> p (c n)"),
                in_=z_words[first // 2, q][:, lo : lo + 1024 * count],
            )

        y_rows = {}

        def second_product(i, n0, width, acc):
            cols = slice((i % 2) * P, (i % 2 + 1) * P)
            for cc in range(CHUNKS):
                nc.tensor.matmul_mx(
                    out=acc,
                    lhsT=z_codes[i // 2][:, cc, cols].bitcast(FP8X4),
                    lhsT_scale=z_scales[i // 2][:, cc, cols],
                    rhs=map_sb[:, cc, 2 * n0 : 2 * (n0 + width)].bitcast(FP4X4),
                    rhs_scale=map_scale_sb[:, cc, n0 : n0 + width],
                    start=(cc == 0),
                    stop=(cc == CHUNKS - 1),
                )

        def y_out(i, n0, width, acc):
            if i not in y_rows:
                if i < TILES - 1:
                    y_rows[i] = work.tile([P, N], F32, name="y", tag="rows", bufs=PARTS - 1)
                else:
                    y_rows[i] = keep.tile([P, N], F32, name="y_last")
            cols = slice(n0, n0 + width)
            nc.vector.tensor_tensor(y_rows[i][:, cols], acc, c_rows[:, cols], op=ADD)
            nc.sync.dma_start(out=out_v[:, i, cols], in_=y_rows[i][:, cols])

        accs = {}
        ybank = {}

        def step(e, h):
            for s in range(2):
                accs[e, s, h] = first_product(e, s, h)

        def zo(e, s, h):
            z_out(e, s, h, accs[e, s, h])

        def both(e, h):
            zo(e, 1, h)
            zo(e, 0, h)

        def part(e):
            head_turn(e, 0)
            head_turn(e, 1)

        def part_out(e):
            head_out(e, 0)
            head_out(e, 1)

        def wide(i):
            widen(i, 0)
            widen(i, 1)

        def y_mm(j):
            i, n0 = j // 2, (j % 2) * BANK
            ybank[j] = take_bank([P, BANK])
            second_product(i, n0, BANK, ybank[j][1][:])

        def y_o(j):
            y_out(j // 2, (j % 2) * BANK, BANK, ybank[j][1][:])
            free_banks.append(ybank[j][0])

        for cp, q in ((0, 0), (1, 0), (0, 1), (0, 2), (1, 2), (1, 3)):
            z_words[cp, q] = keep.tile([P, 2048], BF16, name=f"z_words{cp}_{q}", align_bytes=64)
        z_words[1, 1] = work.tile([P, 2048], BF16, name="z_words1_1", tag="handed", align_bytes=64)

        nc.vector.reciprocal(inv_tau_col[:], tau_sb[:])
        warm_up(3)
        spread_inv_tau(1)
        spread_inv_tau(0)
        wide(0)
        wide(1)
        inv_tau_out(1)
        warm_up(1)
        x_turn(0)
        x_out(0)
        head_turn(0, 0)
        head_out(0, 0)
        x_turn(1)
        x_out(1)
        wide(2)
        wide(3)
        wide(4)
        warm_up(1)
        head_turn(0, 1)
        head_out(0, 1)
        x_turn(2)
        x_out(2)
        warm_up(1)
        x_turn(3)
        x_out(3)
        x_quantise(0)
        head_quantise(0)
        part(1)
        part_out(1)
        x_quantise(1)
        inv_tau_out(0)
        wide(5)
        head_quantise(1)
        warm_up(1)
        part(2)
        x_turn(4)
        step(0, 0)
        part_out(2)
        x_out(4)
        zo(0, 0, 0)
        head_quantise(2)
        zo(0, 1, 0)
        wide(6)
        part(3)
        x_turn(5)
        step(1, 0)
        part_out(3)
        x_out(5)
        head_sort(5)
        zo(1, 0, 0)
        head_quantise(3)
        zo(1, 1, 0)
        wide(7)
        part(4)
        x_turn(6)
        step(2, 0)
        part_out(4)
        x_out(6)
        head_sort(6)
        zo(2, 0, 0)
        head_quantise(4)
        zo(2, 1, 0)
        x_quantise(2)
        part(5)
        x_turn(7)
        step(3, 0)
        part_out(5)
        x_out(7)
        zo(3, 0, 0)
        head_quantise(5)
        zo(3, 1, 0)
        part(6)
        step(4, 0)
        part_out(6)
        zo(4, 0, 0)
        head_quantise(6)
        zo(4, 1, 0)
        x_quantise(3)
        part(7)
        step(5, 0)
        part_out(7)
        head_quantise(7)
        both(5, 0)
        z_interleave(0, 0)
        step(6, 0)
        both(6, 0)
        step(0, 1)
        zo(0, 0, 1)
        zo(0, 1, 1)
        z_interleave(1, 0)
        step(7, 0)
        both(7, 0)
        z_interleave(2, 0)
        z_interleave(0, 1)
        z_interleave(3, 0)
        step(1, 1)
        both(1, 1)
        for cc in range(1, 4):
            z_interleave(cc, 1)
        step(2, 1)
        both(2, 1)
        step(3, 1)
        both(3, 1)
        z_quantise(0, 2, 0)
        z_interleave(0, 2)
        z_interleave(1, 2)
        step(4, 1)
        zo(4, 0, 1)
        z_quantise(2, 2, 0)
        zo(4, 1, 1)
        step(5, 1)
        both(5, 1)
        z_quantise(0, 2, 1)
        z_interleave(2, 2)
        step(6, 1)
        zo(6, 0, 1)
        z_quantise(2, 2, 1)
        zo(6, 1, 1)
        step(7, 1)
        both(7, 1)
        z_words[0, 3] = work.tile([P, 2048], BF16, name="z_words0_3", tag="handed", align_bytes=64)
        z_interleave(3, 2)
        for cc in range(4):
            z_interleave(cc, 3)
        for j in range(14):
            y_mm(j)
            y_o(j)
            if j in ZQ:
                z_quantise(*ZQ[j])
        n, acc = take_bank([P, BANK])
        second_product(TILES - 1, 0, BANK, acc[:])
        y_out(TILES - 1, 0, BANK // 2, acc[:, : BANK // 2])
        y_out(TILES - 1, BANK // 2, BANK // 2, acc[:, BANK // 2 :])
        for n0, width in ((512, 256), (768, 128), (896, 128)):
            n, acc = take_bank([P, width])
            second_product(TILES - 1, n0, width, acc[:])
            y_out(TILES - 1, n0, width, acc[:])
